import numpy as np
import ml_dtypes


def mxq(x, axis, fmt="e4m3"):
    dtype, down = {"e4m3": (ml_dtypes.float8_e4m3fn, 7), "e5m2": (ml_dtypes.float8_e5m2, 14)}[fmt]
    v = np.moveaxis(np.asarray(x, np.float32).astype(ml_dtypes.bfloat16).astype(np.float64), axis, -1)
    blocks = v.reshape(v.shape[:-1] + (-1, 32))
    amax = np.abs(blocks).max(-1, keepdims=True)
    byte = np.maximum(np.where(amax > 0, np.frexp(amax)[1] - 1 + 127, 0) - down, 1)
    scale = np.exp2(byte - 127.0)
    codes = (blocks / scale).astype(np.float32).astype(dtype).astype(np.float64)
    return np.moveaxis((codes * scale).reshape(v.shape), -1, axis)


WIDE = False


def mx_kscale(k):
    if not WIDE:
        return np.ones(k)
    levels = np.array([10, -10, 5, -5, 0])
    if k % 512:
        return np.exp2(np.random.permutation(np.resize(levels, k // 32))).repeat(32)
    a = np.empty((k // 512, 16))
    for p in range(k // 512):
        a[p, :8] = np.random.permutation(np.resize(levels, 8))
        for g in range(8):
            far = levels[np.abs(levels - a[p, g]) >= 10]
            a[p, g + 8] = far[np.random.randint(len(far))]
    return np.exp2(a.ravel()).repeat(32)


def f64(x):
    return np.asarray(x).astype(np.float64)


def striped(idx):
    return np.tile(idx.reshape(-1, 16).T, (8, 1)).astype(np.uint16)


def unstriped(offs):
    return offs[:16].T.reshape(-1).astype(np.int64)


def pack_weight(w):
    k, n = w.shape
    w = f64(np.asarray(w, np.float32).astype(ml_dtypes.bfloat16)).reshape(k // 32, 32, n)
    amax = np.abs(w).max(1)
    byte = np.clip(np.where(amax > 0, np.frexp(amax)[1] - 1 + 127 - 7, 1), 1, 254)
    scaled = (w * np.exp2(127.0 - byte)[:, None, :]).reshape(k, n).astype(np.float32)
    words = np.ascontiguousarray(scaled.reshape(k // 512, 128, 4, n).transpose(0, 1, 3, 2)).astype(ml_dtypes.float8_e4m3fn).view(np.uint8)
    return words, np.ascontiguousarray(byte.astype(np.uint8).reshape(k // 512, 16, n))


def unpack_weight(words, scales):
    g, p, n, _ = words.shape
    vals = np.ascontiguousarray(words).view(ml_dtypes.float8_e4m3fn).astype(np.float64) * np.repeat(np.exp2(scales.astype(np.float64) - 127.0), 8, axis=1)[..., None]
    return vals.transpose(0, 1, 3, 2).reshape(g * 512, n)


def sigmoid(v):
    return 1.0 / (1.0 + np.exp(-np.maximum(v, -700.0)))


K, T, S, H, D, W, U = 512, 2048, 512, 512, 4, 2048, 1024
P = 2 ** 7


def setup_inputs():
    n = np.random.standard_normal
    s = mx_kscale(K)[:, None]
    u = mx_kscale(H)
    packed_xT = pack_weight(n((K, T)) * s)
    packed_eT = pack_weight(n((H, W)) / np.sqrt(H) / u[:, None])
    return {
        "x_words": packed_xT[0],
        "x_scales": packed_xT[1],
        "w1": (n((K, H)) / np.sqrt(K) / s * u).astype(np.float32),
        "e_words": packed_eT[0],
        "e_scales": packed_eT[1],
        "inv": (np.tile(np.random.uniform(0.5, 1.5, W), (P, 1))).astype(np.float32),
        "own": (np.random.uniform(0.5, 1.5, (S, 1))).astype(np.float32),
        "offs": striped(np.random.permutation(T)[:S]),
        "enr": striped(np.random.permutation(W)[:U]),
    }


def reference(x_words, x_scales, w1, e_words, e_scales, inv, own, offs, enr):
    xq = unpack_weight(x_words, x_scales)[:, unstriped(offs)]
    h = mxq(f64(w1), 0, "e4m3").T @ xq
    e_enr = unpack_weight(e_words, e_scales)[:, unstriped(enr)]
    y = mxq(h, 0, "e4m3").T @ e_enr
    z = f64(own) * (y * (f64(inv)[:1][:, unstriped(enr)]))
    best = z.reshape(len(z), -1, D).max(axis=2)
    mean = z.reshape(len(z), -1, D).mean(axis=2)
    return sigmoid(2.0 * best + mean - 1.0)

@@ -1,0 +1,181 @@
+from contextlib import ExitStack
+
+import concourse.mybir as mybir
+from concourse.masks import make_identity
+
+F32 = mybir.dt.float32
+BF16 = mybir.dt.bfloat16
+I32 = mybir.dt.int32
+U32 = mybir.dt.uint32
+U16 = mybir.dt.uint16
+U8 = mybir.dt.uint8
+FP8X4 = mybir.dt.float8_e4m3fn_x4
+ALU = mybir.AluOpType
+ACT = mybir.ActivationFunctionType
+
+P = 128
+K, H, T, S, U, D = 512, 512, 2048, 512, 1024, 4
+V = U // D
+FACE_TILES = S // P
+ID_TILES = V // P
+INV_ROW = 8
+FLOPS = 2 * K * H * S + 2 * H * S * U
+BYTES = 2 * (K * T + 16 * T) + 4 * K * H + 4 * T + 4 * S + 2 * P * (S + U) // 16 + 4 * S * V
+
+
+def tile_picked_ycosm_cal_p_kernel(tc, x_words, x_scales, w1, e_words, e_scales, inv, own, offs, enr, out):
+    nc = tc.nc
+    with ExitStack() as ctx:
+        keep = ctx.enter_context(tc.tile_pool(name="keep", bufs=1))
+        psum = ctx.enter_context(tc.psum_pool(name="psum", bufs=1))
+
+        def sb(name, shape, dtype, tag=None):
+            return keep.tile(shape, dtype, name=name, tag=tag or name, align_bytes=64)
+
+        def bank(b, name, shape):
+            return psum.tile(shape, F32, name=name, tag="bank%d" % b)
+
+        offs_sb = keep.tile([P, S // 16], U16, name="offs_sb")
+        enr_sb = keep.tile([P, U // 16], U16, name="enr_sb")
+        xs_table = sb("xs_table", [P, T], U8)
+        es_table = sb("es_table", [P, T], U8)
+        inv_table = sb("inv_table", [P, T], F32)
+        xw_table = sb("xw_table", [P, T], I32)
+        ew_table = sb("ew_table", [P, T], I32)
+        own_sb = sb("own_sb", [P, FACE_TILES], F32)
+        ident = sb("ident", [P, P], F32)
+        minus_one = sb("minus_one", [P, 1], F32)
+
+        nc.gpsimd.memset(xs_table[:].bitcast(I32), 0)
+        nc.gpsimd.memset(minus_one[:], -1.0)
+        nc.vector.memset(inv_table[:], 0.0)
+        nc.vector.memset(es_table[:].bitcast(I32), 0)
+        make_identity(nc, ident[:])
+
+        def load_scales(table, scales, first):
+            for q in range(4):
+                nc.sync.dma_start(out=table[32 * q + first : 32 * q + first + 4, :].bitcast(I32), in_=scales[0, 4 * q : 4 * q + 4, :].bitcast(I32))
+
+        half = H // 2
+        w_raw = [sb("w_raw%d" % a, [P, 4, half], F32) for a in range(2)]
+        nc.sync.dma_start(offs_sb[:], offs)
+        nc.sync.dma_start(enr_sb[:], enr)
+        load_scales(xs_table, x_scales, 0)
+        nc.scalar.dma_start(out=inv_table[INV_ROW : INV_ROW + 1, :], in_=inv[0:1, :])
+        for a in range(2):
+            nc.sync.dma_start(out=w_raw[a][:], in_=w1[:, a * half : (a + 1) * half].rearrange("(p j) c -> p j c", j=4))
+        nc.sync.dma_start(out=xw_table[:], in_=x_words[0].rearrange("p n t -> p (n t)").bitcast(I32))
+        load_scales(es_table, e_scales, 4)
+        with nc.allow_non_contiguous_dma(reason="one value a face, faces on the partitions"):
+            nc.sync.dma_start(out=own_sb[:], in_=own.rearrange("(q p) o -> p (q o)", p=P))
+        nc.sync.dma_start(out=ew_table[:], in_=e_words[0].rearrange("p n t -> p (n t)").bitcast(I32))
+
+        warm = sb("warm", [P, 1], F32)
+        nc.scalar.activation(warm[:], minus_one[:], ACT.Sigmoid, bias=minus_one[:])
+
+        nonneg = sb("nonneg", [P, FACE_TILES], F32)
+        sign = sb("sign", [P, FACE_TILES], F32)
+        quarter_sign = sb("quarter_sign", [P, FACE_TILES], F32)
+        quarter_abs = sb("quarter_abs", [P, FACE_TILES], F32)
+        nc.gpsimd.tensor_scalar(nonneg[:], own_sb[:], 0.0, None, ALU.is_ge)
+        nc.gpsimd.tensor_scalar(sign[:], nonneg[:], 2.0, -1.0, ALU.mult, ALU.add)
+        nc.gpsimd.tensor_scalar(quarter_sign[:], nonneg[:], 0.5, -0.25, ALU.mult, ALU.add)
+        nc.gpsimd.tensor_tensor(quarter_abs[:], own_sb[:], quarter_sign[:], ALU.mult)
+
+        xs = sb("xs", [P, S], U8)
+        nc.vector.tensor_copy(xs[:], xs_table[:].indirect(offs_sb[:]))
+
+        inv_cols = []
+        for g in range(ID_TILES):
+            inv_listed = sb("inv_listed%d" % g, [P, D * P], F32)
+            nc.vector.tensor_copy(inv_listed[:], inv_table[:].indirect(enr_sb[:, g * 32 : (g + 1) * 32]))
+            turned = bank(6 + g, "inv_turned%d" % g, [P, D, P])
+            for d in range(D):
+                nc.tensor.transpose(turned[:, d, :], inv_listed[:, d : D * P : D], ident[:])
+            cols = sb("inv_cols%d" % g, [P, D], F32)
+            nc.scalar.copy(cols[:], turned[:, :, INV_ROW])
+            inv_cols.append(cols)
+
+        w_codes = sb("w_codes", [P, H], U32)
+        w_scales = sb("w_scales", [P, H], U8)
+        for a in range(2):
+            w_grouped = sb("w_grouped%d" % a, [P, half, 4], BF16)
+            nc.scalar.copy(w_grouped[:].rearrange("p (c i) j -> p c j i", i=4), w_raw[a][:].rearrange("p j (c i) -> p c j i", i=4))
+            cols = slice(a * half, (a + 1) * half)
+            nc.vector.quantize_mx(out=w_codes[:, cols].bitcast(FP8X4), scales=w_scales[:, cols], in_=w_grouped[:].rearrange("p c j -> p (c j)"))
+
+        xw = [sb("xw%d" % a, [P, S // 2], U32) for a in range(2)]
+        for a in range(2):
+            nc.vector.tensor_copy(xw[a][:], xw_table[:].bitcast(U32).indirect(offs_sb[:, a * 16 : (a + 1) * 16]))
+
+        h_codes = sb("h_codes", [P, S], U32)
+        h_scales = sb("h_scales", [P, S], U8)
+        h_grouped = []
+        for q in range(FACE_TILES):
+            acc = bank(q, "h_acc%d" % q, [P, H])
+            cols = slice(q * P, (q + 1) * P)
+            nc.tensor.matmul_mx(out=acc[:], lhsT=xw[q // 2][:, (q % 2) * P : (q % 2 + 1) * P].bitcast(FP8X4), lhsT_scale=xs[:, cols],
+                                rhs=w_codes[:].bitcast(FP8X4), rhs_scale=w_scales[:], start=True, stop=True)
+            h_rows = sb("h_rows%d" % q, [P, 2, P, 2], BF16)
+            nc.scalar.activation(h_rows[:], acc[:].rearrange("t (p u e) -> t u p e", u=2, e=2), ACT.Copy, scale=sign[:, q : q + 1])
+            h_pairs = h_rows[:].rearrange("t u p e -> t (u p e)").bitcast(F32)
+            turned = bank(4 + q, "h_turned%d" % q, [P, 2, P])
+            for u in range(2):
+                nc.tensor.transpose(turned[:, u, :], h_pairs[:, u * P : (u + 1) * P], ident[:])
+            grouped = sb("h_grouped%d" % q, [P, P * 4], BF16)
+            nc.scalar.copy(grouped[:].bitcast(F32).rearrange("p (t u) -> p t u", u=2), turned[:].rearrange("p u t -> p t u"))
+            h_grouped.append(grouped)
+
+        ew = []
+        es = []
+
+        def look_up_identities(g, tags):
+            entries = enr_sb[:, g * 32 : (g + 1) * 32]
+            listed = sb("es_listed%d" % g, [P, D * P], U8, tag=tags[0])
+            nc.vector.tensor_copy(listed[:], es_table[:].indirect(entries))
+            words = sb("ew%d" % g, [P, D, P], U32, tag=tags[1])
+            nc.vector.tensor_copy(words[:].rearrange("p d v -> p v d"), ew_table[:].bitcast(U32).indirect(entries))
+            ew.append(words)
+            scales = sb("es%d" % g, [P, D * P], U8)
+            nc.vector.tensor_copy(
+                scales[:].rearrange("p (d c i) -> p c d i", d=D, i=16),
+                listed[:].rearrange("p (c i d) -> p c d i", d=D, i=16),
+            )
+            es.append(scales)
+
+        look_up_identities(0, ("w_grouped1", None))
+        for q in range(FACE_TILES):
+            cols = slice(q * P, (q + 1) * P)
+            nc.vector.quantize_mx(out=h_codes[:, cols].bitcast(FP8X4), scales=h_scales[:, cols], in_=h_grouped[q][:])
+        look_up_identities(1, ("h_grouped2", "h_grouped3"))
+
+        y = {}
+        for g in range(ID_TILES):
+            for d in range(D):
+                acc = bank(4 * g + d, "y%d_%d" % (g, d), [P, S])
+                nc.tensor.matmul_mx(out=acc[:], lhsT=ew[g][:, d, :].bitcast(FP8X4), lhsT_scale=es[g][4:P, d * P : (d + 1) * P],
+                                    rhs=h_codes[:].bitcast(FP8X4), rhs_scale=h_scales[:], start=True, stop=True)
+                y[g, d] = acc
+
+        for g in range(ID_TILES):
+            z = []
+            for d in range(D):
+                zd = sb("z%d_%d" % (g, d), [P, S], F32)
+                nc.scalar.activation(zd[:], y[g, d][:], ACT.Copy, scale=inv_cols[g][:, d : d + 1])
+                z.append(zd)
+            z0_8 = sb("z0_8_%d" % g, [P, S], F32)
+            nc.vector.tensor_scalar(z0_8[:], z[0][:], 8.0, None, ALU.mult)
+            best01 = sb("best01_%d" % g, [P, S], F32)
+            nc.vector.scalar_tensor_tensor(best01[:], z[1][:], 8.0, z0_8[:], ALU.mult, ALU.max)
+            best012 = sb("best012_%d" % g, [P, S], F32)
+            nc.vector.scalar_tensor_tensor(best012[:], z[2][:], 8.0, best01[:], ALU.mult, ALU.max)
+            best = sb("best_%d" % g, [P, S], F32)
+            nc.vector.scalar_tensor_tensor(best[:], z[3][:], 8.0, best012[:], ALU.mult, ALU.max)
+            result = sb("result%d" % g, [P, FACE_TILES, P], F32)
+            for q in range(FACE_TILES):
+                total = bank(4 * g + q, "total%d_%d" % (g, q), [P, P])
+                terms = z + [best]
+                for n, term in enumerate(terms):
+                    nc.tensor.matmul(total[:], lhsT=term[:, q * P : (q + 1) * P], rhs=ident[:], is_transpose=True, start=(n == 0), stop=(n == len(terms) - 1))
+                nc.scalar.activation(result[:, q, :], total[:], ACT.Sigmoid, bias=minus_one[:], scale=quarter_abs[:, q : q + 1])
+            nc.sync.dma_start(out=out[:, g * P : (g + 1) * P].rearrange("(q p) v -> p q v", p=P), in_=result[:])

@@ -18,7 +18,8 @@ K, H, T, S, U, D = 512, 512, 2048, 512, 1024, 4
 V = U // D
 FACE_TILES = S // P
 ID_TILES = V // P
-INV_ROW = 8
+INV_ROW = 127
+OWN_ROW = 124
 FLOPS = 2 * K * H * S + 2 * H * S * U
 BYTES = 2 * (K * T + 16 * T) + 4 * K * H + 4 * T + 4 * S + 2 * P * (S + U) // 16 + 4 * S * V
 
@@ -42,75 +43,76 @@ def tile_picked_ycosm_cal_p_kernel(tc, x_words, x_scales, w1, e_words, e_scales,
         inv_table = sb("inv_table", [P, T], F32)
         xw_table = sb("xw_table", [P, T], I32)
         ew_table = sb("ew_table", [P, T], I32)
-        own_sb = sb("own_sb", [P, FACE_TILES], F32)
+        own_rows = sb("own_rows", [P, P], F32)
         ident = sb("ident", [P, P], F32)
         minus_one = sb("minus_one", [P, 1], F32)
 
-        nc.gpsimd.memset(xs_table[:].bitcast(I32), 0)
-        nc.gpsimd.memset(minus_one[:], -1.0)
-        nc.vector.memset(inv_table[:], 0.0)
-        nc.vector.memset(es_table[:].bitcast(I32), 0)
+        nc.gpsimd.memset(xs_table[:, 0 : T // 2].bitcast(I32), 0)
+        nc.vector.memset(xs_table[:, T // 2 : T].bitcast(I32), 0)
+        nc.vector.memset(minus_one[:], -1.0)
+        nc.vector.memset(inv_table[0:INV_ROW, :].bitcast(I32), 0)
+        nc.gpsimd.memset(es_table[:].bitcast(I32), 0)
+        nc.gpsimd.memset(own_rows[0:OWN_ROW, :], 0.0)
         make_identity(nc, ident[:])
 
         def load_scales(table, scales, first):
-            for q in range(4):
-                nc.sync.dma_start(out=table[32 * q + first : 32 * q + first + 4, :].bitcast(I32), in_=scales[0, 4 * q : 4 * q + 4, :].bitcast(I32))
+            for r in range(4):
+                nc.sync.dma_start(out=table[first + r : P : 32, :].bitcast(I32), in_=scales[0, r:16:4, :].bitcast(I32))
 
         half = H // 2
-        w_raw = [sb("w_raw%d" % a, [P, 4, half], F32) for a in range(2)]
+        w_raw = sb("w_raw", [P, 4, H], F32)
         nc.sync.dma_start(offs_sb[:], offs)
         nc.sync.dma_start(enr_sb[:], enr)
+        nc.sync.dma_start(out=inv_table[INV_ROW : INV_ROW + 1, :], in_=inv[0:1, :])
         load_scales(xs_table, x_scales, 0)
-        nc.scalar.dma_start(out=inv_table[INV_ROW : INV_ROW + 1, :], in_=inv[0:1, :])
-        for a in range(2):
-            nc.sync.dma_start(out=w_raw[a][:], in_=w1[:, a * half : (a + 1) * half].rearrange("(p j) c -> p j c", j=4))
-        nc.sync.dma_start(out=xw_table[:], in_=x_words[0].rearrange("p n t -> p (n t)").bitcast(I32))
+        nc.sync.dma_start(out=w_raw[:], in_=w1.rearrange("(p j) c -> p j c", j=4))
         load_scales(es_table, e_scales, 4)
-        with nc.allow_non_contiguous_dma(reason="one value a face, faces on the partitions"):
-            nc.sync.dma_start(out=own_sb[:], in_=own.rearrange("(q p) o -> p (q o)", p=P))
+        nc.sync.dma_start(out=own_rows[OWN_ROW : OWN_ROW + FACE_TILES, :], in_=own.rearrange("(q p) o -> q (p o)", p=P))
+        nc.sync.dma_start(out=xw_table[:], in_=x_words[0].rearrange("p n t -> p (n t)").bitcast(I32))
         nc.sync.dma_start(out=ew_table[:], in_=e_words[0].rearrange("p n t -> p (n t)").bitcast(I32))
 
         warm = sb("warm", [P, 1], F32)
         nc.scalar.activation(warm[:], minus_one[:], ACT.Sigmoid, bias=minus_one[:])
 
-        nonneg = sb("nonneg", [P, FACE_TILES], F32)
-        sign = sb("sign", [P, FACE_TILES], F32)
-        quarter_sign = sb("quarter_sign", [P, FACE_TILES], F32)
-        quarter_abs = sb("quarter_abs", [P, FACE_TILES], F32)
-        nc.gpsimd.tensor_scalar(nonneg[:], own_sb[:], 0.0, None, ALU.is_ge)
-        nc.gpsimd.tensor_scalar(sign[:], nonneg[:], 2.0, -1.0, ALU.mult, ALU.add)
-        nc.gpsimd.tensor_scalar(quarter_sign[:], nonneg[:], 0.5, -0.25, ALU.mult, ALU.add)
-        nc.gpsimd.tensor_tensor(quarter_abs[:], own_sb[:], quarter_sign[:], ALU.mult)
-
-        xs = sb("xs", [P, S], U8)
-        nc.vector.tensor_copy(xs[:], xs_table[:].indirect(offs_sb[:]))
-
-        inv_cols = []
+        inv_turned = []
         for g in range(ID_TILES):
             inv_listed = sb("inv_listed%d" % g, [P, D * P], F32)
             nc.vector.tensor_copy(inv_listed[:], inv_table[:].indirect(enr_sb[:, g * 32 : (g + 1) * 32]))
             turned = bank(6 + g, "inv_turned%d" % g, [P, D, P])
             for d in range(D):
                 nc.tensor.transpose(turned[:, d, :], inv_listed[:, d : D * P : D], ident[:])
-            cols = sb("inv_cols%d" % g, [P, D], F32)
-            nc.scalar.copy(cols[:], turned[:, :, INV_ROW])
-            inv_cols.append(cols)
+            inv_turned.append(turned)
+
+        xs = sb("xs", [P, S], U8)
+        nc.vector.tensor_copy(xs[:], xs_table[:].indirect(offs_sb[:]))
+
+        es_listed0 = sb("es_listed0", [P, D * P], U8)
+        nc.vector.tensor_copy(es_listed0[:], es_table[:].indirect(enr_sb[:, 0:32]))
 
         w_codes = sb("w_codes", [P, H], U32)
         w_scales = sb("w_scales", [P, H], U8)
         for a in range(2):
             w_grouped = sb("w_grouped%d" % a, [P, half, 4], BF16)
-            nc.scalar.copy(w_grouped[:].rearrange("p (c i) j -> p c j i", i=4), w_raw[a][:].rearrange("p j (c i) -> p c j i", i=4))
+            nc.scalar.copy(w_grouped[:].rearrange("p (c i) j -> p c j i", i=4), w_raw[:, :, a * half : (a + 1) * half].rearrange("p j (c i) -> p c j i", i=4))
             cols = slice(a * half, (a + 1) * half)
             nc.vector.quantize_mx(out=w_codes[:, cols].bitcast(FP8X4), scales=w_scales[:, cols], in_=w_grouped[:].rearrange("p c j -> p (c j)"))
+
+        inv_cols = sb("inv_cols", [P, ID_TILES, D], F32, tag="w_raw")
+        for g in range(ID_TILES):
+            nc.scalar.copy(inv_cols[:, g, :], inv_turned[g][:, :, INV_ROW])
+
+        own_turned = bank(6, "own_turned", [P, P])
+        nc.tensor.transpose(own_turned[:], own_rows[:], ident[:])
+        sign = sb("sign", [P, FACE_TILES], F32)
+        quarter_abs = sb("quarter_abs", [P, FACE_TILES], F32)
+        nc.scalar.activation(sign[:], own_turned[:, OWN_ROW : OWN_ROW + FACE_TILES], ACT.Sign)
+        nc.scalar.activation(quarter_abs[:], own_turned[:, OWN_ROW : OWN_ROW + FACE_TILES], ACT.Abs, scale=0.25)
 
         xw = [sb("xw%d" % a, [P, S // 2], U32) for a in range(2)]
         for a in range(2):
             nc.vector.tensor_copy(xw[a][:], xw_table[:].bitcast(U32).indirect(offs_sb[:, a * 16 : (a + 1) * 16]))
 
-        h_codes = sb("h_codes", [P, S], U32)
-        h_scales = sb("h_scales", [P, S], U8)
-        h_grouped = []
+        h_grouped = [sb("h_grouped%d" % a, [P, 2, P * 4], BF16) for a in range(2)]
         for q in range(FACE_TILES):
             acc = bank(q, "h_acc%d" % q, [P, H])
             cols = slice(q * P, (q + 1) * P)
@@ -122,60 +124,77 @@ def tile_picked_ycosm_cal_p_kernel(tc, x_words, x_scales, w1, e_words, e_scales,
             turned = bank(4 + q, "h_turned%d" % q, [P, 2, P])
             for u in range(2):
                 nc.tensor.transpose(turned[:, u, :], h_pairs[:, u * P : (u + 1) * P], ident[:])
-            grouped = sb("h_grouped%d" % q, [P, P * 4], BF16)
-            nc.scalar.copy(grouped[:].bitcast(F32).rearrange("p (t u) -> p t u", u=2), turned[:].rearrange("p u t -> p t u"))
-            h_grouped.append(grouped)
+            nc.scalar.copy(h_grouped[q // 2][:, q % 2, :].bitcast(F32).rearrange("p (t u) -> p t u", u=2), turned[:].rearrange("p u t -> p t u"))
 
-        ew = []
-        es = []
-
-        def look_up_identities(g, tags):
-            entries = enr_sb[:, g * 32 : (g + 1) * 32]
-            listed = sb("es_listed%d" % g, [P, D * P], U8, tag=tags[0])
-            nc.vector.tensor_copy(listed[:], es_table[:].indirect(entries))
-            words = sb("ew%d" % g, [P, D, P], U32, tag=tags[1])
-            nc.vector.tensor_copy(words[:].rearrange("p d v -> p v d"), ew_table[:].bitcast(U32).indirect(entries))
-            ew.append(words)
-            scales = sb("es%d" % g, [P, D * P], U8)
+        def deal_scales(name, listed, tag):
+            scales = sb(name, [P, D * P], U8, tag=tag)
             nc.vector.tensor_copy(
                 scales[:].rearrange("p (d c i) -> p c d i", d=D, i=16),
                 listed[:].rearrange("p (c i d) -> p c d i", d=D, i=16),
             )
-            es.append(scales)
+            return scales
 
-        look_up_identities(0, ("w_grouped1", None))
-        for q in range(FACE_TILES):
-            cols = slice(q * P, (q + 1) * P)
-            nc.vector.quantize_mx(out=h_codes[:, cols].bitcast(FP8X4), scales=h_scales[:, cols], in_=h_grouped[q][:])
-        look_up_identities(1, ("h_grouped2", "h_grouped3"))
+        def quantise_h(a, tag):
+            codes = sb("h_codes%d" % a, [P, 2 * P], U32, tag=tag)
+            scales = sb("h_scales%d" % a, [P, 2 * P], U8)
+            nc.vector.quantize_mx(out=codes[:].bitcast(FP8X4), scales=scales[:], in_=h_grouped[a][:].rearrange("p q c -> p (q c)"))
+            return codes, scales
 
-        y = {}
+        es = [deal_scales("es0", es_listed0, "xw_table")]
+        ew = sb("ew", [P, D, V], U32)
+        nc.vector.tensor_copy(ew[:].rearrange("p d v -> p v d"), ew_table[:].bitcast(U32).indirect(enr_sb[:]))
+        h_mx = [quantise_h(0, "ew_table")]
+        es_listed1 = sb("es_listed1", [P, D * P], U8, tag="h_grouped0")
+        nc.vector.tensor_copy(es_listed1[:], es_table[:].indirect(enr_sb[:, 32:64]))
+        h_mx.append(quantise_h(1, "es_table"))
+        es.append(deal_scales("es1", es_listed1, None))
+
+        HS = S // 2
+        z = {}
         for g in range(ID_TILES):
             for d in range(D):
-                acc = bank(4 * g + d, "y%d_%d" % (g, d), [P, S])
-                nc.tensor.matmul_mx(out=acc[:], lhsT=ew[g][:, d, :].bitcast(FP8X4), lhsT_scale=es[g][4:P, d * P : (d + 1) * P],
-                                    rhs=h_codes[:].bitcast(FP8X4), rhs_scale=h_scales[:], start=True, stop=True)
-                y[g, d] = acc
+                z[g, d] = sb("z%d_%d" % (g, d), [P, S], F32)
+
+        def product(acc, g, d, a):
+            nc.tensor.matmul_mx(out=acc, lhsT=ew[:, d, g * P : (g + 1) * P].bitcast(FP8X4), lhsT_scale=es[g][4:P, d * P : (d + 1) * P],
+                                rhs=h_mx[a][0][:].bitcast(FP8X4), rhs_scale=h_mx[a][1][:], start=True, stop=True)
+
+        reads = []
+        for a in range(2):
+            for pair in range(2):
+                acc = bank(2 * a + pair, "y0_%d_%d" % (a, pair), [P, 2, HS])
+                for e in range(2):
+                    product(acc[:, e, :], 0, 2 * pair + e, a)
+                    reads.append((z[0, 2 * pair + e][:, a * HS : (a + 1) * HS], acc[:, e, :], 0, 2 * pair + e))
+        for d in range(D):
+            acc = bank(4 + d, "y1_%d" % d, [P, 2, HS])
+            for a in range(2):
+                product(acc[:, a, :], 1, d, a)
+            reads.append((z[1, d][:], acc[:].rearrange("p a t -> p (a t)"), 1, d))
+        for target, source, g, d in reads:
+            nc.scalar.activation(target, source, ACT.Copy, scale=inv_cols[:, g, d : d + 1])
 
         for g in range(ID_TILES):
-            z = []
+            chain = [sb("best%d_%d" % (g, d), [P, S], F32) for d in range(D)]
             for d in range(D):
-                zd = sb("z%d_%d" % (g, d), [P, S], F32)
-                nc.scalar.activation(zd[:], y[g, d][:], ACT.Copy, scale=inv_cols[g][:, d : d + 1])
-                z.append(zd)
-            z0_8 = sb("z0_8_%d" % g, [P, S], F32)
-            nc.vector.tensor_scalar(z0_8[:], z[0][:], 8.0, None, ALU.mult)
-            best01 = sb("best01_%d" % g, [P, S], F32)
-            nc.vector.scalar_tensor_tensor(best01[:], z[1][:], 8.0, z0_8[:], ALU.mult, ALU.max)
-            best012 = sb("best012_%d" % g, [P, S], F32)
-            nc.vector.scalar_tensor_tensor(best012[:], z[2][:], 8.0, best01[:], ALU.mult, ALU.max)
-            best = sb("best_%d" % g, [P, S], F32)
-            nc.vector.scalar_tensor_tensor(best[:], z[3][:], 8.0, best012[:], ALU.mult, ALU.max)
-            result = sb("result%d" % g, [P, FACE_TILES, P], F32)
-            for q in range(FACE_TILES):
-                total = bank(4 * g + q, "total%d_%d" % (g, q), [P, P])
-                terms = z + [best]
+                for a in range(2):
+                    cols = slice(a * HS, (a + 1) * HS)
+                    if d == 0:
+                        nc.vector.tensor_scalar(chain[0][:, cols], z[g, 0][:, cols], 8.0, None, ALU.mult)
+                    else:
+                        nc.vector.scalar_tensor_tensor(chain[d][:, cols], z[g, d][:, cols], 8.0, chain[d - 1][:, cols], ALU.mult, ALU.max)
+            result = sb("result%d" % g, [P, FACE_TILES, P], F32, tag="w_raw" if g == 0 else None)
+            terms = [z[g, d] for d in range(D)] + [chain[D - 1]]
+            for a in range(2):
+                total = bank(2 * a + g, "total%d_%d" % (g, a), [P, 2, P])
                 for n, term in enumerate(terms):
-                    nc.tensor.matmul(total[:], lhsT=term[:, q * P : (q + 1) * P], rhs=ident[:], is_transpose=True, start=(n == 0), stop=(n == len(terms) - 1))
-                nc.scalar.activation(result[:, q, :], total[:], ACT.Sigmoid, bias=minus_one[:], scale=quarter_abs[:, q : q + 1])
-            nc.sync.dma_start(out=out[:, g * P : (g + 1) * P].rearrange("(q p) v -> p q v", p=P), in_=result[:])
+                    for e in range(2):
+                        q = 2 * a + e
+                        nc.tensor.matmul(total[:, e, :], lhsT=term[:, q * P : (q + 1) * P], rhs=ident[:], is_transpose=True, start=(n == 0 and e == 0), stop=(n == len(terms) - 1 and e == 1))
+                for e in range(2):
+                    q = 2 * a + e
+                    nc.scalar.activation(result[:, q, :], total[:, e, :], ACT.Sigmoid, bias=minus_one[:], scale=quarter_abs[:, q : q + 1])
+            pieces = g + 1
+            for a in range(pieces):
+                tiles = slice(a * FACE_TILES // pieces, (a + 1) * FACE_TILES // pieces)
+                nc.sync.dma_start(out=out[:, g * P : (g + 1) * P].rearrange("(q p) v -> p q v", p=P)[:, tiles, :], in_=result[:, tiles, :])

@@ -134,6 +134,14 @@ def tile_picked_ycosm_cal_p_kernel(tc, x_words, x_scales, w1, e_words, e_scales,
             )
             return scales
 
+        def deal_words(g):
+            words = sb("ew%d" % g, [P, D * P], U32)
+            nc.vector.tensor_copy(
+                words[:].rearrange("p (d c i) -> p c d i", d=D, i=4),
+                ew_listed[:, g * D * P : (g + 1) * D * P].rearrange("p (c i d) -> p c d i", d=D, i=4),
+            )
+            return words
+
         def quantise_h(a, tag):
             codes = sb("h_codes%d" % a, [P, 2 * P], U32, tag=tag)
             scales = sb("h_scales%d" % a, [P, 2 * P], U8)
@@ -141,12 +149,14 @@ def tile_picked_ycosm_cal_p_kernel(tc, x_words, x_scales, w1, e_words, e_scales,
             return codes, scales
 
         es = [deal_scales("es0", es_listed0, "xw_table")]
-        ew = sb("ew", [P, D, V], U32)
-        nc.vector.tensor_copy(ew[:].rearrange("p d v -> p v d"), ew_table[:].bitcast(U32).indirect(enr_sb[:]))
+        ew_listed = sb("ew_listed", [P, U], U32)
+        nc.vector.tensor_copy(ew_listed[:], ew_table[:].bitcast(U32).indirect(enr_sb[:]))
+        ew = [deal_words(0)]
         h_mx = [quantise_h(0, "ew_table")]
         es_listed1 = sb("es_listed1", [P, D * P], U8, tag="h_grouped0")
         nc.vector.tensor_copy(es_listed1[:], es_table[:].indirect(enr_sb[:, 32:64]))
         h_mx.append(quantise_h(1, "es_table"))
+        ew.append(deal_words(1))
         es.append(deal_scales("es1", es_listed1, None))
 
         HS = S // 2
@@ -156,7 +166,7 @@ def tile_picked_ycosm_cal_p_kernel(tc, x_words, x_scales, w1, e_words, e_scales,
                 z[g, d] = sb("z%d_%d" % (g, d), [P, S], F32)
 
         def product(acc, g, d, a):
-            nc.tensor.matmul_mx(out=acc, lhsT=ew[:, d, g * P : (g + 1) * P].bitcast(FP8X4), lhsT_scale=es[g][4:P, d * P : (d + 1) * P],
+            nc.tensor.matmul_mx(out=acc, lhsT=ew[g][:, d * P : (d + 1) * P].bitcast(FP8X4), lhsT_scale=es[g][4:P, d * P : (d + 1) * P],
                                 rhs=h_mx[a][0][:].bitcast(FP8X4), rhs_scale=h_mx[a][1][:], start=True, stop=True)
 
         reads = []
@@ -170,7 +180,11 @@ def tile_picked_ycosm_cal_p_kernel(tc, x_words, x_scales, w1, e_words, e_scales,
             acc = bank(4 + d, "y1_%d" % d, [P, 2, HS])
             for a in range(2):
                 product(acc[:, a, :], 1, d, a)
-            reads.append((z[1, d][:], acc[:].rearrange("p a t -> p (a t)"), 1, d))
+            if d < D - 1:
+                reads.append((z[1, d][:], acc[:].rearrange("p a t -> p (a t)"), 1, d))
+            else:
+                for a in range(2):
+                    reads.append((z[1, d][:, a * HS : (a + 1) * HS], acc[:, a, :], 1, d))
         for target, source, g, d in reads:
             nc.scalar.activation(target, source, ACT.Copy, scale=inv_cols[:, g, d : d + 1])
 

@@ -14,14 +14,23 @@ ALU = mybir.AluOpType
 ACT = mybir.ActivationFunctionType
 
 P = 128
-K, H, T, S, U, D = 512, 512, 2048, 512, 1024, 4
-V = U // D
-FACE_TILES = S // P
-ID_TILES = V // P
-INV_ROW = 127
-OWN_ROW = 124
-FLOPS = 2 * K * H * S + 2 * H * S * U
-BYTES = 2 * (K * T + 16 * T) + 4 * K * H + 4 * T + 4 * S + 2 * P * (S + U) // 16 + 4 * S * V
+K, H = 512, 512
+TABLE = 2048
+FACES, ENTRIES, D = 512, 1024, 4
+PACK = 4
+STRIPE = 16
+SCALE_ROWS = K // 32
+FACE_TILES = FACES // P
+ID_TILES = ENTRIES // (D * P)
+ID_ENTRIES = D * P
+HALF = FACES // 2
+E_SCALE_ROW = 4
+INV_ROW = P - 1
+OWN_ROW = P - FACE_TILES
+BEST_WEIGHT = 2.0 * D
+
+FLOPS = 2 * K * H * FACES + 2 * H * FACES * ENTRIES
+BYTES = 2 * (K + SCALE_ROWS) * TABLE + 4 * K * H + 4 * TABLE + 4 * FACES + 2 * P * (FACES + ENTRIES) // STRIPE + 4 * FACES * ENTRIES // D
 
 
 def tile_picked_ycosm_cal_p_kernel(tc, x_words, x_scales, w1, e_words, e_scales, inv, own, offs, enr, out):
@@ -30,185 +39,202 @@ def tile_picked_ycosm_cal_p_kernel(tc, x_words, x_scales, w1, e_words, e_scales,
         keep = ctx.enter_context(tc.tile_pool(name="keep", bufs=1))
         psum = ctx.enter_context(tc.psum_pool(name="psum", bufs=1))
 
-        def sb(name, shape, dtype, tag=None):
-            return keep.tile(shape, dtype, name=name, tag=tag or name, align_bytes=64)
+        def sb(name, shape, dtype, after=None):
+            return keep.tile(shape, dtype, name=name, tag=after or name, align_bytes=64)
 
         def bank(b, name, shape):
             return psum.tile(shape, F32, name=name, tag="bank%d" % b)
 
-        offs_sb = keep.tile([P, S // 16], U16, name="offs_sb")
-        enr_sb = keep.tile([P, U // 16], U16, name="enr_sb")
-        xs_table = sb("xs_table", [P, T], U8)
-        es_table = sb("es_table", [P, T], U8)
-        inv_table = sb("inv_table", [P, T], F32)
-        xw_table = sb("xw_table", [P, T], I32)
-        ew_table = sb("ew_table", [P, T], I32)
+        offs_sb = keep.tile([P, FACES // STRIPE], U16, name="offs_sb")
+        enr_sb = keep.tile([P, ENTRIES // STRIPE], U16, name="enr_sb")
+        xs_table = sb("xs_table", [P, TABLE], U8)
+        es_table = sb("es_table", [P, TABLE], U8)
+        inv_table = sb("inv_table", [P, TABLE], F32)
+        xw_table = sb("xw_table", [P, TABLE], I32)
+        ew_table = sb("ew_table", [P, TABLE], I32)
         own_rows = sb("own_rows", [P, P], F32)
         ident = sb("ident", [P, P], F32)
         minus_one = sb("minus_one", [P, 1], F32)
 
-        nc.gpsimd.memset(xs_table[:, 0 : T // 2].bitcast(I32), 0)
-        nc.vector.memset(xs_table[:, T // 2 : T].bitcast(I32), 0)
+        nc.gpsimd.memset(xs_table[:, 0 : TABLE // 2].bitcast(I32), 0)
+        nc.vector.memset(xs_table[:, TABLE // 2 : TABLE].bitcast(I32), 0)
         nc.vector.memset(minus_one[:], -1.0)
         nc.vector.memset(inv_table[0:INV_ROW, :].bitcast(I32), 0)
         nc.gpsimd.memset(es_table[:].bitcast(I32), 0)
         nc.gpsimd.memset(own_rows[0:OWN_ROW, :], 0.0)
         make_identity(nc, ident[:])
 
-        def load_scales(table, scales, first):
+        def load_scales(table, scales, first_row):
             for r in range(4):
-                nc.sync.dma_start(out=table[first + r : P : 32, :].bitcast(I32), in_=scales[0, r:16:4, :].bitcast(I32))
+                nc.sync.dma_start(out=table[first_row + r : P : 32, :].bitcast(I32), in_=scales[0, r:SCALE_ROWS:4, :].bitcast(I32))
 
-        half = H // 2
-        w_raw = sb("w_raw", [P, 4, H], F32)
+        def list_slice(list_sb, first, count):
+            return list_sb[:, first // STRIPE : (first + count) // STRIPE]
+
+        w_raw = sb("w_raw", [P, PACK, H], F32)
         nc.sync.dma_start(offs_sb[:], offs)
         nc.sync.dma_start(enr_sb[:], enr)
         nc.sync.dma_start(out=inv_table[INV_ROW : INV_ROW + 1, :], in_=inv[0:1, :])
         load_scales(xs_table, x_scales, 0)
-        nc.sync.dma_start(out=w_raw[:], in_=w1.rearrange("(p j) c -> p j c", j=4))
-        load_scales(es_table, e_scales, 4)
-        nc.sync.dma_start(out=own_rows[OWN_ROW : OWN_ROW + FACE_TILES, :], in_=own.rearrange("(q p) o -> q (p o)", p=P))
+        nc.sync.dma_start(out=w_raw[:], in_=w1.rearrange("(p j) c -> p j c", j=PACK))
+        load_scales(es_table, e_scales, E_SCALE_ROW)
+        nc.sync.dma_start(out=own_rows[OWN_ROW:P, :], in_=own.rearrange("(q p) o -> q (p o)", p=P))
         nc.sync.dma_start(out=xw_table[:], in_=x_words[0].rearrange("p n t -> p (n t)").bitcast(I32))
         nc.sync.dma_start(out=ew_table[:], in_=e_words[0].rearrange("p n t -> p (n t)").bitcast(I32))
 
-        warm = sb("warm", [P, 1], F32)
-        nc.scalar.activation(warm[:], minus_one[:], ACT.Sigmoid, bias=minus_one[:])
-
         inv_turned = []
         for g in range(ID_TILES):
-            inv_listed = sb("inv_listed%d" % g, [P, D * P], F32)
-            nc.vector.tensor_copy(inv_listed[:], inv_table[:].indirect(enr_sb[:, g * 32 : (g + 1) * 32]))
+            inv_listed = sb("inv_listed%d" % g, [P, ID_ENTRIES], F32)
+            nc.vector.tensor_copy(inv_listed[:], inv_table[:].indirect(list_slice(enr_sb, g * ID_ENTRIES, ID_ENTRIES)))
             turned = bank(6 + g, "inv_turned%d" % g, [P, D, P])
             for d in range(D):
-                nc.tensor.transpose(turned[:, d, :], inv_listed[:, d : D * P : D], ident[:])
+                nc.tensor.transpose(turned[:, d, :], inv_listed[:, d:ID_ENTRIES:D], ident[:])
             inv_turned.append(turned)
 
-        xs = sb("xs", [P, S], U8)
+        xs = sb("xs", [P, FACES], U8)
         nc.vector.tensor_copy(xs[:], xs_table[:].indirect(offs_sb[:]))
 
-        es_listed0 = sb("es_listed0", [P, D * P], U8)
-        nc.vector.tensor_copy(es_listed0[:], es_table[:].indirect(enr_sb[:, 0:32]))
+        es_listed0 = sb("es_listed0", [P, ID_ENTRIES], U8)
+        nc.vector.tensor_copy(es_listed0[:], es_table[:].indirect(list_slice(enr_sb, 0, ID_ENTRIES)))
 
         w_codes = sb("w_codes", [P, H], U32)
         w_scales = sb("w_scales", [P, H], U8)
         for a in range(2):
-            w_grouped = sb("w_grouped%d" % a, [P, half, 4], BF16)
-            nc.scalar.copy(w_grouped[:].rearrange("p (c i) j -> p c j i", i=4), w_raw[:, :, a * half : (a + 1) * half].rearrange("p j (c i) -> p c j i", i=4))
-            cols = slice(a * half, (a + 1) * half)
+            cols = slice(a * HALF, (a + 1) * HALF)
+            w_grouped = sb("w_grouped%d" % a, [P, HALF, PACK], BF16)
+            nc.scalar.copy(w_grouped[:].rearrange("p (c i) j -> p c j i", i=4), w_raw[:, :, cols].rearrange("p j (c i) -> p c j i", i=4))
             nc.vector.quantize_mx(out=w_codes[:, cols].bitcast(FP8X4), scales=w_scales[:, cols], in_=w_grouped[:].rearrange("p c j -> p (c j)"))
 
-        inv_cols = sb("inv_cols", [P, ID_TILES, D], F32, tag="w_raw")
+        inv_cols = sb("inv_cols", [P, ID_TILES, D], F32, after="w_raw")
         for g in range(ID_TILES):
             nc.scalar.copy(inv_cols[:, g, :], inv_turned[g][:, :, INV_ROW])
+        inv_once = sb("inv_once", [P, ID_TILES, D], F32)
+        inv_eight = sb("inv_eight", [P, ID_TILES, D], F32)
+        nc.scalar.copy(inv_once[:], inv_cols[:])
+        nc.scalar.activation(inv_eight[:], inv_cols[:], ACT.Copy, scale=BEST_WEIGHT)
 
         own_turned = bank(6, "own_turned", [P, P])
         nc.tensor.transpose(own_turned[:], own_rows[:], ident[:])
         sign = sb("sign", [P, FACE_TILES], F32)
         quarter_abs = sb("quarter_abs", [P, FACE_TILES], F32)
-        nc.scalar.activation(sign[:], own_turned[:, OWN_ROW : OWN_ROW + FACE_TILES], ACT.Sign)
-        nc.scalar.activation(quarter_abs[:], own_turned[:, OWN_ROW : OWN_ROW + FACE_TILES], ACT.Abs, scale=0.25)
+        nc.scalar.activation(sign[:], own_turned[:, OWN_ROW:P], ACT.Sign)
+        nc.scalar.activation(quarter_abs[:], own_turned[:, OWN_ROW:P], ACT.Abs, scale=1.0 / D)
 
-        xw = [sb("xw%d" % a, [P, S // 2], U32) for a in range(2)]
+        xw = [sb("xw%d" % a, [P, HALF], U32) for a in range(2)]
         for a in range(2):
-            nc.vector.tensor_copy(xw[a][:], xw_table[:].bitcast(U32).indirect(offs_sb[:, a * 16 : (a + 1) * 16]))
+            nc.vector.tensor_copy(xw[a][:], xw_table[:].bitcast(U32).indirect(list_slice(offs_sb, a * HALF, HALF)))
 
-        h_grouped = [sb("h_grouped%d" % a, [P, 2, P * 4], BF16) for a in range(2)]
+        h_grouped = [sb("h_grouped%d" % a, [P, 2, P * PACK], BF16) for a in range(2)]
         for q in range(FACE_TILES):
+            a, within = divmod(q, 2)
             acc = bank(q, "h_acc%d" % q, [P, H])
-            cols = slice(q * P, (q + 1) * P)
-            nc.tensor.matmul_mx(out=acc[:], lhsT=xw[q // 2][:, (q % 2) * P : (q % 2 + 1) * P].bitcast(FP8X4), lhsT_scale=xs[:, cols],
-                                rhs=w_codes[:].bitcast(FP8X4), rhs_scale=w_scales[:], start=True, stop=True)
+            nc.tensor.matmul_mx(
+                out=acc[:],
+                lhsT=xw[a][:, within * P : (within + 1) * P].bitcast(FP8X4),
+                lhsT_scale=xs[:, q * P : (q + 1) * P],
+                rhs=w_codes[:].bitcast(FP8X4),
+                rhs_scale=w_scales[:],
+                start=True,
+                stop=True,
+            )
             h_rows = sb("h_rows%d" % q, [P, 2, P, 2], BF16)
             nc.scalar.activation(h_rows[:], acc[:].rearrange("t (p u e) -> t u p e", u=2, e=2), ACT.Copy, scale=sign[:, q : q + 1])
             h_pairs = h_rows[:].rearrange("t u p e -> t (u p e)").bitcast(F32)
-            turned = bank(4 + q, "h_turned%d" % q, [P, 2, P])
+            turned = bank(FACE_TILES + q, "h_turned%d" % q, [P, 2, P])
             for u in range(2):
                 nc.tensor.transpose(turned[:, u, :], h_pairs[:, u * P : (u + 1) * P], ident[:])
-            nc.scalar.copy(h_grouped[q // 2][:, q % 2, :].bitcast(F32).rearrange("p (t u) -> p t u", u=2), turned[:].rearrange("p u t -> p t u"))
+            nc.scalar.copy(h_grouped[a][:, within, :].bitcast(F32).rearrange("p (t u) -> p t u", u=2), turned[:].rearrange("p u t -> p t u"))
 
-        def deal_scales(name, listed, tag):
-            scales = sb(name, [P, D * P], U8, tag=tag)
+        def deal(name, listed, dtype, run, after=None):
+            dealt = sb(name, [P, ID_ENTRIES], dtype, after=after)
             nc.vector.tensor_copy(
-                scales[:].rearrange("p (d c i) -> p c d i", d=D, i=16),
-                listed[:].rearrange("p (c i d) -> p c d i", d=D, i=16),
+                dealt[:].rearrange("p (d c i) -> p c d i", d=D, i=run),
+                listed.rearrange("p (c i d) -> p c d i", d=D, i=run),
             )
-            return scales
+            return dealt
 
-        def deal_words(g):
-            words = sb("ew%d" % g, [P, D * P], U32)
-            nc.vector.tensor_copy(
-                words[:].rearrange("p (d c i) -> p c d i", d=D, i=4),
-                ew_listed[:, g * D * P : (g + 1) * D * P].rearrange("p (c i d) -> p c d i", d=D, i=4),
-            )
-            return words
-
-        def quantise_h(a, tag):
-            codes = sb("h_codes%d" % a, [P, 2 * P], U32, tag=tag)
-            scales = sb("h_scales%d" % a, [P, 2 * P], U8)
+        def quantise_h(a, after):
+            codes = sb("h_codes%d" % a, [P, HALF], U32, after=after)
+            scales = sb("h_scales%d" % a, [P, HALF], U8)
             nc.vector.quantize_mx(out=codes[:].bitcast(FP8X4), scales=scales[:], in_=h_grouped[a][:].rearrange("p q c -> p (q c)"))
             return codes, scales
 
-        es = [deal_scales("es0", es_listed0, "xw_table")]
-        ew_listed = sb("ew_listed", [P, U], U32)
+        es = [deal("es0", es_listed0[:], U8, 16, after="xw_table")]
+        ew_listed = sb("ew_listed", [P, ENTRIES], U32)
         nc.vector.tensor_copy(ew_listed[:], ew_table[:].bitcast(U32).indirect(enr_sb[:]))
-        ew = [deal_words(0)]
-        h_mx = [quantise_h(0, "ew_table")]
-        es_listed1 = sb("es_listed1", [P, D * P], U8, tag="h_grouped0")
-        nc.vector.tensor_copy(es_listed1[:], es_table[:].indirect(enr_sb[:, 32:64]))
-        h_mx.append(quantise_h(1, "es_table"))
-        ew.append(deal_words(1))
-        es.append(deal_scales("es1", es_listed1, None))
-
-        HS = S // 2
-        z = {}
-        for g in range(ID_TILES):
-            for d in range(D):
-                z[g, d] = sb("z%d_%d" % (g, d), [P, S], F32)
+        ew = [deal("ew0", ew_listed[:, 0:ID_ENTRIES], U32, 4)]
+        h_mx = [quantise_h(0, after="ew_table")]
+        es_listed1 = sb("es_listed1", [P, ID_ENTRIES], U8, after="h_grouped0")
+        nc.vector.tensor_copy(es_listed1[:], es_table[:].indirect(list_slice(enr_sb, ID_ENTRIES, ID_ENTRIES)))
+        h_mx.append(quantise_h(1, after="es_table"))
+        ew.append(deal("ew1", ew_listed[:, ID_ENTRIES:ENTRIES], U32, 4))
+        es.append(deal("es1", es_listed1[:], U8, 16))
 
         def product(acc, g, d, a):
-            nc.tensor.matmul_mx(out=acc, lhsT=ew[g][:, d * P : (d + 1) * P].bitcast(FP8X4), lhsT_scale=es[g][4:P, d * P : (d + 1) * P],
-                                rhs=h_mx[a][0][:].bitcast(FP8X4), rhs_scale=h_mx[a][1][:], start=True, stop=True)
+            cols = slice(d * P, (d + 1) * P)
+            nc.tensor.matmul_mx(
+                out=acc,
+                lhsT=ew[g][:, cols].bitcast(FP8X4),
+                lhsT_scale=es[g][E_SCALE_ROW:P, cols],
+                rhs=h_mx[a][0][:].bitcast(FP8X4),
+                rhs_scale=h_mx[a][1][:],
+                start=True,
+                stop=True,
+            )
 
-        reads = []
+        y = {}
         for a in range(2):
-            for pair in range(2):
-                acc = bank(2 * a + pair, "y0_%d_%d" % (a, pair), [P, 2, HS])
-                for e in range(2):
-                    product(acc[:, e, :], 0, 2 * pair + e, a)
-                    reads.append((z[0, 2 * pair + e][:, a * HS : (a + 1) * HS], acc[:, e, :], 0, 2 * pair + e))
+            for odd in range(2):
+                acc = bank(2 * a + odd, "y0_%d_%d" % (a, odd), [P, 2, HALF])
+                for pair in range(2):
+                    product(acc[:, pair, :], 0, 2 * pair + odd, a)
+                    y[0, 2 * pair + odd, a] = acc[:, pair, :]
+        y1_both_halves = {}
         for d in range(D):
-            acc = bank(4 + d, "y1_%d" % d, [P, 2, HS])
+            acc = bank(4 + d, "y1_%d" % d, [P, 2, HALF])
             for a in range(2):
                 product(acc[:, a, :], 1, d, a)
-            if d < D - 1:
-                reads.append((z[1, d][:], acc[:].rearrange("p a t -> p (a t)"), 1, d))
-            else:
-                for a in range(2):
-                    reads.append((z[1, d][:, a * HS : (a + 1) * HS], acc[:, a, :], 1, d))
-        for target, source, g, d in reads:
-            nc.scalar.activation(target, source, ACT.Copy, scale=inv_cols[:, g, d : d + 1])
+                y[1, d, a] = acc[:, a, :]
+            y1_both_halves[d] = acc[:].rearrange("p a t -> p (a t)")
+
+        names = ("z0", "z0_eight", "z2", "sum01", "best01", "best012", "sum23", "best")
+        work = [dict((n, sb("%s_%d" % (n, g), [P, FACES], F32)) for n in names) for g in range(ID_TILES)]
+
+        def read_even_templates(g, cols, y0, y2):
+            nc.scalar.activation(work[g]["z0_eight"][:, cols], y0, ACT.Copy, scale=inv_eight[:, g, 0:1])
+            nc.scalar.activation(work[g]["z0"][:, cols], y0, ACT.Copy, scale=inv_cols[:, g, 0:1])
+            nc.scalar.activation(work[g]["z2"][:, cols], y2, ACT.Copy, scale=inv_cols[:, g, 2:3])
+
+        for a in range(2):
+            read_even_templates(0, slice(a * HALF, (a + 1) * HALF), y[0, 0, a], y[0, 2, a])
+        read_even_templates(1, slice(0, FACES), y1_both_halves[0], y1_both_halves[2])
 
         for g in range(ID_TILES):
-            chain = [sb("best%d_%d" % (g, d), [P, S], F32) for d in range(D)]
-            for d in range(D):
-                for a in range(2):
-                    cols = slice(a * HS, (a + 1) * HS)
-                    if d == 0:
-                        nc.vector.tensor_scalar(chain[0][:, cols], z[g, 0][:, cols], 8.0, None, ALU.mult)
-                    else:
-                        nc.vector.scalar_tensor_tensor(chain[d][:, cols], z[g, d][:, cols], 8.0, chain[d - 1][:, cols], ALU.mult, ALU.max)
-            result = sb("result%d" % g, [P, FACE_TILES, P], F32, tag="w_raw" if g == 0 else None)
-            terms = [z[g, d] for d in range(D)] + [chain[D - 1]]
+            w = work[g]
+            for a in range(2):
+                cols = slice(a * HALF, (a + 1) * HALF)
+                nc.vector.scalar_tensor_tensor(w["best01"][:, cols], y[g, 1, a], inv_eight[:, g, 1:2], w["z0_eight"][:, cols], ALU.mult, ALU.max)
+                nc.vector.scalar_tensor_tensor(w["sum01"][:, cols], y[g, 1, a], inv_once[:, g, 1:2], w["z0"][:, cols], ALU.mult, ALU.add)
+                nc.vector.scalar_tensor_tensor(w["best012"][:, cols], w["z2"][:, cols], BEST_WEIGHT, w["best01"][:, cols], ALU.mult, ALU.max)
+                nc.vector.scalar_tensor_tensor(w["sum23"][:, cols], y[g, 3, a], inv_once[:, g, 3:4], w["z2"][:, cols], ALU.mult, ALU.add)
+                nc.vector.scalar_tensor_tensor(w["best"][:, cols], y[g, 3, a], inv_eight[:, g, 3:4], w["best012"][:, cols], ALU.mult, ALU.max)
+            result = sb("result%d" % g, [P, FACE_TILES, P], F32, after="w_raw" if g == 0 else None)
+            terms = [w["sum01"], w["sum23"], w["best"]]
             for a in range(2):
                 total = bank(2 * a + g, "total%d_%d" % (g, a), [P, 2, P])
                 for n, term in enumerate(terms):
-                    for e in range(2):
-                        q = 2 * a + e
-                        nc.tensor.matmul(total[:, e, :], lhsT=term[:, q * P : (q + 1) * P], rhs=ident[:], is_transpose=True, start=(n == 0 and e == 0), stop=(n == len(terms) - 1 and e == 1))
-                for e in range(2):
-                    q = 2 * a + e
-                    nc.scalar.activation(result[:, q, :], total[:, e, :], ACT.Sigmoid, bias=minus_one[:], scale=quarter_abs[:, q : q + 1])
-            pieces = g + 1
-            for a in range(pieces):
-                tiles = slice(a * FACE_TILES // pieces, (a + 1) * FACE_TILES // pieces)
+                    for within in range(2):
+                        q = 2 * a + within
+                        nc.tensor.matmul(
+                            total[:, within, :],
+                            lhsT=term[:, q * P : (q + 1) * P],
+                            rhs=ident[:],
+                            is_transpose=True,
+                            start=(n == 0 and within == 0),
+                            stop=(n == len(terms) - 1 and within == 1),
+                        )
+                for within in range(2):
+                    q = 2 * a + within
+                    nc.scalar.activation(result[:, q, :], total[:, within, :], ACT.Sigmoid, bias=minus_one[:], scale=quarter_abs[:, q : q + 1])
+                tiles = slice(2 * a, 2 * a + 2)
                 nc.sync.dma_start(out=out[:, g * P : (g + 1) * P].rearrange("(q p) v -> p q v", p=P)[:, tiles, :], in_=result[:, tiles, :])

@@ -56,13 +56,14 @@ def tile_picked_ycosm_cal_p_kernel(tc, x_words, x_scales, w1, e_words, e_scales,
         ident = sb("ident", [P, P], F32)
         minus_one = sb("minus_one", [P, 1], F32)
 
-        nc.gpsimd.memset(xs_table[:, 0 : TABLE // 2].bitcast(I32), 0)
-        nc.vector.memset(xs_table[:, TABLE // 2 : TABLE].bitcast(I32), 0)
+        nc.gpsimd.memset(xs_table[:].bitcast(I32), 0)
         nc.vector.memset(minus_one[:], -1.0)
         nc.vector.memset(inv_table[0:INV_ROW, :].bitcast(I32), 0)
-        nc.gpsimd.memset(es_table[:].bitcast(I32), 0)
         nc.gpsimd.memset(own_rows[0:OWN_ROW, :], 0.0)
+        nc.gpsimd.memset(es_table[:].bitcast(I32), 0)
         make_identity(nc, ident[:])
+        warm = sb("warm", [P, 1], F32)
+        nc.scalar.activation(warm[:], minus_one[:], ACT.Sigmoid)
 
         def load_scales(table, scales, first_row):
             for r in range(4):
@@ -71,104 +72,130 @@ def tile_picked_ycosm_cal_p_kernel(tc, x_words, x_scales, w1, e_words, e_scales,
         def list_slice(list_sb, first, count):
             return list_sb[:, first // STRIPE : (first + count) // STRIPE]
 
-        w_raw = sb("w_raw", [P, PACK, H], F32)
-        nc.sync.dma_start(offs_sb[:], offs)
+        w_raw = [sb("w_raw%d" % a, [P, PACK, HALF], F32) for a in range(2)]
         nc.sync.dma_start(enr_sb[:], enr)
         nc.sync.dma_start(out=inv_table[INV_ROW : INV_ROW + 1, :], in_=inv[0:1, :])
-        load_scales(xs_table, x_scales, 0)
-        nc.sync.dma_start(out=w_raw[:], in_=w1.rearrange("(p j) c -> p j c", j=PACK))
-        load_scales(es_table, e_scales, E_SCALE_ROW)
-        nc.sync.dma_start(out=own_rows[OWN_ROW:P, :], in_=own.rearrange("(q p) o -> q (p o)", p=P))
+        nc.sync.dma_start(offs_sb[:], offs)
         nc.sync.dma_start(out=xw_table[:], in_=x_words[0].rearrange("p n t -> p (n t)").bitcast(I32))
+        load_scales(xs_table, x_scales, 0)
+        for a in range(2):
+            nc.sync.dma_start(out=w_raw[a][:], in_=w1.rearrange("(p j) c -> p j c", j=PACK)[:, :, a * HALF : (a + 1) * HALF])
+        nc.sync.dma_start(out=own_rows[OWN_ROW:P, :], in_=own.rearrange("(q p) o -> q (p o)", p=P))
+        load_scales(es_table, e_scales, E_SCALE_ROW)
         nc.sync.dma_start(out=ew_table[:], in_=e_words[0].rearrange("p n t -> p (n t)").bitcast(I32))
 
         inv_turned = []
         for g in range(ID_TILES):
             inv_listed = sb("inv_listed%d" % g, [P, ID_ENTRIES], F32)
             nc.vector.tensor_copy(inv_listed[:], inv_table[:].indirect(list_slice(enr_sb, g * ID_ENTRIES, ID_ENTRIES)))
+            inv_dealt = sb("inv_dealt%d" % g, [P, D, P], F32)
+            nc.scalar.copy(inv_dealt[:].rearrange("p d (c i) -> p c d i", i=4), inv_listed[:].rearrange("p (c i d) -> p c d i", d=D, i=4))
             turned = bank(6 + g, "inv_turned%d" % g, [P, D, P])
             for d in range(D):
-                nc.tensor.transpose(turned[:, d, :], inv_listed[:, d:ID_ENTRIES:D], ident[:])
+                nc.tensor.transpose(turned[:, d, :], inv_dealt[:, d, :], ident[:])
             inv_turned.append(turned)
 
+        xw = sb("xw", [P, FACES], U32)
+        nc.vector.tensor_copy(xw[:], xw_table[:].bitcast(U32).indirect(offs_sb[:]))
         xs = sb("xs", [P, FACES], U8)
         nc.vector.tensor_copy(xs[:], xs_table[:].indirect(offs_sb[:]))
-
-        es_listed0 = sb("es_listed0", [P, ID_ENTRIES], U8)
-        nc.vector.tensor_copy(es_listed0[:], es_table[:].indirect(list_slice(enr_sb, 0, ID_ENTRIES)))
 
         w_codes = sb("w_codes", [P, H], U32)
         w_scales = sb("w_scales", [P, H], U8)
         for a in range(2):
             cols = slice(a * HALF, (a + 1) * HALF)
             w_grouped = sb("w_grouped%d" % a, [P, HALF, PACK], BF16)
-            nc.scalar.copy(w_grouped[:].rearrange("p (c i) j -> p c j i", i=4), w_raw[:, :, cols].rearrange("p j (c i) -> p c j i", i=4))
+            grouped = w_grouped[:].rearrange("p (c i) j -> p c j i", i=4)
+            raw = w_raw[a][:].rearrange("p j (c i) -> p c j i", i=4)
+            if a == 0:
+                nc.scalar.copy(grouped, raw)
+            else:
+                nc.scalar.copy(grouped[:, 0:32], raw[:, 0:32])
+                nc.vector.tensor_copy(grouped[:, 32:64], raw[:, 32:64])
             nc.vector.quantize_mx(out=w_codes[:, cols].bitcast(FP8X4), scales=w_scales[:, cols], in_=w_grouped[:].rearrange("p c j -> p (c j)"))
 
-        inv_cols = sb("inv_cols", [P, ID_TILES, D], F32, after="w_raw")
+        inv_cols = sb("inv_cols", [P, ID_TILES * D], F32, after="w_grouped1")
         for g in range(ID_TILES):
-            nc.scalar.copy(inv_cols[:, g, :], inv_turned[g][:, :, INV_ROW])
-        inv_once = sb("inv_once", [P, ID_TILES, D], F32)
-        inv_eight = sb("inv_eight", [P, ID_TILES, D], F32)
-        nc.scalar.copy(inv_once[:], inv_cols[:])
-        nc.scalar.activation(inv_eight[:], inv_cols[:], ACT.Copy, scale=BEST_WEIGHT)
+            nc.scalar.copy(inv_cols[:, g * D : (g + 1) * D], inv_turned[g][:, :, INV_ROW])
+        inv_once = sb("inv_once", [P, ID_TILES * D], F32)
+        inv_eight = sb("inv_eight", [P, ID_TILES * D], F32)
+        first_eight = sb("first_eight", [P, 1], F32)
+        nc.gpsimd.tensor_scalar(first_eight[:], inv_cols[:, 0:1], BEST_WEIGHT, 0.0, ALU.mult, ALU.add)
+        nc.gpsimd.tensor_scalar(inv_eight[:], inv_cols[:], BEST_WEIGHT, 0.0, ALU.mult, ALU.add)
+        nc.gpsimd.tensor_scalar(inv_once[:], inv_cols[:], 1.0, 0.0, ALU.mult, ALU.add)
 
-        own_turned = bank(6, "own_turned", [P, P])
+        own_turned = bank(5, "own_turned", [P, P])
         nc.tensor.transpose(own_turned[:], own_rows[:], ident[:])
         sign = sb("sign", [P, FACE_TILES], F32)
         quarter_abs = sb("quarter_abs", [P, FACE_TILES], F32)
         nc.scalar.activation(sign[:], own_turned[:, OWN_ROW:P], ACT.Sign)
         nc.scalar.activation(quarter_abs[:], own_turned[:, OWN_ROW:P], ACT.Abs, scale=1.0 / D)
 
-        xw = [sb("xw%d" % a, [P, HALF], U32) for a in range(2)]
-        for a in range(2):
-            nc.vector.tensor_copy(xw[a][:], xw_table[:].bitcast(U32).indirect(list_slice(offs_sb, a * HALF, HALF)))
+
+        es_listed = sb("es_listed", [P, ID_TILES, ID_ENTRIES], U8, after="w_raw1")
+        for g in range(ID_TILES):
+            nc.vector.tensor_copy(es_listed[:, g, :], es_table[:].indirect(list_slice(enr_sb, g * ID_ENTRIES, ID_ENTRIES)))
 
         h_grouped = [sb("h_grouped%d" % a, [P, 2, P * PACK], BF16) for a in range(2)]
+        h_rows = []
         for q in range(FACE_TILES):
-            a, within = divmod(q, 2)
             acc = bank(q, "h_acc%d" % q, [P, H])
             nc.tensor.matmul_mx(
                 out=acc[:],
-                lhsT=xw[a][:, within * P : (within + 1) * P].bitcast(FP8X4),
+                lhsT=xw[:, q * P : (q + 1) * P].bitcast(FP8X4),
                 lhsT_scale=xs[:, q * P : (q + 1) * P],
                 rhs=w_codes[:].bitcast(FP8X4),
                 rhs_scale=w_scales[:],
                 start=True,
                 stop=True,
             )
-            h_rows = sb("h_rows%d" % q, [P, 2, P, 2], BF16)
-            nc.scalar.activation(h_rows[:], acc[:].rearrange("t (p u e) -> t u p e", u=2, e=2), ACT.Copy, scale=sign[:, q : q + 1])
-            h_pairs = h_rows[:].rearrange("t u p e -> t (u p e)").bitcast(F32)
-            turned = bank(FACE_TILES + q, "h_turned%d" % q, [P, 2, P])
-            for u in range(2):
-                nc.tensor.transpose(turned[:, u, :], h_pairs[:, u * P : (u + 1) * P], ident[:])
-            nc.scalar.copy(h_grouped[a][:, within, :].bitcast(F32).rearrange("p (t u) -> p t u", u=2), turned[:].rearrange("p u t -> p t u"))
+            rows = sb("h_rows%d" % q, [P, 2, P, 2], BF16)
+            nc.scalar.activation(rows[:], acc[:].rearrange("t (p u e) -> t u p e", u=2, e=2), ACT.Copy, scale=sign[:, q : q + 1])
+            h_rows.append(rows)
+        for a in range(2):
+            turned = bank(FACE_TILES + a, "h_turned%d" % a, [P, 2, 2, P])
+            for within in range(2):
+                h_pairs = h_rows[2 * a + within][:].rearrange("t u p e -> t (u p e)").bitcast(F32)
+                for u in range(2):
+                    nc.tensor.transpose(turned[:, within, u, :], h_pairs[:, u * P : (u + 1) * P], ident[:])
+            nc.scalar.copy(
+                h_grouped[a][:].rearrange("p w c -> p (w c)").bitcast(F32).rearrange("p (w t u) -> p w t u", w=2, u=2),
+                turned[:].rearrange("p w u t -> p w t u"),
+            )
 
-        def deal(name, listed, dtype, run, after=None):
-            dealt = sb(name, [P, ID_ENTRIES], dtype, after=after)
+        def deal(dealt, listed, first, count, run):
             nc.vector.tensor_copy(
-                dealt[:].rearrange("p (d c i) -> p c d i", d=D, i=run),
+                dealt[:].rearrange("p (d c i) -> p c d i", d=D, i=run)[:, first // run : (first + count) // run],
                 listed.rearrange("p (c i d) -> p c d i", d=D, i=run),
             )
-            return dealt
 
-        def quantise_h(a, after):
-            codes = sb("h_codes%d" % a, [P, HALF], U32, after=after)
+        def quantise_h(a):
+            codes = h_codes[:, a * HALF : (a + 1) * HALF]
             scales = sb("h_scales%d" % a, [P, HALF], U8)
-            nc.vector.quantize_mx(out=codes[:].bitcast(FP8X4), scales=scales[:], in_=h_grouped[a][:].rearrange("p q c -> p (q c)"))
-            return codes, scales
+            nc.vector.quantize_mx(out=codes.bitcast(FP8X4), scales=scales[:], in_=h_grouped[a][:].rearrange("p q c -> p (q c)"))
+            return codes, scales[:]
 
-        es = [deal("es0", es_listed0[:], U8, 16, after="xw_table")]
-        ew_listed = sb("ew_listed", [P, ENTRIES], U32)
-        nc.vector.tensor_copy(ew_listed[:], ew_table[:].bitcast(U32).indirect(enr_sb[:]))
-        ew = [deal("ew0", ew_listed[:, 0:ID_ENTRIES], U32, 4)]
-        h_mx = [quantise_h(0, after="ew_table")]
-        es_listed1 = sb("es_listed1", [P, ID_ENTRIES], U8, after="h_grouped0")
-        nc.vector.tensor_copy(es_listed1[:], es_table[:].indirect(list_slice(enr_sb, ID_ENTRIES, ID_ENTRIES)))
-        h_mx.append(quantise_h(1, after="es_table"))
-        ew.append(deal("ew1", ew_listed[:, ID_ENTRIES:ENTRIES], U32, 4))
-        es.append(deal("es1", es_listed1[:], U8, 16))
+        es = [sb("es%d" % g, [P, ID_ENTRIES], U8) for g in range(ID_TILES)]
+        for g in range(ID_TILES):
+            deal(es[g], es_listed[:, g, :], 0, P, 16)
+        part = ID_ENTRIES // 2
+        ew = [sb("ew%d" % g, [P, ID_ENTRIES], U32) for g in range(ID_TILES)]
+
+        def gather_e(g, b, after=None):
+            listed = sb("ew_listed%d_%d" % (g, b), [P, part], U32, after=after)
+            nc.vector.tensor_copy(listed[:], ew_table[:].bitcast(U32).indirect(list_slice(enr_sb, g * ID_ENTRIES + b * part, part)))
+            return listed
+
+        listed = [gather_e(0, b) for b in range(2)]
+        for b in range(2):
+            deal(ew[0], listed[b][:], b * part // D, part // D, 4)
+        h_codes = sb("h_codes", [P, FACES], U32, after="ew_listed0_0")
+        h_mx = [quantise_h(0)]
+        listed = [gather_e(1, 0, after="ew_listed0_1")]
+        h_mx.append(quantise_h(1))
+        listed.append(gather_e(1, 1, after="h_grouped0"))
+        for b in range(2):
+            deal(ew[1], listed[b][:], b * part // D, part // D, 4)
 
         def product(acc, g, d, a):
             cols = slice(d * P, (d + 1) * P)
@@ -176,19 +203,19 @@ def tile_picked_ycosm_cal_p_kernel(tc, x_words, x_scales, w1, e_words, e_scales,
                 out=acc,
                 lhsT=ew[g][:, cols].bitcast(FP8X4),
                 lhsT_scale=es[g][E_SCALE_ROW:P, cols],
-                rhs=h_mx[a][0][:].bitcast(FP8X4),
-                rhs_scale=h_mx[a][1][:],
+                rhs=h_mx[a][0].bitcast(FP8X4),
+                rhs_scale=h_mx[a][1],
                 start=True,
                 stop=True,
             )
 
         y = {}
         for a in range(2):
-            for odd in range(2):
-                acc = bank(2 * a + odd, "y0_%d_%d" % (a, odd), [P, 2, HALF])
-                for pair in range(2):
-                    product(acc[:, pair, :], 0, 2 * pair + odd, a)
-                    y[0, 2 * pair + odd, a] = acc[:, pair, :]
+            for pair in range(2):
+                acc = bank(2 * a + pair, "y0_%d_%d" % (a, pair), [P, 2, HALF])
+                for e in range(2):
+                    product(acc[:, e, :], 0, 2 * pair + e, a)
+                    y[0, 2 * pair + e, a] = acc[:, e, :]
         y1_both_halves = {}
         for d in range(D):
             acc = bank(4 + d, "y1_%d" % d, [P, 2, HALF])
@@ -197,44 +224,85 @@ def tile_picked_ycosm_cal_p_kernel(tc, x_words, x_scales, w1, e_words, e_scales,
                 y[1, d, a] = acc[:, a, :]
             y1_both_halves[d] = acc[:].rearrange("p a t -> p (a t)")
 
-        names = ("z0", "z0_eight", "z2", "sum01", "best01", "best012", "sum23", "best")
+        halves = [slice(a * HALF, (a + 1) * HALF) for a in range(2)]
+        whole = slice(0, FACES)
+        names = ("z0", "z0_eight", "z1", "z2", "z3", "sum23", "best01", "best012")
         work = [dict((n, sb("%s_%d" % (n, g), [P, FACES], F32)) for n in names) for g in range(ID_TILES)]
 
-        def read_even_templates(g, cols, y0, y2):
-            nc.scalar.activation(work[g]["z0_eight"][:, cols], y0, ACT.Copy, scale=inv_eight[:, g, 0:1])
-            nc.scalar.activation(work[g]["z0"][:, cols], y0, ACT.Copy, scale=inv_cols[:, g, 0:1])
-            nc.scalar.activation(work[g]["z2"][:, cols], y2, ACT.Copy, scale=inv_cols[:, g, 2:3])
+        def read_bank(g, name, cols, src, factor):
+            nc.scalar.activation(work[g][name][:, cols], src, ACT.Copy, scale=factor)
 
-        for a in range(2):
-            read_even_templates(0, slice(a * HALF, (a + 1) * HALF), y[0, 0, a], y[0, 2, a])
-        read_even_templates(1, slice(0, FACES), y1_both_halves[0], y1_both_halves[2])
+        def col(factors, g, d):
+            return factors[:, g * D + d : g * D + d + 1]
+
+        read_bank(0, "z0_eight", halves[0], y[0, 0, 0], first_eight[:])
+        read_bank(0, "z1", halves[0], y[0, 1, 0], col(inv_cols, 0, 1))
+        read_bank(0, "z2", halves[0], y[0, 2, 0], col(inv_cols, 0, 2))
+        read_bank(0, "z1", halves[1], y[0, 1, 1], col(inv_cols, 0, 1))
+        read_bank(0, "z0_eight", halves[1], y[0, 0, 1], first_eight[:])
+        read_bank(0, "z2", halves[1], y[0, 2, 1], col(inv_cols, 0, 2))
+        read_bank(1, "z0_eight", whole, y1_both_halves[0], col(inv_eight, 1, 0))
+        for d in (1, 2, 3):
+            read_bank(1, "z%d" % d, whole, y1_both_halves[d], col(inv_cols, 1, d))
+        for g, cols in ((0, halves[0]), (0, halves[1]), (1, whole)):
+            nc.gpsimd.tensor_scalar(work[g]["z0"][:, cols], work[g]["z0_eight"][:, cols], 1.0 / BEST_WEIGHT, 0.0, ALU.mult, ALU.add)
+
+        best = {}
+
+        def step_best01(g, a):
+            w, cols = work[g], halves[a]
+            nc.vector.scalar_tensor_tensor(w["best01"][:, cols], w["z1"][:, cols], BEST_WEIGHT, w["z0_eight"][:, cols], ALU.mult, ALU.max)
+
+        def step_best012(g, a):
+            w, cols = work[g], halves[a]
+            nc.vector.scalar_tensor_tensor(w["best012"][:, cols], w["z2"][:, cols], BEST_WEIGHT, w["best01"][:, cols], ALU.mult, ALU.max)
+
+        def step_sum23(g, a):
+            w, cols = work[g], halves[a]
+            nc.vector.scalar_tensor_tensor(w["sum23"][:, cols], y[g, 3, a], col(inv_once, g, 3), w["z2"][:, cols], ALU.mult, ALU.add)
+
+        def step_best(g, a, after=None):
+            best[g, a] = sb("best%d_%d" % (g, a), [P, HALF], F32, after=after)
+            if g == 0:
+                nc.vector.scalar_tensor_tensor(best[g, a][:], y[g, 3, a], col(inv_eight, g, 3), work[g]["best012"][:, halves[a]], ALU.mult, ALU.max)
+            else:
+                nc.vector.scalar_tensor_tensor(best[g, a][:], work[g]["z3"][:, halves[a]], BEST_WEIGHT, work[g]["best012"][:, halves[a]], ALU.mult, ALU.max)
+
+        step_best01(0, 0)
+        step_sum23(0, 0)
+        step_best012(0, 0)
+        step_best01(0, 1)
+        step_best(0, 0, after="first_eight")
+        step_best012(0, 1)
+        step_sum23(0, 1)
+        step_best(0, 1)
+        for step in (step_best01, step_best012, step_best):
+            for a in range(2):
+                step(1, a)
+
+        def turn(total, term, first, last):
+            for within in range(2):
+                nc.tensor.matmul(
+                    total[:, within, :],
+                    lhsT=term[:, within * P : (within + 1) * P],
+                    rhs=ident[:],
+                    is_transpose=True,
+                    start=(first and within == 0),
+                    stop=(last and within == 1),
+                )
 
         for g in range(ID_TILES):
             w = work[g]
+            result = sb("result%d" % g, [P, FACE_TILES, P], F32, after="w_grouped1" if g == 0 else None)
+            sums = ("z1", "z0", "sum23") if g == 0 else ("z1", "z0", "z2", "z3")
+            total = [bank(2 * a + g, "total%d_%d" % (g, a), [P, 2, P]) for a in range(2)]
+            for n, name in enumerate(sums):
+                for a in range(2):
+                    turn(total[a], w[name][:, halves[a]], n == 0, False)
             for a in range(2):
-                cols = slice(a * HALF, (a + 1) * HALF)
-                nc.vector.scalar_tensor_tensor(w["best01"][:, cols], y[g, 1, a], inv_eight[:, g, 1:2], w["z0_eight"][:, cols], ALU.mult, ALU.max)
-                nc.vector.scalar_tensor_tensor(w["sum01"][:, cols], y[g, 1, a], inv_once[:, g, 1:2], w["z0"][:, cols], ALU.mult, ALU.add)
-                nc.vector.scalar_tensor_tensor(w["best012"][:, cols], w["z2"][:, cols], BEST_WEIGHT, w["best01"][:, cols], ALU.mult, ALU.max)
-                nc.vector.scalar_tensor_tensor(w["sum23"][:, cols], y[g, 3, a], inv_once[:, g, 3:4], w["z2"][:, cols], ALU.mult, ALU.add)
-                nc.vector.scalar_tensor_tensor(w["best"][:, cols], y[g, 3, a], inv_eight[:, g, 3:4], w["best012"][:, cols], ALU.mult, ALU.max)
-            result = sb("result%d" % g, [P, FACE_TILES, P], F32, after="w_raw" if g == 0 else None)
-            terms = [w["sum01"], w["sum23"], w["best"]]
-            for a in range(2):
-                total = bank(2 * a + g, "total%d_%d" % (g, a), [P, 2, P])
-                for n, term in enumerate(terms):
-                    for within in range(2):
-                        q = 2 * a + within
-                        nc.tensor.matmul(
-                            total[:, within, :],
-                            lhsT=term[:, q * P : (q + 1) * P],
-                            rhs=ident[:],
-                            is_transpose=True,
-                            start=(n == 0 and within == 0),
-                            stop=(n == len(terms) - 1 and within == 1),
-                        )
+                turn(total[a], best[g, a][:], False, True)
                 for within in range(2):
                     q = 2 * a + within
-                    nc.scalar.activation(result[:, q, :], total[:, within, :], ACT.Sigmoid, bias=minus_one[:], scale=quarter_abs[:, q : q + 1])
+                    nc.scalar.activation(result[:, q, :], total[a][:, within, :], ACT.Sigmoid, bias=minus_one[:], scale=quarter_abs[:, q : q + 1])
                 tiles = slice(2 * a, 2 * a + 2)
                 nc.sync.dma_start(out=out[:, g * P : (g + 1) * P].rearrange("(q p) v -> p q v", p=P)[:, tiles, :], in_=result[:, tiles, :])

@@ -57,17 +57,15 @@ def tile_picked_ycosm_cal_p_kernel(tc, x_words, x_scales, w1, e_words, e_scales,
         minus_one = sb("minus_one", [P, 1], F32)
 
         nc.gpsimd.memset(xs_table[:].bitcast(I32), 0)
-        nc.vector.memset(minus_one[:], -1.0)
+        nc.gpsimd.memset(minus_one[:], -1.0)
         nc.vector.memset(inv_table[0:INV_ROW, :].bitcast(I32), 0)
         nc.gpsimd.memset(own_rows[0:OWN_ROW, :], 0.0)
         nc.gpsimd.memset(es_table[:].bitcast(I32), 0)
         make_identity(nc, ident[:])
-        warm = sb("warm", [P, 1], F32)
-        nc.scalar.activation(warm[:], minus_one[:], ACT.Sigmoid)
 
-        def load_scales(table, scales, first_row):
+        def load_scales(queue, table, scales, first_row):
             for r in range(4):
-                nc.sync.dma_start(out=table[first_row + r : P : 32, :].bitcast(I32), in_=scales[0, r:SCALE_ROWS:4, :].bitcast(I32))
+                queue.dma_start(out=table[first_row + r : P : 32, :].bitcast(I32), in_=scales[0, r:SCALE_ROWS:4, :].bitcast(I32))
 
         def list_slice(list_sb, first, count):
             return list_sb[:, first // STRIPE : (first + count) // STRIPE]
@@ -77,12 +75,15 @@ def tile_picked_ycosm_cal_p_kernel(tc, x_words, x_scales, w1, e_words, e_scales,
         nc.sync.dma_start(out=inv_table[INV_ROW : INV_ROW + 1, :], in_=inv[0:1, :])
         nc.sync.dma_start(offs_sb[:], offs)
         nc.sync.dma_start(out=xw_table[:], in_=x_words[0].rearrange("p n t -> p (n t)").bitcast(I32))
-        load_scales(xs_table, x_scales, 0)
+        load_scales(nc.scalar, xs_table, x_scales, 0)
         for a in range(2):
             nc.sync.dma_start(out=w_raw[a][:], in_=w1.rearrange("(p j) c -> p j c", j=PACK)[:, :, a * HALF : (a + 1) * HALF])
         nc.sync.dma_start(out=own_rows[OWN_ROW:P, :], in_=own.rearrange("(q p) o -> q (p o)", p=P))
-        load_scales(es_table, e_scales, E_SCALE_ROW)
+        load_scales(nc.sync, es_table, e_scales, E_SCALE_ROW)
         nc.sync.dma_start(out=ew_table[:], in_=e_words[0].rearrange("p n t -> p (n t)").bitcast(I32))
+
+        warm = sb("warm", [P, 1], F32)
+        nc.scalar.activation(warm[:], minus_one[:], ACT.Sigmoid)
 
         inv_turned = []
         for g in range(ID_TILES):
@@ -175,9 +176,8 @@ def tile_picked_ycosm_cal_p_kernel(tc, x_words, x_scales, w1, e_words, e_scales,
             nc.vector.quantize_mx(out=codes.bitcast(FP8X4), scales=scales[:], in_=h_grouped[a][:].rearrange("p q c -> p (q c)"))
             return codes, scales[:]
 
-        es = [sb("es%d" % g, [P, ID_ENTRIES], U8) for g in range(ID_TILES)]
-        for g in range(ID_TILES):
-            deal(es[g], es_listed[:, g, :], 0, P, 16)
+        es = [sb("es0", [P, ID_ENTRIES], U8)]
+        deal(es[0], es_listed[:, 0, :], 0, P, 16)
         part = ID_ENTRIES // 2
         ew = [sb("ew%d" % g, [P, ID_ENTRIES], U32) for g in range(ID_TILES)]
 
@@ -194,6 +194,8 @@ def tile_picked_ycosm_cal_p_kernel(tc, x_words, x_scales, w1, e_words, e_scales,
         listed = [gather_e(1, 0, after="ew_listed0_1")]
         h_mx.append(quantise_h(1))
         listed.append(gather_e(1, 1, after="h_grouped0"))
+        es.append(sb("es1", [P, ID_ENTRIES], U8, after="h_grouped1"))
+        deal(es[1], es_listed[:, 1, :], 0, P, 16)
         for b in range(2):
             deal(ew[1], listed[b][:], b * part // D, part // D, 4)
 

@@ -58,9 +58,10 @@ def tile_picked_ycosm_cal_p_kernel(tc, x_words, x_scales, w1, e_words, e_scales,
 
         nc.gpsimd.memset(xs_table[:].bitcast(I32), 0)
         nc.gpsimd.memset(minus_one[:], -1.0)
+        nc.gpsimd.dma_start(out=own_rows[OWN_ROW:P, :], in_=own.rearrange("(q p) o -> q (p o)", p=P))
         nc.vector.memset(inv_table[0:INV_ROW, :].bitcast(I32), 0)
-        nc.gpsimd.memset(own_rows[0:OWN_ROW, :], 0.0)
         nc.gpsimd.memset(es_table[:].bitcast(I32), 0)
+        nc.gpsimd.memset(own_rows[0:OWN_ROW, :], 0.0)
         make_identity(nc, ident[:])
 
         def load_scales(queue, table, scales, first_row):
@@ -73,31 +74,29 @@ def tile_picked_ycosm_cal_p_kernel(tc, x_words, x_scales, w1, e_words, e_scales,
         w_raw = [sb("w_raw%d" % a, [P, PACK, HALF], F32) for a in range(2)]
         nc.sync.dma_start(enr_sb[:], enr)
         nc.sync.dma_start(out=inv_table[INV_ROW : INV_ROW + 1, :], in_=inv[0:1, :])
-        nc.sync.dma_start(offs_sb[:], offs)
-        nc.sync.dma_start(out=xw_table[:], in_=x_words[0].rearrange("p n t -> p (n t)").bitcast(I32))
-        load_scales(nc.scalar, xs_table, x_scales, 0)
         for a in range(2):
             nc.sync.dma_start(out=w_raw[a][:], in_=w1.rearrange("(p j) c -> p j c", j=PACK)[:, :, a * HALF : (a + 1) * HALF])
-        nc.sync.dma_start(out=own_rows[OWN_ROW:P, :], in_=own.rearrange("(q p) o -> q (p o)", p=P))
+        load_scales(nc.scalar, xs_table, x_scales, 0)
+        nc.sync.dma_start(offs_sb[:], offs)
+        nc.sync.dma_start(out=xw_table[:], in_=x_words[0].rearrange("p n t -> p (n t)").bitcast(I32))
         load_scales(nc.sync, es_table, e_scales, E_SCALE_ROW)
         nc.sync.dma_start(out=ew_table[:], in_=e_words[0].rearrange("p n t -> p (n t)").bitcast(I32))
 
         warm = sb("warm", [P, 1], F32)
         nc.scalar.activation(warm[:], minus_one[:], ACT.Sigmoid)
 
-        inv_turned = []
+        inv_listed = [sb("inv_listed%d" % g, [P, ID_ENTRIES], F32) for g in range(ID_TILES)]
         for g in range(ID_TILES):
-            inv_listed = sb("inv_listed%d" % g, [P, ID_ENTRIES], F32)
-            nc.vector.tensor_copy(inv_listed[:], inv_table[:].indirect(list_slice(enr_sb, g * ID_ENTRIES, ID_ENTRIES)))
-            inv_dealt = sb("inv_dealt%d" % g, [P, D, P], F32)
-            nc.scalar.copy(inv_dealt[:].rearrange("p d (c i) -> p c d i", i=4), inv_listed[:].rearrange("p (c i d) -> p c d i", d=D, i=4))
-            turned = bank(6 + g, "inv_turned%d" % g, [P, D, P])
-            for d in range(D):
-                nc.tensor.transpose(turned[:, d, :], inv_dealt[:, d, :], ident[:])
-            inv_turned.append(turned)
+            nc.vector.tensor_copy(inv_listed[g][:], inv_table[:].indirect(list_slice(enr_sb, g * ID_ENTRIES, ID_ENTRIES)))
+        inv_cols = sb("inv_cols", [P, ID_TILES, 2 * D], F32)
+        for g in range(ID_TILES):
+            nc.sync.dma_start(out=inv_cols[:, g, 0:D], in_=inv_listed[g][INV_ROW:P, :].rearrange("o (v d) -> o v d", d=D))
+        first_eight = sb("first_eight", [P, ID_TILES], F32)
+        nc.gpsimd.tensor_scalar(first_eight[:], inv_cols[:, :, 0], BEST_WEIGHT, 0.0, ALU.mult, ALU.add)
 
-        xw = sb("xw", [P, FACES], U32)
-        nc.vector.tensor_copy(xw[:], xw_table[:].bitcast(U32).indirect(offs_sb[:]))
+        second_eight = sb("second_eight", [P, 1], F32)
+        nc.gpsimd.tensor_scalar(second_eight[:], inv_cols[:, 1, 1:2], BEST_WEIGHT, 0.0, ALU.mult, ALU.add)
+
         xs = sb("xs", [P, FACES], U8)
         nc.vector.tensor_copy(xs[:], xs_table[:].indirect(offs_sb[:]))
 
@@ -106,205 +105,192 @@ def tile_picked_ycosm_cal_p_kernel(tc, x_words, x_scales, w1, e_words, e_scales,
         for a in range(2):
             cols = slice(a * HALF, (a + 1) * HALF)
             w_grouped = sb("w_grouped%d" % a, [P, HALF, PACK], BF16)
-            grouped = w_grouped[:].rearrange("p (c i) j -> p c j i", i=4)
-            raw = w_raw[a][:].rearrange("p j (c i) -> p c j i", i=4)
-            if a == 0:
-                nc.scalar.copy(grouped, raw)
-            else:
-                nc.scalar.copy(grouped[:, 0:32], raw[:, 0:32])
-                nc.vector.tensor_copy(grouped[:, 32:64], raw[:, 32:64])
+            nc.scalar.copy(w_grouped[:].rearrange("p (c i) j -> p c j i", i=4), w_raw[a][:].rearrange("p j (c i) -> p c j i", i=4))
             nc.vector.quantize_mx(out=w_codes[:, cols].bitcast(FP8X4), scales=w_scales[:, cols], in_=w_grouped[:].rearrange("p c j -> p (c j)"))
 
-        inv_cols = sb("inv_cols", [P, ID_TILES * D], F32, after="w_grouped1")
-        for g in range(ID_TILES):
-            nc.scalar.copy(inv_cols[:, g * D : (g + 1) * D], inv_turned[g][:, :, INV_ROW])
-        inv_once = sb("inv_once", [P, ID_TILES * D], F32)
-        inv_eight = sb("inv_eight", [P, ID_TILES * D], F32)
-        first_eight = sb("first_eight", [P, 1], F32)
-        nc.gpsimd.tensor_scalar(first_eight[:], inv_cols[:, 0:1], BEST_WEIGHT, 0.0, ALU.mult, ALU.add)
-        nc.gpsimd.tensor_scalar(inv_eight[:], inv_cols[:], BEST_WEIGHT, 0.0, ALU.mult, ALU.add)
-        nc.gpsimd.tensor_scalar(inv_once[:], inv_cols[:], 1.0, 0.0, ALU.mult, ALU.add)
+        xw = [sb("xw%d" % a, [P, HALF], U32) for a in range(2)]
+        for a in range(2):
+            nc.vector.tensor_copy(xw[a][:], xw_table[:].bitcast(U32).indirect(list_slice(offs_sb, a * HALF, HALF)))
 
-        own_turned = bank(5, "own_turned", [P, P])
+        own_turned = bank(6, "own_turned", [P, P])
         nc.tensor.transpose(own_turned[:], own_rows[:], ident[:])
         sign = sb("sign", [P, FACE_TILES], F32)
         quarter_abs = sb("quarter_abs", [P, FACE_TILES], F32)
         nc.scalar.activation(sign[:], own_turned[:, OWN_ROW:P], ACT.Sign)
         nc.scalar.activation(quarter_abs[:], own_turned[:, OWN_ROW:P], ACT.Abs, scale=1.0 / D)
 
-
-        es_listed = sb("es_listed", [P, ID_TILES, ID_ENTRIES], U8, after="w_raw1")
-        for g in range(ID_TILES):
-            nc.vector.tensor_copy(es_listed[:, g, :], es_table[:].indirect(list_slice(enr_sb, g * ID_ENTRIES, ID_ENTRIES)))
-
         h_grouped = [sb("h_grouped%d" % a, [P, 2, P * PACK], BF16) for a in range(2)]
         h_rows = []
+        accs = []
         for q in range(FACE_TILES):
             acc = bank(q, "h_acc%d" % q, [P, H])
             nc.tensor.matmul_mx(
                 out=acc[:],
-                lhsT=xw[:, q * P : (q + 1) * P].bitcast(FP8X4),
+                lhsT=xw[q // 2][:, (q % 2) * P : (q % 2 + 1) * P].bitcast(FP8X4),
                 lhsT_scale=xs[:, q * P : (q + 1) * P],
                 rhs=w_codes[:].bitcast(FP8X4),
                 rhs_scale=w_scales[:],
                 start=True,
                 stop=True,
             )
+            accs.append(acc)
+
+        def read_h(q):
             rows = sb("h_rows%d" % q, [P, 2, P, 2], BF16)
-            nc.scalar.activation(rows[:], acc[:].rearrange("t (p u e) -> t u p e", u=2, e=2), ACT.Copy, scale=sign[:, q : q + 1])
+            nc.scalar.activation(rows[:], accs[q][:].rearrange("t (p u e) -> t u p e", u=2, e=2), ACT.Copy, scale=sign[:, q : q + 1])
             h_rows.append(rows)
-        for a in range(2):
+
+        h_turned = []
+
+        def turn_h(a):
             turned = bank(FACE_TILES + a, "h_turned%d" % a, [P, 2, 2, P])
             for within in range(2):
                 h_pairs = h_rows[2 * a + within][:].rearrange("t u p e -> t (u p e)").bitcast(F32)
                 for u in range(2):
                     nc.tensor.transpose(turned[:, within, u, :], h_pairs[:, u * P : (u + 1) * P], ident[:])
+            h_turned.append(turned)
+
+        def group_h(a):
             nc.scalar.copy(
                 h_grouped[a][:].rearrange("p w c -> p (w c)").bitcast(F32).rearrange("p (w t u) -> p w t u", w=2, u=2),
-                turned[:].rearrange("p w u t -> p w t u"),
+                h_turned[a][:].rearrange("p w u t -> p w t u"),
             )
 
-        def deal(dealt, listed, first, count, run):
-            nc.vector.tensor_copy(
-                dealt[:].rearrange("p (d c i) -> p c d i", d=D, i=run)[:, first // run : (first + count) // run],
-                listed.rearrange("p (c i d) -> p c d i", d=D, i=run),
-            )
+        read_h(0)
+        read_h(1)
+        turn_h(0)
+        read_h(2)
+        group_h(0)
+        read_h(3)
+        turn_h(1)
+        group_h(1)
 
-        def quantise_h(a):
-            codes = h_codes[:, a * HALF : (a + 1) * HALF]
-            scales = sb("h_scales%d" % a, [P, HALF], U8)
-            nc.vector.quantize_mx(out=codes.bitcast(FP8X4), scales=scales[:], in_=h_grouped[a][:].rearrange("p q c -> p (q c)"))
-            return codes, scales[:]
-
-        es = [sb("es0", [P, ID_ENTRIES], U8)]
-        deal(es[0], es_listed[:, 0, :], 0, P, 16)
-        part = ID_ENTRIES // 2
-        ew = [sb("ew%d" % g, [P, ID_ENTRIES], U32) for g in range(ID_TILES)]
-
-        def gather_e(g, b, after=None):
-            listed = sb("ew_listed%d_%d" % (g, b), [P, part], U32, after=after)
-            nc.vector.tensor_copy(listed[:], ew_table[:].bitcast(U32).indirect(list_slice(enr_sb, g * ID_ENTRIES + b * part, part)))
+        def gather_scales(name, first, count, after):
+            listed = sb(name, [P, count], U8, after=after)
+            nc.vector.tensor_copy(listed[:], es_table[:].indirect(list_slice(enr_sb, first, count)))
             return listed
 
-        listed = [gather_e(0, b) for b in range(2)]
-        for b in range(2):
-            deal(ew[0], listed[b][:], b * part // D, part // D, 4)
-        h_codes = sb("h_codes", [P, FACES], U32, after="ew_listed0_0")
-        h_mx = [quantise_h(0)]
-        listed = [gather_e(1, 0, after="ew_listed0_1")]
-        h_mx.append(quantise_h(1))
-        listed.append(gather_e(1, 1, after="h_grouped0"))
-        es.append(sb("es1", [P, ID_ENTRIES], U8, after="h_grouped1"))
-        deal(es[1], es_listed[:, 1, :], 0, P, 16)
-        for b in range(2):
-            deal(ew[1], listed[b][:], b * part // D, part // D, 4)
+        es = [sb("es%d" % g, [P, ID_ENTRIES], U8) for g in range(ID_TILES)]
 
-        def product(acc, g, d, a):
-            cols = slice(d * P, (d + 1) * P)
+        def deal_scales(g, listed, first, count):
+            runs = slice(first // (16 * D), (first + count) // (16 * D))
+            nc.vector.tensor_copy(es[g][:].rearrange("p (d c i) -> p c d i", d=D, i=16)[:, runs], listed[:].rearrange("p (c i d) -> p c d i", d=D, i=16))
+
+        def gather_words(g, after):
+            dealt = sb("ew%d" % g, [P, D, P], U32, after=after)
+            nc.vector.tensor_copy(dealt[:].rearrange("p d v -> p v d"), ew_table[:].bitcast(U32).indirect(list_slice(enr_sb, g * ID_ENTRIES, ID_ENTRIES)))
+            return dealt
+
+        halves = [slice(a * HALF, (a + 1) * HALF) for a in range(2)]
+        whole = slice(0, FACES)
+        h_codes = sb("h_codes", [P, FACES], U32, after="inv_listed1")
+        h_scales = sb("h_scales", [P, FACES], U8)
+
+        def quantise_h(a):
+            nc.vector.quantize_mx(out=h_codes[:, halves[a]].bitcast(FP8X4), scales=h_scales[:, halves[a]], in_=h_grouped[a][:].rearrange("p q c -> p (q c)"))
+
+        listed = gather_scales("es_listed0", 0, ID_ENTRIES, "w_grouped1")
+        ew = [gather_words(0, None)]
+        deal_scales(0, listed, 0, ID_ENTRIES)
+        part = ID_ENTRIES // 2
+        listed = []
+        for a in range(2):
+            listed.append(gather_scales("es_listed1_%d" % a, ID_ENTRIES + a * part, part, ("inv_listed0", "h_grouped0")[a]))
+            quantise_h(a)
+        for a in range(2):
+            deal_scales(1, listed[a], a * part, part)
+        ew.append(gather_words(1, "h_grouped1"))
+
+        def product(acc, g, d, cols):
             nc.tensor.matmul_mx(
                 out=acc,
-                lhsT=ew[g][:, cols].bitcast(FP8X4),
-                lhsT_scale=es[g][E_SCALE_ROW:P, cols],
-                rhs=h_mx[a][0].bitcast(FP8X4),
-                rhs_scale=h_mx[a][1],
+                lhsT=ew[g][:, d, :].bitcast(FP8X4),
+                lhsT_scale=es[g][E_SCALE_ROW:P, d * P : (d + 1) * P],
+                rhs=h_codes[:, cols].bitcast(FP8X4),
+                rhs_scale=h_scales[:, cols],
                 start=True,
                 stop=True,
             )
 
-        y = {}
-        for a in range(2):
-            for pair in range(2):
-                acc = bank(2 * a + pair, "y0_%d_%d" % (a, pair), [P, 2, HALF])
-                for e in range(2):
-                    product(acc[:, e, :], 0, 2 * pair + e, a)
-                    y[0, 2 * pair + e, a] = acc[:, e, :]
-        y1_both_halves = {}
-        for d in range(D):
-            acc = bank(4 + d, "y1_%d" % d, [P, 2, HALF])
-            for a in range(2):
-                product(acc[:, a, :], 1, d, a)
-                y[1, d, a] = acc[:, a, :]
-            y1_both_halves[d] = acc[:].rearrange("p a t -> p (a t)")
-
-        halves = [slice(a * HALF, (a + 1) * HALF) for a in range(2)]
-        whole = slice(0, FACES)
-        names = ("z0", "z0_eight", "z1", "z2", "z3", "sum23", "best01", "best012")
+        names = ("z0", "z0_eight", "z1", "z2", "z3", "best01", "best23")
         work = [dict((n, sb("%s_%d" % (n, g), [P, FACES], F32)) for n in names) for g in range(ID_TILES)]
 
-        def read_bank(g, name, cols, src, factor):
-            nc.scalar.activation(work[g][name][:, cols], src, ACT.Copy, scale=factor)
-
-        def col(factors, g, d):
-            return factors[:, g * D + d : g * D + d + 1]
-
-        read_bank(0, "z0_eight", halves[0], y[0, 0, 0], first_eight[:])
-        read_bank(0, "z1", halves[0], y[0, 1, 0], col(inv_cols, 0, 1))
-        read_bank(0, "z2", halves[0], y[0, 2, 0], col(inv_cols, 0, 2))
-        read_bank(0, "z1", halves[1], y[0, 1, 1], col(inv_cols, 0, 1))
-        read_bank(0, "z0_eight", halves[1], y[0, 0, 1], first_eight[:])
-        read_bank(0, "z2", halves[1], y[0, 2, 1], col(inv_cols, 0, 2))
-        read_bank(1, "z0_eight", whole, y1_both_halves[0], col(inv_eight, 1, 0))
-        for d in (1, 2, 3):
-            read_bank(1, "z%d" % d, whole, y1_both_halves[d], col(inv_cols, 1, d))
-        for g, cols in ((0, halves[0]), (0, halves[1]), (1, whole)):
-            nc.gpsimd.tensor_scalar(work[g]["z0"][:, cols], work[g]["z0_eight"][:, cols], 1.0 / BEST_WEIGHT, 0.0, ALU.mult, ALU.add)
-
-        best = {}
-
-        def step_best01(g, a):
-            w, cols = work[g], halves[a]
-            nc.vector.scalar_tensor_tensor(w["best01"][:, cols], w["z1"][:, cols], BEST_WEIGHT, w["z0_eight"][:, cols], ALU.mult, ALU.max)
-
-        def step_best012(g, a):
-            w, cols = work[g], halves[a]
-            nc.vector.scalar_tensor_tensor(w["best012"][:, cols], w["z2"][:, cols], BEST_WEIGHT, w["best01"][:, cols], ALU.mult, ALU.max)
-
-        def step_sum23(g, a):
-            w, cols = work[g], halves[a]
-            nc.vector.scalar_tensor_tensor(w["sum23"][:, cols], y[g, 3, a], col(inv_once, g, 3), w["z2"][:, cols], ALU.mult, ALU.add)
-
-        def step_best(g, a, after=None):
-            best[g, a] = sb("best%d_%d" % (g, a), [P, HALF], F32, after=after)
-            if g == 0:
-                nc.vector.scalar_tensor_tensor(best[g, a][:], y[g, 3, a], col(inv_eight, g, 3), work[g]["best012"][:, halves[a]], ALU.mult, ALU.max)
+        def read_bank(g, d, cols, src):
+            w = work[g]
+            if d == 0:
+                nc.scalar.activation(w["z0_eight"][:, cols], src, ACT.Copy, scale=first_eight[:, g : g + 1])
+                nc.gpsimd.tensor_scalar(w["z0"][:, cols], w["z0_eight"][:, cols], 1.0 / BEST_WEIGHT, 0.0, ALU.mult, ALU.add)
             else:
-                nc.vector.scalar_tensor_tensor(best[g, a][:], work[g]["z3"][:, halves[a]], BEST_WEIGHT, work[g]["best012"][:, halves[a]], ALU.mult, ALU.max)
+                nc.scalar.activation(w["z%d" % d][:, cols], src, ACT.Copy, scale=inv_cols[:, g, d : d + 1])
 
-        step_best01(0, 0)
-        step_sum23(0, 0)
-        step_best012(0, 0)
-        step_best01(0, 1)
-        step_best(0, 0, after="first_eight")
-        step_best012(0, 1)
-        step_sum23(0, 1)
-        step_best(0, 1)
-        for step in (step_best01, step_best012, step_best):
-            for a in range(2):
-                step(1, a)
+        total = {}
 
-        def turn(total, term, first, last):
+        def turn(g, a, term, first, last):
             for within in range(2):
                 nc.tensor.matmul(
-                    total[:, within, :],
-                    lhsT=term[:, within * P : (within + 1) * P],
+                    total[g, a][:, within, :],
+                    lhsT=term[:, a * HALF + within * P : a * HALF + (within + 1) * P],
                     rhs=ident[:],
                     is_transpose=True,
                     start=(first and within == 0),
                     stop=(last and within == 1),
                 )
 
-        for g in range(ID_TILES):
-            w = work[g]
-            result = sb("result%d" % g, [P, FACE_TILES, P], F32, after="w_grouped1" if g == 0 else None)
-            sums = ("z1", "z0", "sum23") if g == 0 else ("z1", "z0", "z2", "z3")
-            total = [bank(2 * a + g, "total%d_%d" % (g, a), [P, 2, P]) for a in range(2)]
-            for n, name in enumerate(sums):
-                for a in range(2):
-                    turn(total[a], w[name][:, halves[a]], n == 0, False)
+        def turn_sums(g, which):
+            for n, name in enumerate(("z1", "z0", "z2", "z3") if g == 0 else ("z2", "z0", "z3", "z1")):
+                for a in which:
+                    turn(g, a, work[g][name], n == 0, False)
+
+        for pair in range(2):
+            acc = bank(pair, "y0_0_%d" % pair, [P, 2, HALF])
+            for e in range(2):
+                product(acc[:, e, :], 0, 2 * pair + e, halves[0])
+            for e in range(2):
+                read_bank(0, 2 * pair + e, halves[0], acc[:, e, :])
+        for d, b in enumerate((2, 3, 6, 7)):
+            acc = bank(b, "y0_1_%d" % d, [P, HALF])
+            product(acc[:], 0, d, halves[1])
+            read_bank(0, d, halves[1], acc[:])
+        for a in range(2):
+            total[0, a] = bank(4 + a, "total0_%d" % a, [P, 2, P])
+        turn_sums(0, [0])
+        y1 = {}
+        for d, b in ((0, 1), (2, 2), (1, 3), (3, 6)):
+            y1[d] = bank(b, "y1_%d" % d, [P, FACES])
+            product(y1[d][:], 1, d, whole)
+        for a, b in enumerate((7, 0)):
+            total[1, a] = bank(b, "total1_%d" % a, [P, 2, P])
+        for d in (0, 2, 3):
+            read_bank(1, d, whole, y1[d][:])
+        turn_sums(0, [1])
+
+        best = [sb("best%d" % g, [P, FACES], F32) for g in range(ID_TILES)]
+
+        def larger(dst, scaled, other, cols):
+            nc.vector.scalar_tensor_tensor(dst[:, cols], scaled[:, cols], BEST_WEIGHT, other[:, cols], ALU.mult, ALU.max)
+
+        w = work[0]
+        larger(w["best01"], w["z1"], w["z0_eight"], whole)
+        for a in range(2):
+            nc.vector.tensor_tensor(w["best23"][:, halves[a]], w["z2"][:, halves[a]], w["z3"][:, halves[a]], ALU.max)
+        for a in range(2):
+            larger(best[0], w["best23"], w["best01"], halves[a])
+        w = work[1]
+        nc.vector.scalar_tensor_tensor(w["best01"][:], y1[1][:], second_eight[:], w["z0_eight"][:], ALU.mult, ALU.max)
+        read_bank(1, 1, whole, y1[1][:])
+        for dst, scaled, other in ((w["best23"], w["z2"], w["best01"]), (best[1], w["z3"], w["best23"])):
             for a in range(2):
-                turn(total[a], best[g, a][:], False, True)
+                larger(dst, scaled, other, halves[a])
+
+        def finish(g, result):
+            for a in range(2):
+                turn(g, a, best[g], False, True)
                 for within in range(2):
                     q = 2 * a + within
-                    nc.scalar.activation(result[:, q, :], total[a][:, within, :], ACT.Sigmoid, bias=minus_one[:], scale=quarter_abs[:, q : q + 1])
+                    nc.scalar.activation(result[:, q, :], total[g, a][:, within, :], ACT.Sigmoid, bias=minus_one[:], scale=quarter_abs[:, q : q + 1])
                 tiles = slice(2 * a, 2 * a + 2)
                 nc.sync.dma_start(out=out[:, g * P : (g + 1) * P].rearrange("(q p) v -> p q v", p=P)[:, tiles, :], in_=result[:, tiles, :])
+
+        finish(0, sb("result0", [P, FACE_TILES, P], F32, after="inv_cols"))
+        turn_sums(1, [0, 1])
+        finish(1, sb("result1", [P, FACE_TILES, P], F32))

@@ -58,7 +58,6 @@ def tile_picked_ycosm_cal_p_kernel(tc, x_words, x_scales, w1, e_words, e_scales,
 
         nc.gpsimd.memset(xs_table[:].bitcast(I32), 0)
         nc.gpsimd.memset(minus_one[:], -1.0)
-        nc.gpsimd.dma_start(out=own_rows[OWN_ROW:P, :], in_=own.rearrange("(q p) o -> q (p o)", p=P))
         nc.vector.memset(inv_table[0:INV_ROW, :].bitcast(I32), 0)
         nc.gpsimd.memset(es_table[:].bitcast(I32), 0)
         nc.gpsimd.memset(own_rows[0:OWN_ROW, :], 0.0)
@@ -71,13 +70,13 @@ def tile_picked_ycosm_cal_p_kernel(tc, x_words, x_scales, w1, e_words, e_scales,
         def list_slice(list_sb, first, count):
             return list_sb[:, first // STRIPE : (first + count) // STRIPE]
 
-        w_raw = [sb("w_raw%d" % a, [P, PACK, HALF], F32) for a in range(2)]
+        w_raw = sb("w_raw", [P, PACK, H], F32)
         nc.sync.dma_start(enr_sb[:], enr)
         nc.sync.dma_start(out=inv_table[INV_ROW : INV_ROW + 1, :], in_=inv[0:1, :])
-        for a in range(2):
-            nc.sync.dma_start(out=w_raw[a][:], in_=w1.rearrange("(p j) c -> p j c", j=PACK)[:, :, a * HALF : (a + 1) * HALF])
+        nc.sync.dma_start(out=w_raw[:], in_=w1.rearrange("(p j) c -> p j c", j=PACK))
         load_scales(nc.scalar, xs_table, x_scales, 0)
         nc.sync.dma_start(offs_sb[:], offs)
+        nc.sync.dma_start(out=own_rows[OWN_ROW:P, :], in_=own.rearrange("(q p) o -> q (p o)", p=P))
         nc.sync.dma_start(out=xw_table[:], in_=x_words[0].rearrange("p n t -> p (n t)").bitcast(I32))
         load_scales(nc.sync, es_table, e_scales, E_SCALE_ROW)
         nc.sync.dma_start(out=ew_table[:], in_=e_words[0].rearrange("p n t -> p (n t)").bitcast(I32))
@@ -85,12 +84,11 @@ def tile_picked_ycosm_cal_p_kernel(tc, x_words, x_scales, w1, e_words, e_scales,
         warm = sb("warm", [P, 1], F32)
         nc.scalar.activation(warm[:], minus_one[:], ACT.Sigmoid)
 
-        inv_listed = [sb("inv_listed%d" % g, [P, ID_ENTRIES], F32) for g in range(ID_TILES)]
-        for g in range(ID_TILES):
-            nc.vector.tensor_copy(inv_listed[g][:], inv_table[:].indirect(list_slice(enr_sb, g * ID_ENTRIES, ID_ENTRIES)))
+        inv_listed = sb("inv_listed", [P, ENTRIES], F32)
+        nc.vector.tensor_copy(inv_listed[:], inv_table[:].indirect(enr_sb[:]))
         inv_cols = sb("inv_cols", [P, ID_TILES, 2 * D], F32)
         for g in range(ID_TILES):
-            nc.sync.dma_start(out=inv_cols[:, g, 0:D], in_=inv_listed[g][INV_ROW:P, :].rearrange("o (v d) -> o v d", d=D))
+            nc.sync.dma_start(out=inv_cols[:, g, 0:D], in_=inv_listed[INV_ROW:P, g * ID_ENTRIES : (g + 1) * ID_ENTRIES].rearrange("o (v d) -> o v d", d=D))
         first_eight = sb("first_eight", [P, ID_TILES], F32)
         nc.gpsimd.tensor_scalar(first_eight[:], inv_cols[:, :, 0], BEST_WEIGHT, 0.0, ALU.mult, ALU.add)
 
@@ -100,12 +98,28 @@ def tile_picked_ycosm_cal_p_kernel(tc, x_words, x_scales, w1, e_words, e_scales,
         xs = sb("xs", [P, FACES], U8)
         nc.vector.tensor_copy(xs[:], xs_table[:].indirect(offs_sb[:]))
 
+        def gather_scales(name, first, count, after):
+            listed = sb(name, [P, count], U8, after=after)
+            nc.vector.tensor_copy(listed[:], es_table[:].indirect(list_slice(enr_sb, first, count)))
+            return listed
+
+        def deal_scales(g, listed, after):
+            dealt = sb("es%d" % g, [P, ID_ENTRIES], U8, after=after)
+            nc.vector.tensor_copy(dealt[:].rearrange("p (d c i) -> p c d i", d=D, i=16), listed[:].rearrange("p (c i d) -> p c d i", d=D, i=16))
+            return dealt
+
         w_codes = sb("w_codes", [P, H], U32)
         w_scales = sb("w_scales", [P, H], U8)
         for a in range(2):
             cols = slice(a * HALF, (a + 1) * HALF)
             w_grouped = sb("w_grouped%d" % a, [P, HALF, PACK], BF16)
-            nc.scalar.copy(w_grouped[:].rearrange("p (c i) j -> p c j i", i=4), w_raw[a][:].rearrange("p j (c i) -> p c j i", i=4))
+            grouped = w_grouped[:].rearrange("p (c i) j -> p c j i", i=4)
+            raw = w_raw[:, :, cols].rearrange("p j (c i) -> p c j i", i=4)
+            if a == 0:
+                nc.scalar.copy(grouped, raw)
+            else:
+                nc.scalar.copy(grouped[:, 0:32], raw[:, 0:32])
+                nc.vector.tensor_copy(grouped[:, 32:64], raw[:, 32:64])
             nc.vector.quantize_mx(out=w_codes[:, cols].bitcast(FP8X4), scales=w_scales[:, cols], in_=w_grouped[:].rearrange("p c j -> p (c j)"))
 
         xw = [sb("xw%d" % a, [P, HALF], U32) for a in range(2)]
@@ -165,17 +179,6 @@ def tile_picked_ycosm_cal_p_kernel(tc, x_words, x_scales, w1, e_words, e_scales,
         turn_h(1)
         group_h(1)
 
-        def gather_scales(name, first, count, after):
-            listed = sb(name, [P, count], U8, after=after)
-            nc.vector.tensor_copy(listed[:], es_table[:].indirect(list_slice(enr_sb, first, count)))
-            return listed
-
-        es = [sb("es%d" % g, [P, ID_ENTRIES], U8) for g in range(ID_TILES)]
-
-        def deal_scales(g, listed, first, count):
-            runs = slice(first // (16 * D), (first + count) // (16 * D))
-            nc.vector.tensor_copy(es[g][:].rearrange("p (d c i) -> p c d i", d=D, i=16)[:, runs], listed[:].rearrange("p (c i d) -> p c d i", d=D, i=16))
-
         def gather_words(g, after):
             dealt = sb("ew%d" % g, [P, D, P], U32, after=after)
             nc.vector.tensor_copy(dealt[:].rearrange("p d v -> p v d"), ew_table[:].bitcast(U32).indirect(list_slice(enr_sb, g * ID_ENTRIES, ID_ENTRIES)))
@@ -183,22 +186,18 @@ def tile_picked_ycosm_cal_p_kernel(tc, x_words, x_scales, w1, e_words, e_scales,
 
         halves = [slice(a * HALF, (a + 1) * HALF) for a in range(2)]
         whole = slice(0, FACES)
-        h_codes = sb("h_codes", [P, FACES], U32, after="inv_listed1")
+        h_codes = sb("h_codes", [P, FACES], U32, after="inv_listed")
         h_scales = sb("h_scales", [P, FACES], U8)
 
         def quantise_h(a):
             nc.vector.quantize_mx(out=h_codes[:, halves[a]].bitcast(FP8X4), scales=h_scales[:, halves[a]], in_=h_grouped[a][:].rearrange("p q c -> p (q c)"))
 
-        listed = gather_scales("es_listed0", 0, ID_ENTRIES, "w_grouped1")
+        listed = [gather_scales("es_listed%d" % g, g * ID_ENTRIES, ID_ENTRIES, ("w_grouped1", "xw_table")[g]) for g in range(ID_TILES)]
+        es = [deal_scales(0, listed[0], None)]
         ew = [gather_words(0, None)]
-        deal_scales(0, listed, 0, ID_ENTRIES)
-        part = ID_ENTRIES // 2
-        listed = []
-        for a in range(2):
-            listed.append(gather_scales("es_listed1_%d" % a, ID_ENTRIES + a * part, part, ("inv_listed0", "h_grouped0")[a]))
-            quantise_h(a)
-        for a in range(2):
-            deal_scales(1, listed[a], a * part, part)
+        quantise_h(0)
+        es.append(deal_scales(1, listed[1], "h_grouped0"))
+        quantise_h(1)
         ew.append(gather_words(1, "h_grouped1"))
 
         def product(acc, g, d, cols):
@@ -212,34 +211,34 @@ def tile_picked_ycosm_cal_p_kernel(tc, x_words, x_scales, w1, e_words, e_scales,
                 stop=True,
             )
 
-        names = ("z0", "z0_eight", "z1", "z2", "z3", "best01", "best23")
+        names = ("z0_eight", "z1", "z2", "z3", "best01", "best23")
         work = [dict((n, sb("%s_%d" % (n, g), [P, FACES], F32)) for n in names) for g in range(ID_TILES)]
 
         def read_bank(g, d, cols, src):
             w = work[g]
             if d == 0:
                 nc.scalar.activation(w["z0_eight"][:, cols], src, ACT.Copy, scale=first_eight[:, g : g + 1])
-                nc.gpsimd.tensor_scalar(w["z0"][:, cols], w["z0_eight"][:, cols], 1.0 / BEST_WEIGHT, 0.0, ALU.mult, ALU.add)
             else:
                 nc.scalar.activation(w["z%d" % d][:, cols], src, ACT.Copy, scale=inv_cols[:, g, d : d + 1])
 
         total = {}
 
-        def turn(g, a, term, first, last):
-            for within in range(2):
+        def turn(acc, term, first, last):
+            count = acc.shape[1]
+            for within in range(count):
                 nc.tensor.matmul(
-                    total[g, a][:, within, :],
-                    lhsT=term[:, a * HALF + within * P : a * HALF + (within + 1) * P],
+                    acc[:, within, :],
+                    lhsT=term[:, within * P : (within + 1) * P],
                     rhs=ident[:],
                     is_transpose=True,
                     start=(first and within == 0),
-                    stop=(last and within == 1),
+                    stop=(last and within == count - 1),
                 )
 
-        def turn_sums(g, which):
-            for n, name in enumerate(("z1", "z0", "z2", "z3") if g == 0 else ("z2", "z0", "z3", "z1")):
-                for a in which:
-                    turn(g, a, work[g][name], n == 0, False)
+        def eighth(name, g, cols, after):
+            z0 = sb(name, [P, cols.stop - cols.start], F32, after=after)
+            nc.gpsimd.tensor_scalar(z0[:], work[g]["z0_eight"][:, cols], 1.0 / BEST_WEIGHT, 0.0, ALU.mult, ALU.add)
+            return z0
 
         for pair in range(2):
             acc = bank(pair, "y0_0_%d" % pair, [P, 2, HALF])
@@ -253,44 +252,54 @@ def tile_picked_ycosm_cal_p_kernel(tc, x_words, x_scales, w1, e_words, e_scales,
             read_bank(0, d, halves[1], acc[:])
         for a in range(2):
             total[0, a] = bank(4 + a, "total0_%d" % a, [P, 2, P])
-        turn_sums(0, [0])
+        z0 = eighth("z0_0_0", 0, halves[0], "xw_table")
+        for n, term in enumerate((work[0]["z1"], z0, work[0]["z2"], work[0]["z3"])):
+            turn(total[0, 0], term[:, halves[0]], n == 0, False)
         y1 = {}
         for d, b in ((0, 1), (2, 2), (1, 3), (3, 6)):
             y1[d] = bank(b, "y1_%d" % d, [P, FACES])
             product(y1[d][:], 1, d, whole)
-        for a, b in enumerate((7, 0)):
-            total[1, a] = bank(b, "total1_%d" % a, [P, 2, P])
         for d in (0, 2, 3):
             read_bank(1, d, whole, y1[d][:])
-        turn_sums(0, [1])
-
-        best = [sb("best%d" % g, [P, FACES], F32) for g in range(ID_TILES)]
+        z0 = eighth("z0_0_1", 0, halves[1], None)
+        for n, term in enumerate((work[0]["z1"][:, halves[1]], z0[:], work[0]["z2"][:, halves[1]], work[0]["z3"][:, halves[1]])):
+            turn(total[0, 1], term, n == 0, False)
 
         def larger(dst, scaled, other, cols):
             nc.vector.scalar_tensor_tensor(dst[:, cols], scaled[:, cols], BEST_WEIGHT, other[:, cols], ALU.mult, ALU.max)
 
-        w = work[0]
-        larger(w["best01"], w["z1"], w["z0_eight"], whole)
+        w0, w = work
+        best = [sb("best%d" % g, [P, FACES], F32) for g in range(ID_TILES)]
+        larger(w0["best01"], w0["z1"], w0["z0_eight"], whole)
         for a in range(2):
-            nc.vector.tensor_tensor(w["best23"][:, halves[a]], w["z2"][:, halves[a]], w["z3"][:, halves[a]], ALU.max)
+            nc.vector.tensor_tensor(w0["best23"][:, halves[a]], w0["z2"][:, halves[a]], w0["z3"][:, halves[a]], ALU.max)
         for a in range(2):
-            larger(best[0], w["best23"], w["best01"], halves[a])
-        w = work[1]
-        nc.vector.scalar_tensor_tensor(w["best01"][:], y1[1][:], second_eight[:], w["z0_eight"][:], ALU.mult, ALU.max)
+            larger(best[0], w0["best23"], w0["best01"], halves[a])
+            turn(total[0, a], best[0][:, halves[a]], False, True)
+        z0 = eighth("z0_1", 1, whole, None)
+        for a in range(2):
+            nc.vector.scalar_tensor_tensor(w["best01"][:, halves[a]], y1[1][:, halves[a]], second_eight[:], w["z0_eight"][:, halves[a]], ALU.mult, ALU.max)
         read_bank(1, 1, whole, y1[1][:])
-        for dst, scaled, other in ((w["best23"], w["z2"], w["best01"]), (best[1], w["z3"], w["best23"])):
-            for a in range(2):
-                larger(dst, scaled, other, halves[a])
+        for a in range(2):
+            larger(w["best23"], w["z2"], w["best01"], halves[a])
+        pieces = (slice(0, 2 * P), slice(2 * P, 3 * P), slice(3 * P, 4 * P))
+        for cols in pieces:
+            larger(best[1], w["z3"], w["best23"], cols)
 
-        def finish(g, result):
-            for a in range(2):
-                turn(g, a, best[g], False, True)
-                for within in range(2):
-                    q = 2 * a + within
-                    nc.scalar.activation(result[:, q, :], total[g, a][:, within, :], ACT.Sigmoid, bias=minus_one[:], scale=quarter_abs[:, q : q + 1])
-                tiles = slice(2 * a, 2 * a + 2)
-                nc.sync.dma_start(out=out[:, g * P : (g + 1) * P].rearrange("(q p) v -> p q v", p=P)[:, tiles, :], in_=result[:, tiles, :])
+        def finish(g, cols, acc, result, queue):
+            tiles = slice(cols.start // P, cols.stop // P)
+            for q in range(tiles.start, tiles.stop):
+                nc.scalar.activation(result[:, q, :], acc[:, q - tiles.start, :], ACT.Sigmoid, bias=minus_one[:], scale=quarter_abs[:, q : q + 1])
+            queue.dma_start(out=out[:, g * P : (g + 1) * P].rearrange("(q p) v -> p q v", p=P)[:, tiles, :], in_=result[:, tiles, :])
 
-        finish(0, sb("result0", [P, FACE_TILES, P], F32, after="inv_cols"))
-        turn_sums(1, [0, 1])
-        finish(1, sb("result1", [P, FACE_TILES, P], F32))
+        result = sb("result0", [P, FACE_TILES, P], F32, after="inv_cols")
+        for a in range(2):
+            finish(0, halves[a], total[0, a], result, nc.sync)
+        total1 = [bank(b, "total1_%d" % n, [P, (cols.stop - cols.start) // P, P]) for n, (b, cols) in enumerate(zip((7, 0, 1), pieces))]
+        for n, term in enumerate((w["z2"], z0, w["z3"], w["z1"])):
+            for acc, cols in zip(total1, pieces):
+                turn(acc, term[:, cols], n == 0, False)
+        result = sb("result1", [P, FACE_TILES, P], F32)
+        for acc, cols in zip(total1, pieces):
+            turn(acc, best[1][:, cols], False, True)
+            finish(1, cols, acc, result, nc.scalar if cols.stop == FACES else nc.sync)

@@ -25,6 +25,7 @@ ID_TILES = ENTRIES // (D * P)
 ID_ENTRIES = D * P
 HALF = FACES // 2
 E_SCALE_ROW = 4
+SCALE_ROW0 = P - SCALE_ROWS
 INV_ROW = P - 1
 OWN_ROW = P - FACE_TILES
 BEST_WEIGHT = 2.0 * D
@@ -51,80 +52,84 @@ def tile_picked_ycosm_cal_p_kernel(tc, x_words, x_scales, w1, e_words, e_scales,
         es_table = sb("es_table", [P, TABLE], U8)
         inv_table = sb("inv_table", [P, TABLE], F32)
         xw_table = sb("xw_table", [P, TABLE], I32)
-        ew_table = sb("ew_table", [P, TABLE], I32)
         own_rows = sb("own_rows", [P, P], F32)
         ident = sb("ident", [P, P], F32)
         minus_one = sb("minus_one", [P, 1], F32)
 
-        nc.gpsimd.memset(xs_table[:].bitcast(I32), 0)
+        xs = sb("xs", [P, FACES], U8)
+        es = sb("es", [P, ENTRIES], U8)
+        nc.gpsimd.memset(xs_table[0:SCALE_ROW0, :].bitcast(I32), 0)
         nc.gpsimd.memset(minus_one[:], -1.0)
+        nc.gpsimd.memset(es_table[0:SCALE_ROW0, :].bitcast(I32), 0)
         nc.vector.memset(inv_table[0:INV_ROW, :].bitcast(I32), 0)
-        nc.gpsimd.memset(es_table[:].bitcast(I32), 0)
+        nc.gpsimd.memset(xs[:].bitcast(I32), 0)
+        nc.gpsimd.memset(es[:].bitcast(I32), 0)
         nc.gpsimd.memset(own_rows[0:OWN_ROW, :], 0.0)
         make_identity(nc, ident[:])
-
-        def load_scales(queue, table, scales, first_row):
-            for r in range(4):
-                queue.dma_start(out=table[first_row + r : P : 32, :].bitcast(I32), in_=scales[0, r:SCALE_ROWS:4, :].bitcast(I32))
 
         def list_slice(list_sb, first, count):
             return list_sb[:, first // STRIPE : (first + count) // STRIPE]
 
+        def place_scales(placed, listed, first_row):
+            for r in range(4):
+                nc.sync.dma_start(out=placed[first_row + r : P : 32, :].bitcast(I32), in_=listed[SCALE_ROW0 + r : P : 4, :].bitcast(I32))
+
         w_raw = sb("w_raw", [P, PACK, H], F32)
+        nc.sync.dma_start(offs_sb[:], offs)
+        nc.scalar.dma_start(out=xs_table[SCALE_ROW0:P, :].bitcast(I32), in_=x_scales[0].bitcast(I32))
         nc.sync.dma_start(enr_sb[:], enr)
+        nc.scalar.dma_start(out=es_table[SCALE_ROW0:P, :].bitcast(I32), in_=e_scales[0].bitcast(I32))
         nc.sync.dma_start(out=inv_table[INV_ROW : INV_ROW + 1, :], in_=inv[0:1, :])
         nc.sync.dma_start(out=w_raw[:], in_=w1.rearrange("(p j) c -> p j c", j=PACK))
-        load_scales(nc.scalar, xs_table, x_scales, 0)
-        nc.sync.dma_start(offs_sb[:], offs)
-        nc.sync.dma_start(out=own_rows[OWN_ROW:P, :], in_=own.rearrange("(q p) o -> q (p o)", p=P))
         nc.sync.dma_start(out=xw_table[:], in_=x_words[0].rearrange("p n t -> p (n t)").bitcast(I32))
-        load_scales(nc.sync, es_table, e_scales, E_SCALE_ROW)
+        nc.sync.dma_start(out=own_rows[OWN_ROW:P, :], in_=own.rearrange("(q p) o -> q (p o)", p=P))
+
+        xs_listed = sb("xs_listed", [P, FACES], U8)
+        nc.vector.tensor_copy(xs_listed[:], xs_table[:].indirect(offs_sb[:]))
+        place_scales(xs, xs_listed, 0)
+        ew_table = sb("ew_table", [P, TABLE], I32, after="xs_table")
         nc.sync.dma_start(out=ew_table[:], in_=e_words[0].rearrange("p n t -> p (n t)").bitcast(I32))
+        es_listed = sb("es_listed", [P, ENTRIES], U8)
+        nc.vector.tensor_copy(es_listed[:].rearrange("p (g d v) -> p g v d", g=ID_TILES, d=D), es_table[:].indirect(enr_sb[:]))
+        place_scales(es, es_listed, E_SCALE_ROW)
 
         warm = sb("warm", [P, 1], F32)
         nc.scalar.activation(warm[:], minus_one[:], ACT.Sigmoid)
 
         inv_listed = sb("inv_listed", [P, ENTRIES], F32)
-        nc.vector.tensor_copy(inv_listed[:], inv_table[:].indirect(enr_sb[:]))
+        nc.scalar.activation(inv_listed[:], inv_table[:].indirect(enr_sb[:]), ACT.Copy)
         inv_cols = sb("inv_cols", [P, ID_TILES, 2 * D], F32)
         for g in range(ID_TILES):
             nc.sync.dma_start(out=inv_cols[:, g, 0:D], in_=inv_listed[INV_ROW:P, g * ID_ENTRIES : (g + 1) * ID_ENTRIES].rearrange("o (v d) -> o v d", d=D))
-        first_eight = sb("first_eight", [P, ID_TILES], F32)
-        nc.gpsimd.tensor_scalar(first_eight[:], inv_cols[:, :, 0], BEST_WEIGHT, 0.0, ALU.mult, ALU.add)
+        inv_eight = sb("inv_eight", [P, ID_TILES, D], F32)
+        nc.gpsimd.tensor_scalar(inv_eight[:], inv_cols[:, :, 0:D], BEST_WEIGHT, 0.0, ALU.mult, ALU.add)
 
-        second_eight = sb("second_eight", [P, 1], F32)
-        nc.gpsimd.tensor_scalar(second_eight[:], inv_cols[:, 1, 1:2], BEST_WEIGHT, 0.0, ALU.mult, ALU.add)
-
-        xs = sb("xs", [P, FACES], U8)
-        nc.vector.tensor_copy(xs[:], xs_table[:].indirect(offs_sb[:]))
-
-        def gather_scales(name, first, count, after):
-            listed = sb(name, [P, count], U8, after=after)
-            nc.vector.tensor_copy(listed[:], es_table[:].indirect(list_slice(enr_sb, first, count)))
-            return listed
-
-        def deal_scales(g, listed, after):
-            dealt = sb("es%d" % g, [P, ID_ENTRIES], U8, after=after)
-            nc.vector.tensor_copy(dealt[:].rearrange("p (d c i) -> p c d i", d=D, i=16), listed[:].rearrange("p (c i d) -> p c d i", d=D, i=16))
-            return dealt
 
         w_codes = sb("w_codes", [P, H], U32)
         w_scales = sb("w_scales", [P, H], U8)
-        for a in range(2):
-            cols = slice(a * HALF, (a + 1) * HALF)
-            w_grouped = sb("w_grouped%d" % a, [P, HALF, PACK], BF16)
-            grouped = w_grouped[:].rearrange("p (c i) j -> p c j i", i=4)
-            raw = w_raw[:, :, cols].rearrange("p j (c i) -> p c j i", i=4)
-            if a == 0:
-                nc.scalar.copy(grouped, raw)
-            else:
-                nc.scalar.copy(grouped[:, 0:32], raw[:, 0:32])
-                nc.vector.tensor_copy(grouped[:, 32:64], raw[:, 32:64])
-            nc.vector.quantize_mx(out=w_codes[:, cols].bitcast(FP8X4), scales=w_scales[:, cols], in_=w_grouped[:].rearrange("p c j -> p (c j)"))
+        w_grouped = [sb("w_grouped%d" % a, [P, HALF, PACK], BF16) for a in range(2)]
 
-        xw = [sb("xw%d" % a, [P, HALF], U32) for a in range(2)]
-        for a in range(2):
-            nc.vector.tensor_copy(xw[a][:], xw_table[:].bitcast(U32).indirect(list_slice(offs_sb, a * HALF, HALF)))
+        def cast_w(engine_copy, a, first, last):
+            grouped = w_grouped[a][:].rearrange("p (c i) j -> p c j i", i=4)
+            raw = w_raw[:, :, a * HALF : (a + 1) * HALF].rearrange("p j (c i) -> p c j i", i=4)
+            engine_copy(grouped[:, first:last], raw[:, first:last])
+
+        def quantise_w(a, first, last):
+            cols = slice(a * HALF + first, a * HALF + last)
+            nc.vector.quantize_mx(out=w_codes[:, cols].bitcast(FP8X4), scales=w_scales[:, cols], in_=w_grouped[a][:, first:last, :].rearrange("p c j -> p (c j)"))
+
+        cast_w(nc.scalar.copy, 0, 0, 64)
+        cast_w(nc.scalar.copy, 1, 0, 48)
+        cast_w(nc.vector.tensor_copy, 1, 48, 64)
+        quantise_w(0, 0, HALF)
+        quantise_w(1, 0, HALF)
+
+        xw = []
+        for n, (first, count) in enumerate(((0, P), (P, P), (2 * P, 2 * P))):
+            piece = sb("xw%d" % n, [P, count], U32)
+            nc.vector.tensor_copy(piece[:], xw_table[:].bitcast(U32).indirect(list_slice(offs_sb, first, count)))
+            for within in range(count // P):
+                xw.append(piece[:, within * P : (within + 1) * P])
 
         own_turned = bank(6, "own_turned", [P, P])
         nc.tensor.transpose(own_turned[:], own_rows[:], ident[:])
@@ -133,14 +138,13 @@ def tile_picked_ycosm_cal_p_kernel(tc, x_words, x_scales, w1, e_words, e_scales,
         nc.scalar.activation(sign[:], own_turned[:, OWN_ROW:P], ACT.Sign)
         nc.scalar.activation(quarter_abs[:], own_turned[:, OWN_ROW:P], ACT.Abs, scale=1.0 / D)
 
-        h_grouped = [sb("h_grouped%d" % a, [P, 2, P * PACK], BF16) for a in range(2)]
         h_rows = []
         accs = []
         for q in range(FACE_TILES):
             acc = bank(q, "h_acc%d" % q, [P, H])
             nc.tensor.matmul_mx(
                 out=acc[:],
-                lhsT=xw[q // 2][:, (q % 2) * P : (q % 2 + 1) * P].bitcast(FP8X4),
+                lhsT=xw[q].bitcast(FP8X4),
                 lhsT_scale=xs[:, q * P : (q + 1) * P],
                 rhs=w_codes[:].bitcast(FP8X4),
                 rhs_scale=w_scales[:],
@@ -151,60 +155,58 @@ def tile_picked_ycosm_cal_p_kernel(tc, x_words, x_scales, w1, e_words, e_scales,
 
         def read_h(q):
             rows = sb("h_rows%d" % q, [P, 2, P, 2], BF16)
-            nc.scalar.activation(rows[:], accs[q][:].rearrange("t (p u e) -> t u p e", u=2, e=2), ACT.Copy, scale=sign[:, q : q + 1])
+            src = accs[q][:].rearrange("t (p u e) -> t u p e", u=2, e=2)
+            nc.scalar.activation(rows[:], src, ACT.Copy, scale=sign[:, q : q + 1])
             h_rows.append(rows)
 
         h_turned = []
 
-        def turn_h(a):
-            turned = bank(FACE_TILES + a, "h_turned%d" % a, [P, 2, 2, P])
-            for within in range(2):
-                h_pairs = h_rows[2 * a + within][:].rearrange("t u p e -> t (u p e)").bitcast(F32)
-                for u in range(2):
-                    nc.tensor.transpose(turned[:, within, u, :], h_pairs[:, u * P : (u + 1) * P], ident[:])
+        def turn_h(q):
+            turned = bank(FACE_TILES + q, "h_turned%d" % q, [P, 2, P])
+            h_pairs = h_rows[q][:].rearrange("t u p e -> t (u p e)").bitcast(F32)
+            for u in range(2):
+                nc.tensor.transpose(turned[:, u, :], h_pairs[:, u * P : (u + 1) * P], ident[:])
             h_turned.append(turned)
 
-        def group_h(a):
-            nc.scalar.copy(
-                h_grouped[a][:].rearrange("p w c -> p (w c)").bitcast(F32).rearrange("p (w t u) -> p w t u", w=2, u=2),
-                h_turned[a][:].rearrange("p w u t -> p w t u"),
-            )
+        def group_h(q, engine_copy, grouped):
+            engine_copy(grouped.bitcast(F32).rearrange("p (t u) -> p t u", u=2), h_turned[q][:].rearrange("p u t -> p t u"))
 
-        read_h(0)
-        read_h(1)
-        turn_h(0)
-        read_h(2)
-        group_h(0)
-        read_h(3)
-        turn_h(1)
-        group_h(1)
+        for q in range(FACE_TILES):
+            read_h(q)
+            turn_h(q)
 
         def gather_words(g, after):
             dealt = sb("ew%d" % g, [P, D, P], U32, after=after)
             nc.vector.tensor_copy(dealt[:].rearrange("p d v -> p v d"), ew_table[:].bitcast(U32).indirect(list_slice(enr_sb, g * ID_ENTRIES, ID_ENTRIES)))
             return dealt
 
-        halves = [slice(a * HALF, (a + 1) * HALF) for a in range(2)]
-        whole = slice(0, FACES)
-        h_codes = sb("h_codes", [P, FACES], U32, after="inv_listed")
+        h_codes = sb("h_codes", [P, FACES], U32)
         h_scales = sb("h_scales", [P, FACES], U8)
 
-        def quantise_h(a):
-            nc.vector.quantize_mx(out=h_codes[:, halves[a]].bitcast(FP8X4), scales=h_scales[:, halves[a]], in_=h_grouped[a][:].rearrange("p q c -> p (q c)"))
+        def quantise_h(first, count, grouped):
+            cols = slice(first * P, (first + count) * P)
+            nc.vector.quantize_mx(out=h_codes[:, cols].bitcast(FP8X4), scales=h_scales[:, cols], in_=grouped)
 
-        listed = [gather_scales("es_listed%d" % g, g * ID_ENTRIES, ID_ENTRIES, ("w_grouped1", "xw_table")[g]) for g in range(ID_TILES)]
-        es = [deal_scales(0, listed[0], None)]
         ew = [gather_words(0, None)]
-        quantise_h(0)
-        es.append(deal_scales(1, listed[1], "h_grouped0"))
-        quantise_h(1)
-        ew.append(gather_words(1, "h_grouped1"))
+        first_half = sb("h_grouped0", [P, 2, P * PACK], BF16, after="es_listed")
+        for q in range(2):
+            group_h(q, nc.vector.tensor_copy, first_half[:, q, :])
+        for q in range(2):
+            quantise_h(q, 1, first_half[:, q, :])
+        ew.append(gather_words(1, "es_listed"))
+        second_half = sb("h_grouped1", [P, 2, P * PACK], BF16, after="inv_listed")
+        for within in range(2):
+            group_h(2 + within, nc.scalar.copy, second_half[:, within, :])
+        quantise_h(2, 2, second_half[:].rearrange("p w c -> p (w c)"))
+
+        halves = [slice(a * HALF, (a + 1) * HALF) for a in range(2)]
+        whole = slice(0, FACES)
 
         def product(acc, g, d, cols):
             nc.tensor.matmul_mx(
                 out=acc,
                 lhsT=ew[g][:, d, :].bitcast(FP8X4),
-                lhsT_scale=es[g][E_SCALE_ROW:P, d * P : (d + 1) * P],
+                lhsT_scale=es[E_SCALE_ROW:P, (g * D + d) * P : (g * D + d + 1) * P],
                 rhs=h_codes[:, cols].bitcast(FP8X4),
                 rhs_scale=h_scales[:, cols],
                 start=True,
@@ -217,7 +219,7 @@ def tile_picked_ycosm_cal_p_kernel(tc, x_words, x_scales, w1, e_words, e_scales,
         def read_bank(g, d, cols, src):
             w = work[g]
             if d == 0:
-                nc.scalar.activation(w["z0_eight"][:, cols], src, ACT.Copy, scale=first_eight[:, g : g + 1])
+                nc.scalar.activation(w["z0_eight"][:, cols], src, ACT.Copy, scale=inv_eight[:, g, 0:1])
             else:
                 nc.scalar.activation(w["z%d" % d][:, cols], src, ACT.Copy, scale=inv_cols[:, g, d : d + 1])
 
@@ -252,7 +254,7 @@ def tile_picked_ycosm_cal_p_kernel(tc, x_words, x_scales, w1, e_words, e_scales,
             read_bank(0, d, halves[1], acc[:])
         for a in range(2):
             total[0, a] = bank(4 + a, "total0_%d" % a, [P, 2, P])
-        z0 = eighth("z0_0_0", 0, halves[0], "xw_table")
+        z0 = eighth("z0_0_0", 0, halves[0], None)
         for n, term in enumerate((work[0]["z1"], z0, work[0]["z2"], work[0]["z3"])):
             turn(total[0, 0], term[:, halves[0]], n == 0, False)
         y1 = {}
@@ -278,7 +280,7 @@ def tile_picked_ycosm_cal_p_kernel(tc, x_words, x_scales, w1, e_words, e_scales,
             turn(total[0, a], best[0][:, halves[a]], False, True)
         z0 = eighth("z0_1", 1, whole, None)
         for a in range(2):
-            nc.vector.scalar_tensor_tensor(w["best01"][:, halves[a]], y1[1][:, halves[a]], second_eight[:], w["z0_eight"][:, halves[a]], ALU.mult, ALU.max)
+            nc.vector.scalar_tensor_tensor(w["best01"][:, halves[a]], y1[1][:, halves[a]], inv_eight[:, 1, 1:2], w["z0_eight"][:, halves[a]], ALU.mult, ALU.max)
         read_bank(1, 1, whole, y1[1][:])
         for a in range(2):
             larger(w["best23"], w["z2"], w["best01"], halves[a])

@@ -58,13 +58,13 @@ def tile_picked_ycosm_cal_p_kernel(tc, x_words, x_scales, w1, e_words, e_scales,
 
         xs = sb("xs", [P, FACES], U8)
         es = sb("es", [P, ENTRIES], U8)
-        nc.gpsimd.memset(xs_table[0:SCALE_ROW0, :].bitcast(I32), 0)
         nc.gpsimd.memset(minus_one[:], -1.0)
-        nc.gpsimd.memset(es_table[0:SCALE_ROW0, :].bitcast(I32), 0)
+        nc.vector.memset(xs_table[0:SCALE_ROW0, :].bitcast(I32), 0)
         nc.vector.memset(inv_table[0:INV_ROW, :].bitcast(I32), 0)
-        nc.gpsimd.memset(xs[:].bitcast(I32), 0)
-        nc.gpsimd.memset(es[:].bitcast(I32), 0)
-        nc.gpsimd.memset(own_rows[0:OWN_ROW, :], 0.0)
+        nc.vector.memset(es_table[0:SCALE_ROW0, :].bitcast(I32), 0)
+        nc.vector.memset(xs[:].bitcast(I32), 0)
+        nc.vector.memset(es[:].bitcast(I32), 0)
+        nc.vector.memset(own_rows[0:OWN_ROW, :], 0.0)
         make_identity(nc, ident[:])
 
         def list_slice(list_sb, first, count):
@@ -90,8 +90,7 @@ def tile_picked_ycosm_cal_p_kernel(tc, x_words, x_scales, w1, e_words, e_scales,
         ew_table = sb("ew_table", [P, TABLE], I32, after="xs_table")
         nc.sync.dma_start(out=ew_table[:], in_=e_words[0].rearrange("p n t -> p (n t)").bitcast(I32))
         es_listed = sb("es_listed", [P, ENTRIES], U8)
-        nc.vector.tensor_copy(es_listed[:].rearrange("p (g d v) -> p g v d", g=ID_TILES, d=D), es_table[:].indirect(enr_sb[:]))
-        place_scales(es, es_listed, E_SCALE_ROW)
+        nc.vector.tensor_copy(es_listed[:], es_table[:].indirect(enr_sb[:]))
 
         warm = sb("warm", [P, 1], F32)
         nc.scalar.activation(warm[:], minus_one[:], ACT.Sigmoid)
@@ -130,6 +129,13 @@ def tile_picked_ycosm_cal_p_kernel(tc, x_words, x_scales, w1, e_words, e_scales,
             nc.vector.tensor_copy(piece[:], xw_table[:].bitcast(U32).indirect(list_slice(offs_sb, first, count)))
             for within in range(count // P):
                 xw.append(piece[:, within * P : (within + 1) * P])
+
+        es_dealt = sb("es_dealt", [P, ENTRIES], U8, after="xw_table")
+        nc.vector.tensor_copy(
+            es_dealt[:].rearrange("p (g d c i) -> p g c d i", g=ID_TILES, d=D, i=16),
+            es_listed[:].rearrange("p (g c i d) -> p g c d i", g=ID_TILES, d=D, i=16),
+        )
+        place_scales(es, es_dealt, E_SCALE_ROW)
 
         own_turned = bank(6, "own_turned", [P, P])
         nc.tensor.transpose(own_turned[:], own_rows[:], ident[:])
@@ -188,13 +194,13 @@ def tile_picked_ycosm_cal_p_kernel(tc, x_words, x_scales, w1, e_words, e_scales,
             nc.vector.quantize_mx(out=h_codes[:, cols].bitcast(FP8X4), scales=h_scales[:, cols], in_=grouped)
 
         ew = [gather_words(0, None)]
-        first_half = sb("h_grouped0", [P, 2, P * PACK], BF16, after="es_listed")
+        first_half = sb("h_grouped0", [P, 2, P * PACK], BF16, after="inv_listed")
         for q in range(2):
             group_h(q, nc.vector.tensor_copy, first_half[:, q, :])
         for q in range(2):
             quantise_h(q, 1, first_half[:, q, :])
-        ew.append(gather_words(1, "es_listed"))
-        second_half = sb("h_grouped1", [P, 2, P * PACK], BF16, after="inv_listed")
+        ew.append(gather_words(1, "inv_listed"))
+        second_half = sb("h_grouped1", [P, 2, P * PACK], BF16, after="xw_table")
         for within in range(2):
             group_h(2 + within, nc.scalar.copy, second_half[:, within, :])
         quantise_h(2, 2, second_half[:].rearrange("p w c -> p (w c)"))

@@ -101,7 +101,6 @@ def tile_picked_ycosm_cal_p_kernel(tc, x_words, x_scales, w1, e_words, e_scales,
         for g in range(ID_TILES):
             nc.sync.dma_start(out=inv_cols[:, g, 0:D], in_=inv_listed[INV_ROW:P, g * ID_ENTRIES : (g + 1) * ID_ENTRIES].rearrange("o (v d) -> o v d", d=D))
         inv_eight = sb("inv_eight", [P, ID_TILES, D], F32)
-        nc.gpsimd.tensor_scalar(inv_eight[:], inv_cols[:, :, 0:D], BEST_WEIGHT, 0.0, ALU.mult, ALU.add)
 
 
         w_codes = sb("w_codes", [P, H], U32)
@@ -194,6 +193,7 @@ def tile_picked_ycosm_cal_p_kernel(tc, x_words, x_scales, w1, e_words, e_scales,
             nc.vector.quantize_mx(out=h_codes[:, cols].bitcast(FP8X4), scales=h_scales[:, cols], in_=grouped)
 
         ew = [gather_words(0, None)]
+        nc.vector.tensor_scalar(inv_eight[:], inv_cols[:, :, 0:D], BEST_WEIGHT, None, ALU.mult)
         first_half = sb("h_grouped0", [P, 2, P * PACK], BF16, after="inv_listed")
         for q in range(2):
             group_h(q, nc.vector.tensor_copy, first_half[:, q, :])
@@ -248,6 +248,11 @@ def tile_picked_ycosm_cal_p_kernel(tc, x_words, x_scales, w1, e_words, e_scales,
             nc.gpsimd.tensor_scalar(z0[:], work[g]["z0_eight"][:, cols], 1.0 / BEST_WEIGHT, 0.0, ALU.mult, ALU.add)
             return z0
 
+        def larger(dst, scaled, other, cols):
+            nc.vector.scalar_tensor_tensor(dst[:, cols], scaled[:, cols], BEST_WEIGHT, other[:, cols], ALU.mult, ALU.max)
+
+        w0, w = work
+        best = [sb("best%d" % g, [P, FACES], F32) for g in range(ID_TILES)]
         for pair in range(2):
             acc = bank(pair, "y0_0_%d" % pair, [P, 2, HALF])
             for e in range(2):
@@ -260,8 +265,15 @@ def tile_picked_ycosm_cal_p_kernel(tc, x_words, x_scales, w1, e_words, e_scales,
             read_bank(0, d, halves[1], acc[:])
         for a in range(2):
             total[0, a] = bank(4 + a, "total0_%d" % a, [P, 2, P])
-        z0 = eighth("z0_0_0", 0, halves[0], None)
-        for n, term in enumerate((work[0]["z1"], z0, work[0]["z2"], work[0]["z3"])):
+        sum01 = sb("sum01", [P, FACES], F32)
+
+        def add_first_pair(cols):
+            nc.vector.scalar_tensor_tensor(sum01[:, cols], w0["z0_eight"][:, cols], 1.0 / BEST_WEIGHT, w0["z1"][:, cols], ALU.mult, ALU.add)
+
+        larger(w0["best01"], w0["z1"], w0["z0_eight"], halves[0])
+        add_first_pair(halves[0])
+        nc.vector.tensor_tensor(w0["best23"][:, halves[0]], w0["z2"][:, halves[0]], w0["z3"][:, halves[0]], ALU.max)
+        for n, term in enumerate((w0["z2"], sum01, w0["z3"])):
             turn(total[0, 0], term[:, halves[0]], n == 0, False)
         y1 = {}
         for d, b in ((0, 1), (2, 2), (1, 3), (3, 6)):
@@ -269,24 +281,18 @@ def tile_picked_ycosm_cal_p_kernel(tc, x_words, x_scales, w1, e_words, e_scales,
             product(y1[d][:], 1, d, whole)
         for d in (0, 2, 3):
             read_bank(1, d, whole, y1[d][:])
-        z0 = eighth("z0_0_1", 0, halves[1], None)
-        for n, term in enumerate((work[0]["z1"][:, halves[1]], z0[:], work[0]["z2"][:, halves[1]], work[0]["z3"][:, halves[1]])):
-            turn(total[0, 1], term, n == 0, False)
-
-        def larger(dst, scaled, other, cols):
-            nc.vector.scalar_tensor_tensor(dst[:, cols], scaled[:, cols], BEST_WEIGHT, other[:, cols], ALU.mult, ALU.max)
-
-        w0, w = work
-        best = [sb("best%d" % g, [P, FACES], F32) for g in range(ID_TILES)]
-        larger(w0["best01"], w0["z1"], w0["z0_eight"], whole)
-        for a in range(2):
-            nc.vector.tensor_tensor(w0["best23"][:, halves[a]], w0["z2"][:, halves[a]], w0["z3"][:, halves[a]], ALU.max)
-        for a in range(2):
-            larger(best[0], w0["best23"], w0["best01"], halves[a])
-            turn(total[0, a], best[0][:, halves[a]], False, True)
+        larger(best[0], w0["best23"], w0["best01"], halves[0])
+        turn(total[0, 0], best[0][:, halves[0]], False, True)
+        larger(w0["best01"], w0["z1"], w0["z0_eight"], halves[1])
+        add_first_pair(halves[1])
+        nc.vector.tensor_tensor(w0["best23"][:, halves[1]], w0["z2"][:, halves[1]], w0["z3"][:, halves[1]], ALU.max)
+        for n, term in enumerate((w0["z2"], sum01, w0["z3"])):
+            turn(total[0, 1], term[:, halves[1]], n == 0, False)
         z0 = eighth("z0_1", 1, whole, None)
-        for a in range(2):
-            nc.vector.scalar_tensor_tensor(w["best01"][:, halves[a]], y1[1][:, halves[a]], inv_eight[:, 1, 1:2], w["z0_eight"][:, halves[a]], ALU.mult, ALU.max)
+        nc.vector.scalar_tensor_tensor(w["best01"][:, halves[0]], y1[1][:, halves[0]], inv_eight[:, 1, 1:2], w["z0_eight"][:, halves[0]], ALU.mult, ALU.max)
+        larger(best[0], w0["best23"], w0["best01"], halves[1])
+        nc.vector.scalar_tensor_tensor(w["best01"][:, halves[1]], y1[1][:, halves[1]], inv_eight[:, 1, 1:2], w["z0_eight"][:, halves[1]], ALU.mult, ALU.max)
+        turn(total[0, 1], best[0][:, halves[1]], False, True)
         read_bank(1, 1, whole, y1[1][:])
         for a in range(2):
             larger(w["best23"], w["z2"], w["best01"], halves[a])

@@ -19,13 +19,18 @@ TABLE = 2048
 FACES, ENTRIES, D = 512, 1024, 4
 PACK = 4
 STRIPE = 16
+QUADRANT = 32
 SCALE_ROWS = K // 32
+ROWS_A_QUADRANT = SCALE_ROWS * QUADRANT // P
 FACE_TILES = FACES // P
 ID_TILES = ENTRIES // (D * P)
 ID_ENTRIES = D * P
 HALF = FACES // 2
+LINE = 4
+RUN = 16
+SCALAR_COLUMNS = 96
 E_SCALE_ROW = 4
-SCALE_ROW0 = P - SCALE_ROWS
+TABLE_ROW = P - SCALE_ROWS
 INV_ROW = P - 1
 OWN_ROW = P - FACE_TILES
 BEST_WEIGHT = 2.0 * D
@@ -46,6 +51,9 @@ def tile_picked_ycosm_cal_p_kernel(tc, x_words, x_scales, w1, e_words, e_scales,
         def bank(b, name, shape):
             return psum.tile(shape, F32, name=name, tag="bank%d" % b)
 
+        def list_slice(list_sb, first, count):
+            return list_sb[:, first // STRIPE : (first + count) // STRIPE]
+
         offs_sb = keep.tile([P, FACES // STRIPE], U16, name="offs_sb")
         enr_sb = keep.tile([P, ENTRIES // STRIPE], U16, name="enr_sb")
         xs_table = sb("xs_table", [P, TABLE], U8)
@@ -55,34 +63,34 @@ def tile_picked_ycosm_cal_p_kernel(tc, x_words, x_scales, w1, e_words, e_scales,
         own_rows = sb("own_rows", [P, P], F32)
         ident = sb("ident", [P, P], F32)
         minus_one = sb("minus_one", [P, 1], F32)
-
         xs = sb("xs", [P, FACES], U8)
         es = sb("es", [P, ENTRIES], U8)
+
         nc.gpsimd.memset(minus_one[:], -1.0)
-        nc.vector.memset(xs_table[0:SCALE_ROW0, :].bitcast(I32), 0)
+        nc.vector.memset(xs_table[0:TABLE_ROW, :].bitcast(I32), 0)
         nc.vector.memset(inv_table[0:INV_ROW, :].bitcast(I32), 0)
-        nc.vector.memset(es_table[0:SCALE_ROW0, :].bitcast(I32), 0)
+        nc.vector.memset(es_table[0:TABLE_ROW, :].bitcast(I32), 0)
         nc.vector.memset(xs[:].bitcast(I32), 0)
         nc.vector.memset(es[:].bitcast(I32), 0)
         nc.vector.memset(own_rows[0:OWN_ROW, :], 0.0)
         make_identity(nc, ident[:])
 
-        def list_slice(list_sb, first, count):
-            return list_sb[:, first // STRIPE : (first + count) // STRIPE]
-
-        def place_scales(placed, listed, first_row):
-            for r in range(4):
-                nc.sync.dma_start(out=placed[first_row + r : P : 32, :].bitcast(I32), in_=listed[SCALE_ROW0 + r : P : 4, :].bitcast(I32))
-
         w_raw = sb("w_raw", [P, PACK, H], F32)
         nc.sync.dma_start(offs_sb[:], offs)
-        nc.scalar.dma_start(out=xs_table[SCALE_ROW0:P, :].bitcast(I32), in_=x_scales[0].bitcast(I32))
+        nc.scalar.dma_start(out=xs_table[TABLE_ROW:P, :].bitcast(I32), in_=x_scales[0].bitcast(I32))
         nc.sync.dma_start(enr_sb[:], enr)
-        nc.scalar.dma_start(out=es_table[SCALE_ROW0:P, :].bitcast(I32), in_=e_scales[0].bitcast(I32))
+        nc.scalar.dma_start(out=es_table[TABLE_ROW:P, :].bitcast(I32), in_=e_scales[0].bitcast(I32))
         nc.sync.dma_start(out=inv_table[INV_ROW : INV_ROW + 1, :], in_=inv[0:1, :])
         nc.sync.dma_start(out=w_raw[:], in_=w1.rearrange("(p j) c -> p j c", j=PACK))
         nc.sync.dma_start(out=xw_table[:], in_=x_words[0].rearrange("p n t -> p (n t)").bitcast(I32))
         nc.sync.dma_start(out=own_rows[OWN_ROW:P, :], in_=own.rearrange("(q p) o -> q (p o)", p=P))
+
+        def place_scales(placed, listed, first_row):
+            for r in range(ROWS_A_QUADRANT):
+                nc.sync.dma_start(
+                    out=placed[first_row + r : P : QUADRANT, :].bitcast(I32),
+                    in_=listed[TABLE_ROW + r : P : ROWS_A_QUADRANT, :].bitcast(I32),
+                )
 
         xs_listed = sb("xs_listed", [P, FACES], U8)
         nc.vector.tensor_copy(xs_listed[:], xs_table[:].indirect(offs_sb[:]))
@@ -99,28 +107,26 @@ def tile_picked_ycosm_cal_p_kernel(tc, x_words, x_scales, w1, e_words, e_scales,
         nc.scalar.activation(inv_listed[:], inv_table[:].indirect(enr_sb[:]), ACT.Copy)
         inv_cols = sb("inv_cols", [P, ID_TILES, 2 * D], F32)
         for g in range(ID_TILES):
-            nc.sync.dma_start(out=inv_cols[:, g, 0:D], in_=inv_listed[INV_ROW:P, g * ID_ENTRIES : (g + 1) * ID_ENTRIES].rearrange("o (v d) -> o v d", d=D))
-        inv_eight = sb("inv_eight", [P, ID_TILES, D], F32)
-
+            nc.sync.dma_start(
+                out=inv_cols[:, g, 0:D],
+                in_=inv_listed[INV_ROW:P, g * ID_ENTRIES : (g + 1) * ID_ENTRIES].rearrange("o (v d) -> o v d", d=D),
+            )
 
         w_codes = sb("w_codes", [P, H], U32)
         w_scales = sb("w_scales", [P, H], U8)
         w_grouped = [sb("w_grouped%d" % a, [P, HALF, PACK], BF16) for a in range(2)]
 
-        def cast_w(engine_copy, a, first, last):
-            grouped = w_grouped[a][:].rearrange("p (c i) j -> p c j i", i=4)
-            raw = w_raw[:, :, a * HALF : (a + 1) * HALF].rearrange("p j (c i) -> p c j i", i=4)
-            engine_copy(grouped[:, first:last], raw[:, first:last])
+        def round_w(engine_copy, a, first, last):
+            grouped = w_grouped[a][:].rearrange("p (c i) j -> p c j i", i=LINE)
+            raw = w_raw[:, :, a * HALF : (a + 1) * HALF].rearrange("p j (c i) -> p c j i", i=LINE)
+            engine_copy(grouped[:, first // LINE : last // LINE], raw[:, first // LINE : last // LINE])
 
-        def quantise_w(a, first, last):
-            cols = slice(a * HALF + first, a * HALF + last)
-            nc.vector.quantize_mx(out=w_codes[:, cols].bitcast(FP8X4), scales=w_scales[:, cols], in_=w_grouped[a][:, first:last, :].rearrange("p c j -> p (c j)"))
-
-        cast_w(nc.scalar.copy, 0, 0, 64)
-        cast_w(nc.scalar.copy, 1, 0, 48)
-        cast_w(nc.vector.tensor_copy, 1, 48, 64)
-        quantise_w(0, 0, HALF)
-        quantise_w(1, 0, HALF)
+        round_w(nc.scalar.copy, 0, 0, HALF)
+        round_w(nc.scalar.copy, 1, 0, SCALAR_COLUMNS)
+        round_w(nc.vector.tensor_copy, 1, SCALAR_COLUMNS, HALF)
+        for a in range(2):
+            cols = slice(a * HALF, (a + 1) * HALF)
+            nc.vector.quantize_mx(out=w_codes[:, cols].bitcast(FP8X4), scales=w_scales[:, cols], in_=w_grouped[a][:].rearrange("p c j -> p (c j)"))
 
         xw = []
         for n, (first, count) in enumerate(((0, P), (P, P), (2 * P, 2 * P))):
@@ -131,8 +137,8 @@ def tile_picked_ycosm_cal_p_kernel(tc, x_words, x_scales, w1, e_words, e_scales,
 
         es_dealt = sb("es_dealt", [P, ENTRIES], U8, after="xw_table")
         nc.vector.tensor_copy(
-            es_dealt[:].rearrange("p (g d c i) -> p g c d i", g=ID_TILES, d=D, i=16),
-            es_listed[:].rearrange("p (g c i d) -> p g c d i", g=ID_TILES, d=D, i=16),
+            es_dealt[:].rearrange("p (g d c i) -> p g c d i", g=ID_TILES, d=D, i=RUN),
+            es_listed[:].rearrange("p (g c i d) -> p g c d i", g=ID_TILES, d=D, i=RUN),
         )
         place_scales(es, es_dealt, E_SCALE_ROW)
 
@@ -143,8 +149,7 @@ def tile_picked_ycosm_cal_p_kernel(tc, x_words, x_scales, w1, e_words, e_scales,
         nc.scalar.activation(sign[:], own_turned[:, OWN_ROW:P], ACT.Sign)
         nc.scalar.activation(quarter_abs[:], own_turned[:, OWN_ROW:P], ACT.Abs, scale=1.0 / D)
 
-        h_rows = []
-        accs = []
+        h_accs = []
         for q in range(FACE_TILES):
             acc = bank(q, "h_acc%d" % q, [P, H])
             nc.tensor.matmul_mx(
@@ -156,34 +161,20 @@ def tile_picked_ycosm_cal_p_kernel(tc, x_words, x_scales, w1, e_words, e_scales,
                 start=True,
                 stop=True,
             )
-            accs.append(acc)
-
-        def read_h(q):
-            rows = sb("h_rows%d" % q, [P, 2, P, 2], BF16)
-            src = accs[q][:].rearrange("t (p u e) -> t u p e", u=2, e=2)
-            nc.scalar.activation(rows[:], src, ACT.Copy, scale=sign[:, q : q + 1])
-            h_rows.append(rows)
+            h_accs.append(acc)
 
         h_turned = []
-
-        def turn_h(q):
+        for q in range(FACE_TILES):
+            h_rows = sb("h_rows%d" % q, [P, 2, P, 2], BF16)
+            nc.scalar.activation(h_rows[:], h_accs[q][:].rearrange("t (p u e) -> t u p e", u=2, e=2), ACT.Copy, scale=sign[:, q : q + 1])
             turned = bank(FACE_TILES + q, "h_turned%d" % q, [P, 2, P])
-            h_pairs = h_rows[q][:].rearrange("t u p e -> t (u p e)").bitcast(F32)
+            h_pairs = h_rows[:].rearrange("t u p e -> t (u p e)").bitcast(F32)
             for u in range(2):
                 nc.tensor.transpose(turned[:, u, :], h_pairs[:, u * P : (u + 1) * P], ident[:])
             h_turned.append(turned)
 
         def group_h(q, engine_copy, grouped):
             engine_copy(grouped.bitcast(F32).rearrange("p (t u) -> p t u", u=2), h_turned[q][:].rearrange("p u t -> p t u"))
-
-        for q in range(FACE_TILES):
-            read_h(q)
-            turn_h(q)
-
-        def gather_words(g, after):
-            dealt = sb("ew%d" % g, [P, D, P], U32, after=after)
-            nc.vector.tensor_copy(dealt[:].rearrange("p d v -> p v d"), ew_table[:].bitcast(U32).indirect(list_slice(enr_sb, g * ID_ENTRIES, ID_ENTRIES)))
-            return dealt
 
         h_codes = sb("h_codes", [P, FACES], U32)
         h_scales = sb("h_scales", [P, FACES], U8)
@@ -192,7 +183,13 @@ def tile_picked_ycosm_cal_p_kernel(tc, x_words, x_scales, w1, e_words, e_scales,
             cols = slice(first * P, (first + count) * P)
             nc.vector.quantize_mx(out=h_codes[:, cols].bitcast(FP8X4), scales=h_scales[:, cols], in_=grouped)
 
+        def gather_words(g, after):
+            dealt = sb("ew%d" % g, [P, D, P], U32, after=after)
+            nc.vector.tensor_copy(dealt[:].rearrange("p d v -> p v d"), ew_table[:].bitcast(U32).indirect(list_slice(enr_sb, g * ID_ENTRIES, ID_ENTRIES)))
+            return dealt
+
         ew = [gather_words(0, None)]
+        inv_eight = sb("inv_eight", [P, ID_TILES, D], F32)
         nc.vector.tensor_scalar(inv_eight[:], inv_cols[:, :, 0:D], BEST_WEIGHT, None, ALU.mult)
         first_half = sb("h_grouped0", [P, 2, P * PACK], BF16, after="inv_listed")
         for q in range(2):
@@ -205,115 +202,133 @@ def tile_picked_ycosm_cal_p_kernel(tc, x_words, x_scales, w1, e_words, e_scales,
             group_h(2 + within, nc.scalar.copy, second_half[:, within, :])
         quantise_h(2, 2, second_half[:].rearrange("p w c -> p (w c)"))
 
-        halves = [slice(a * HALF, (a + 1) * HALF) for a in range(2)]
-        whole = slice(0, FACES)
+        unit_banks = ((0, 1), (2, 3), (4, 5), (7, 0))
+        y = {}
+        term = {}
 
-        def product(acc, g, d, cols):
-            nc.tensor.matmul_mx(
-                out=acc,
-                lhsT=ew[g][:, d, :].bitcast(FP8X4),
-                lhsT_scale=es[E_SCALE_ROW:P, (g * D + d) * P : (g * D + d + 1) * P],
-                rhs=h_codes[:, cols].bitcast(FP8X4),
-                rhs_scale=h_scales[:, cols],
-                start=True,
-                stop=True,
-            )
+        def new_term(u, name, after=None):
+            term[u, name] = sb("%s_%d" % (name, u), [P, HALF], F32, after=after)
+            return term[u, name]
 
-        names = ("z0_eight", "z1", "z2", "z3", "best01", "best23")
-        work = [dict((n, sb("%s_%d" % (n, g), [P, FACES], F32)) for n in names) for g in range(ID_TILES)]
+        def products(u):
+            g, faces = u % ID_TILES, slice(u // ID_TILES * HALF, (u // ID_TILES + 1) * HALF)
+            for pair in range(2):
+                acc = bank(unit_banks[u][pair], "y%d_%d" % (u, pair), [P, 2, HALF])
+                for e in range(2):
+                    d = 2 * pair + e
+                    nc.tensor.matmul_mx(
+                        out=acc[:, e, :],
+                        lhsT=ew[g][:, d, :].bitcast(FP8X4),
+                        lhsT_scale=es[E_SCALE_ROW:P, (g * D + d) * P : (g * D + d + 1) * P],
+                        rhs=h_codes[:, faces].bitcast(FP8X4),
+                        rhs_scale=h_scales[:, faces],
+                        start=True,
+                        stop=True,
+                    )
+                    y[u, d] = acc[:, e, :]
 
-        def read_bank(g, d, cols, src):
-            w = work[g]
-            if d == 0:
-                nc.scalar.activation(w["z0_eight"][:, cols], src, ACT.Copy, scale=inv_eight[:, g, 0:1])
-            else:
-                nc.scalar.activation(w["z%d" % d][:, cols], src, ACT.Copy, scale=inv_cols[:, g, d : d + 1])
+        def read(u, name, d, factors):
+            nc.scalar.activation(new_term(u, name)[:], y[u, d], ACT.Copy, scale=factors[:, u % ID_TILES, d : d + 1])
+
+        def reads(u, after=None):
+            read(u, "z0_eight", 0, inv_eight)
+            read(u, "z1", 1, inv_cols)
+            read(u, "z2", 2, inv_cols)
+            nc.gpsimd.tensor_scalar(new_term(u, "z0", after)[:], term[u, "z0_eight"][:], 1.0 / BEST_WEIGHT, 0.0, ALU.mult, ALU.add)
+
+        def step(u, name, d, factors, op, other):
+            nc.vector.scalar_tensor_tensor(new_term(u, name)[:], y[u, d], factors[:, u % ID_TILES, d : d + 1], term[u, other][:], ALU.mult, op)
+
+        def step_best01(u):
+            step(u, "best01", 1, inv_eight, ALU.max, "z0_eight")
+
+        def step_best012(u):
+            step(u, "best012", 2, inv_eight, ALU.max, "best01")
+
+        def step_best(u):
+            step(u, "best", 3, inv_eight, ALU.max, "best012")
+
+        def step_sum23(u):
+            step(u, "sum23", 3, inv_cols, ALU.add, "z2")
+
+        def larger(u, name, scaled, other, cols):
+            nc.vector.scalar_tensor_tensor(term[u, name][:, cols], term[u, scaled][:, cols], BEST_WEIGHT, term[u, other][:, cols], ALU.mult, ALU.max)
 
         total = {}
 
-        def turn(acc, term, first, last):
-            count = acc.shape[1]
-            for within in range(count):
+        def turn(u, name, opens=False, closes=False, tiles=(0, 1)):
+            for within in tiles:
+                acc, first, last = total[u, within]
                 nc.tensor.matmul(
-                    acc[:, within, :],
-                    lhsT=term[:, within * P : (within + 1) * P],
+                    acc,
+                    lhsT=term[u, name][:, within * P : (within + 1) * P],
                     rhs=ident[:],
                     is_transpose=True,
-                    start=(first and within == 0),
-                    stop=(last and within == count - 1),
+                    start=(opens and first),
+                    stop=(closes and last),
                 )
 
-        def eighth(name, g, cols, after):
-            z0 = sb(name, [P, cols.stop - cols.start], F32, after=after)
-            nc.gpsimd.tensor_scalar(z0[:], work[g]["z0_eight"][:, cols], 1.0 / BEST_WEIGHT, 0.0, ALU.mult, ALU.add)
-            return z0
+        result = sb("result", [P, FACE_TILES, ID_TILES * P], F32)
+        out_tiles = out.rearrange("(q p) v -> p q v", p=P)
 
-        def larger(dst, scaled, other, cols):
-            nc.vector.scalar_tensor_tensor(dst[:, cols], scaled[:, cols], BEST_WEIGHT, other[:, cols], ALU.mult, ALU.max)
+        def finish(sums, tiles, cols, queue):
+            for acc, q in zip(sums, range(tiles.start, tiles.stop)):
+                nc.scalar.activation(result[:, q, cols], acc, ACT.Sigmoid, bias=minus_one[:], scale=quarter_abs[:, q : q + 1])
+            queue.dma_start(out=out_tiles[:, tiles, cols], in_=result[:, tiles, cols])
 
-        w0, w = work
-        best = [sb("best%d" % g, [P, FACES], F32) for g in range(ID_TILES)]
-        for pair in range(2):
-            acc = bank(pair, "y0_0_%d" % pair, [P, 2, HALF])
-            for e in range(2):
-                product(acc[:, e, :], 0, 2 * pair + e, halves[0])
-            for e in range(2):
-                read_bank(0, 2 * pair + e, halves[0], acc[:, e, :])
-        for d, b in enumerate((2, 3, 6, 7)):
-            acc = bank(b, "y0_1_%d" % d, [P, HALF])
-            product(acc[:], 0, d, halves[1])
-            read_bank(0, d, halves[1], acc[:])
-        for a in range(2):
-            total[0, a] = bank(4 + a, "total0_%d" % a, [P, 2, P])
-        sum01 = sb("sum01", [P, FACES], F32)
+        products(0)
+        reads(0, after="xw_table")
+        products(1)
+        step_best01(0)
+        step_sum23(0)
+        reads(1)
+        step_best012(0)
+        products(2)
+        products(3)
+        step_best01(1)
+        step_best(0)
+        first_total = bank(6, "total01", [P, 2, ID_TILES, P])
+        for u in range(2):
+            for within in range(2):
+                total[u, within] = (first_total[:, within, u, :], within == 0, within == 1)
+        turn(0, "z1", opens=True)
+        turn(0, "sum23")
+        step_sum23(1)
+        reads(2)
+        step_best012(1)
+        turn(0, "z0")
+        turn(1, "z1")
+        turn(1, "z0")
+        turn(0, "best")
+        step_best01(2)
+        step_best(1)
+        turn(1, "sum23")
+        turn(1, "best", closes=True)
+        step_sum23(2)
 
-        def add_first_pair(cols):
-            nc.vector.scalar_tensor_tensor(sum01[:, cols], w0["z0_eight"][:, cols], 1.0 / BEST_WEIGHT, w0["z1"][:, cols], ALU.mult, ALU.add)
-
-        larger(w0["best01"], w0["z1"], w0["z0_eight"], halves[0])
-        add_first_pair(halves[0])
-        nc.vector.tensor_tensor(w0["best23"][:, halves[0]], w0["z2"][:, halves[0]], w0["z3"][:, halves[0]], ALU.max)
-        for n, term in enumerate((w0["z2"], sum01, w0["z3"])):
-            turn(total[0, 0], term[:, halves[0]], n == 0, False)
-        y1 = {}
-        for d, b in ((0, 1), (2, 2), (1, 3), (3, 6)):
-            y1[d] = bank(b, "y1_%d" % d, [P, FACES])
-            product(y1[d][:], 1, d, whole)
-        for d in (0, 2, 3):
-            read_bank(1, d, whole, y1[d][:])
-        larger(best[0], w0["best23"], w0["best01"], halves[0])
-        turn(total[0, 0], best[0][:, halves[0]], False, True)
-        larger(w0["best01"], w0["z1"], w0["z0_eight"], halves[1])
-        add_first_pair(halves[1])
-        nc.vector.tensor_tensor(w0["best23"][:, halves[1]], w0["z2"][:, halves[1]], w0["z3"][:, halves[1]], ALU.max)
-        for n, term in enumerate((w0["z2"], sum01, w0["z3"])):
-            turn(total[0, 1], term[:, halves[1]], n == 0, False)
-        z0 = eighth("z0_1", 1, whole, None)
-        nc.vector.scalar_tensor_tensor(w["best01"][:, halves[0]], y1[1][:, halves[0]], inv_eight[:, 1, 1:2], w["z0_eight"][:, halves[0]], ALU.mult, ALU.max)
-        larger(best[0], w0["best23"], w0["best01"], halves[1])
-        nc.vector.scalar_tensor_tensor(w["best01"][:, halves[1]], y1[1][:, halves[1]], inv_eight[:, 1, 1:2], w["z0_eight"][:, halves[1]], ALU.mult, ALU.max)
-        turn(total[0, 1], best[0][:, halves[1]], False, True)
-        read_bank(1, 1, whole, y1[1][:])
-        for a in range(2):
-            larger(w["best23"], w["z2"], w["best01"], halves[a])
-        pieces = (slice(0, 2 * P), slice(2 * P, 3 * P), slice(3 * P, 4 * P))
-        for cols in pieces:
-            larger(best[1], w["z3"], w["best23"], cols)
-
-        def finish(g, cols, acc, result, queue):
-            tiles = slice(cols.start // P, cols.stop // P)
-            for q in range(tiles.start, tiles.stop):
-                nc.scalar.activation(result[:, q, :], acc[:, q - tiles.start, :], ACT.Sigmoid, bias=minus_one[:], scale=quarter_abs[:, q : q + 1])
-            queue.dma_start(out=out[:, g * P : (g + 1) * P].rearrange("(q p) v -> p q v", p=P)[:, tiles, :], in_=result[:, tiles, :])
-
-        result = sb("result0", [P, FACE_TILES, P], F32, after="inv_cols")
-        for a in range(2):
-            finish(0, halves[a], total[0, a], result, nc.sync)
-        total1 = [bank(b, "total1_%d" % n, [P, (cols.stop - cols.start) // P, P]) for n, (b, cols) in enumerate(zip((7, 0, 1), pieces))]
-        for n, term in enumerate((w["z2"], z0, w["z3"], w["z1"])):
-            for acc, cols in zip(total1, pieces):
-                turn(acc, term[:, cols], n == 0, False)
-        result = sb("result1", [P, FACE_TILES, P], F32)
-        for acc, cols in zip(total1, pieces):
-            turn(acc, best[1][:, cols], False, True)
-            finish(1, cols, acc, result, nc.scalar if cols.stop == FACES else nc.sync)
+        reads(3)
+        read(3, "z3", 3, inv_cols)
+        finish([first_total[:, within].rearrange("p g v -> p (g v)") for within in range(2)], slice(0, 2), slice(0, 2 * P), nc.sync)
+        step_best012(2)
+        step_best01(3)
+        step_best(2)
+        new_term(3, "best012")
+        larger(3, "best012", "z2", "best01", slice(0, HALF))
+        third_total = bank(1, "total2", [P, 2, P])
+        for within in range(2):
+            total[2, within] = (third_total[:, within, :], within == 0, within == 1)
+            total[3, within] = (bank(2 + within, "total3_%d" % within, [P, P])[:], True, True)
+        turn(2, "z1", opens=True)
+        turn(2, "z0")
+        turn(2, "sum23")
+        turn(3, "z1", opens=True)
+        turn(3, "z0")
+        turn(2, "best", closes=True)
+        turn(3, "z2")
+        turn(3, "z3")
+        finish([third_total[:, within, :] for within in range(2)], slice(2, 4), slice(0, P), nc.sync)
+        new_term(3, "best")
+        for within in range(2):
+            larger(3, "best", "z3", "best012", slice(within * P, (within + 1) * P))
+            turn(3, "best", closes=True, tiles=(within,))
+            finish([total[3, within][0]], slice(2 + within, 3 + within), slice(P, 2 * P), (nc.sync, nc.scalar)[within])

@@ -28,7 +28,7 @@ ID_ENTRIES = D * P
 HALF = FACES // 2
 LINE = 4
 RUN = 16
-SCALAR_COLUMNS = 96
+SCALAR_COLUMNS = 64
 E_SCALE_ROW = 4
 TABLE_ROW = P - SCALE_ROWS
 INV_ROW = P - 1
@@ -81,9 +81,9 @@ def tile_picked_ycosm_cal_p_kernel(tc, x_words, x_scales, w1, e_words, e_scales,
         nc.sync.dma_start(enr_sb[:], enr)
         nc.scalar.dma_start(out=es_table[TABLE_ROW:P, :].bitcast(I32), in_=e_scales[0].bitcast(I32))
         nc.sync.dma_start(out=inv_table[INV_ROW : INV_ROW + 1, :], in_=inv[0:1, :])
+        nc.scalar.dma_start(out=own_rows[OWN_ROW:P, :], in_=own.rearrange("(q p) o -> q (p o)", p=P))
         nc.sync.dma_start(out=w_raw[:], in_=w1.rearrange("(p j) c -> p j c", j=PACK))
         nc.sync.dma_start(out=xw_table[:], in_=x_words[0].rearrange("p n t -> p (n t)").bitcast(I32))
-        nc.sync.dma_start(out=own_rows[OWN_ROW:P, :], in_=own.rearrange("(q p) o -> q (p o)", p=P))
 
         def place_scales(placed, listed, first_row):
             for r in range(ROWS_A_QUADRANT):
@@ -144,8 +144,8 @@ def tile_picked_ycosm_cal_p_kernel(tc, x_words, x_scales, w1, e_words, e_scales,
 
         own_turned = bank(6, "own_turned", [P, P])
         nc.tensor.transpose(own_turned[:], own_rows[:], ident[:])
-        sign = sb("sign", [P, FACE_TILES], F32)
-        quarter_abs = sb("quarter_abs", [P, FACE_TILES], F32)
+        sign = sb("sign", [P, FACE_TILES], F32, after="w_raw")
+        quarter_abs = sb("quarter_abs", [P, FACE_TILES], F32, after="w_grouped1")
         nc.scalar.activation(sign[:], own_turned[:, OWN_ROW:P], ACT.Sign)
         nc.scalar.activation(quarter_abs[:], own_turned[:, OWN_ROW:P], ACT.Abs, scale=1.0 / D)
 
@@ -295,6 +295,7 @@ def tile_picked_ycosm_cal_p_kernel(tc, x_words, x_scales, w1, e_words, e_scales,
         turn(0, "sum23")
         step_sum23(1)
         reads(2)
+        read(2, "z3", 3, inv_cols)
         step_best012(1)
         turn(0, "z0")
         turn(1, "z1")
@@ -304,7 +305,6 @@ def tile_picked_ycosm_cal_p_kernel(tc, x_words, x_scales, w1, e_words, e_scales,
         step_best(1)
         turn(1, "sum23")
         turn(1, "best", closes=True)
-        step_sum23(2)
 
         reads(3)
         read(3, "z3", 3, inv_cols)
@@ -313,14 +313,16 @@ def tile_picked_ycosm_cal_p_kernel(tc, x_words, x_scales, w1, e_words, e_scales,
         step_best01(3)
         step_best(2)
         new_term(3, "best012")
-        larger(3, "best012", "z2", "best01", slice(0, HALF))
+        for within in range(2):
+            larger(3, "best012", "z2", "best01", slice(within * P, (within + 1) * P))
         third_total = bank(1, "total2", [P, 2, P])
         for within in range(2):
             total[2, within] = (third_total[:, within, :], within == 0, within == 1)
             total[3, within] = (bank(2 + within, "total3_%d" % within, [P, P])[:], True, True)
         turn(2, "z1", opens=True)
         turn(2, "z0")
-        turn(2, "sum23")
+        turn(2, "z2")
+        turn(2, "z3")
         turn(3, "z1", opens=True)
         turn(3, "z0")
         turn(2, "best", closes=True)

@@ -30,9 +30,10 @@ LINE = 4
 RUN = 16
 SCALAR_COLUMNS = 64
 E_SCALE_ROW = 4
-TABLE_ROW = P - SCALE_ROWS
+X_TABLE_ROW = P - SCALE_ROWS
+E_TABLE_ROW = P // 2 - SCALE_ROWS
 INV_ROW = P - 1
-OWN_ROW = P - FACE_TILES
+OWN_ROW = P // 2 - FACE_TILES
 BEST_WEIGHT = 2.0 * D
 
 FLOPS = 2 * K * H * FACES + 2 * H * FACES * ENTRIES
@@ -67,34 +68,36 @@ def tile_picked_ycosm_cal_p_kernel(tc, x_words, x_scales, w1, e_words, e_scales,
         es = sb("es", [P, ENTRIES], U8)
 
         nc.gpsimd.memset(minus_one[:], -1.0)
-        nc.vector.memset(xs_table[0:TABLE_ROW, :].bitcast(I32), 0)
+        nc.vector.memset(xs_table[0:X_TABLE_ROW, :].bitcast(I32), 0)
         nc.vector.memset(inv_table[0:INV_ROW, :].bitcast(I32), 0)
-        nc.vector.memset(es_table[0:TABLE_ROW, :].bitcast(I32), 0)
+        nc.vector.memset(es_table[0:E_TABLE_ROW, :].bitcast(I32), 0)
+        nc.vector.memset(es_table[P // 2 : P, :].bitcast(I32), 0)
         nc.vector.memset(xs[:].bitcast(I32), 0)
         nc.vector.memset(es[:].bitcast(I32), 0)
         nc.vector.memset(own_rows[0:OWN_ROW, :], 0.0)
+        nc.vector.memset(own_rows[P // 2 : P, :], 0.0)
         make_identity(nc, ident[:])
 
         w_raw = sb("w_raw", [P, PACK, H], F32)
         nc.sync.dma_start(offs_sb[:], offs)
-        nc.scalar.dma_start(out=xs_table[TABLE_ROW:P, :].bitcast(I32), in_=x_scales[0].bitcast(I32))
+        nc.scalar.dma_start(out=xs_table[X_TABLE_ROW:P, :].bitcast(I32), in_=x_scales[0].bitcast(I32))
         nc.sync.dma_start(enr_sb[:], enr)
-        nc.scalar.dma_start(out=es_table[TABLE_ROW:P, :].bitcast(I32), in_=e_scales[0].bitcast(I32))
+        nc.scalar.dma_start(out=es_table[E_TABLE_ROW : P // 2, :].bitcast(I32), in_=e_scales[0].bitcast(I32))
         nc.sync.dma_start(out=inv_table[INV_ROW : INV_ROW + 1, :], in_=inv[0:1, :])
-        nc.scalar.dma_start(out=own_rows[OWN_ROW:P, :], in_=own.rearrange("(q p) o -> q (p o)", p=P))
+        nc.scalar.dma_start(out=own_rows[OWN_ROW : P // 2, :], in_=own.rearrange("(q p) o -> q (p o)", p=P))
         nc.sync.dma_start(out=w_raw[:], in_=w1.rearrange("(p j) c -> p j c", j=PACK))
         nc.sync.dma_start(out=xw_table[:], in_=x_words[0].rearrange("p n t -> p (n t)").bitcast(I32))
 
-        def place_scales(placed, listed, first_row):
+        def place_scales(placed, listed, table_row, first_row):
             for r in range(ROWS_A_QUADRANT):
                 nc.sync.dma_start(
                     out=placed[first_row + r : P : QUADRANT, :].bitcast(I32),
-                    in_=listed[TABLE_ROW + r : P : ROWS_A_QUADRANT, :].bitcast(I32),
+                    in_=listed[table_row + r : table_row + SCALE_ROWS : ROWS_A_QUADRANT, :].bitcast(I32),
                 )
 
         xs_listed = sb("xs_listed", [P, FACES], U8)
         nc.vector.tensor_copy(xs_listed[:], xs_table[:].indirect(offs_sb[:]))
-        place_scales(xs, xs_listed, 0)
+        place_scales(xs, xs_listed, X_TABLE_ROW, 0)
         ew_table = sb("ew_table", [P, TABLE], I32, after="xs_table")
         nc.sync.dma_start(out=ew_table[:], in_=e_words[0].rearrange("p n t -> p (n t)").bitcast(I32))
         es_listed = sb("es_listed", [P, ENTRIES], U8)
@@ -140,14 +143,14 @@ def tile_picked_ycosm_cal_p_kernel(tc, x_words, x_scales, w1, e_words, e_scales,
             es_dealt[:].rearrange("p (g d c i) -> p g c d i", g=ID_TILES, d=D, i=RUN),
             es_listed[:].rearrange("p (g c i d) -> p g c d i", g=ID_TILES, d=D, i=RUN),
         )
-        place_scales(es, es_dealt, E_SCALE_ROW)
+        place_scales(es, es_dealt, E_TABLE_ROW, E_SCALE_ROW)
 
         own_turned = bank(6, "own_turned", [P, P])
         nc.tensor.transpose(own_turned[:], own_rows[:], ident[:])
         sign = sb("sign", [P, FACE_TILES], F32, after="w_raw")
         quarter_abs = sb("quarter_abs", [P, FACE_TILES], F32, after="w_grouped1")
-        nc.scalar.activation(sign[:], own_turned[:, OWN_ROW:P], ACT.Sign)
-        nc.scalar.activation(quarter_abs[:], own_turned[:, OWN_ROW:P], ACT.Abs, scale=1.0 / D)
+        nc.scalar.activation(sign[:], own_turned[:, OWN_ROW : P // 2], ACT.Sign)
+        nc.scalar.activation(quarter_abs[:], own_turned[:, OWN_ROW : P // 2], ACT.Abs, scale=1.0 / D)
 
         h_accs = []
         for q in range(FACE_TILES):

@@ -68,14 +68,14 @@ def tile_picked_ycosm_cal_p_kernel(tc, x_words, x_scales, w1, e_words, e_scales,
         es = sb("es", [P, ENTRIES], U8)
 
         nc.gpsimd.memset(minus_one[:], -1.0)
+        nc.gpsimd.memset(es_table[P // 2 : P, :].bitcast(I32), 0)
+        nc.gpsimd.memset(own_rows[P // 2 : P, :], 0.0)
         nc.vector.memset(xs_table[0:X_TABLE_ROW, :].bitcast(I32), 0)
         nc.vector.memset(inv_table[0:INV_ROW, :].bitcast(I32), 0)
         nc.vector.memset(es_table[0:E_TABLE_ROW, :].bitcast(I32), 0)
-        nc.vector.memset(es_table[P // 2 : P, :].bitcast(I32), 0)
         nc.vector.memset(xs[:].bitcast(I32), 0)
         nc.vector.memset(es[:].bitcast(I32), 0)
         nc.vector.memset(own_rows[0:OWN_ROW, :], 0.0)
-        nc.vector.memset(own_rows[P // 2 : P, :], 0.0)
         make_identity(nc, ident[:])
 
         w_raw = sb("w_raw", [P, PACK, H], F32)

from contextlib import ExitStack

import concourse.mybir as mybir
from concourse.masks import make_identity

F32 = mybir.dt.float32
BF16 = mybir.dt.bfloat16
I32 = mybir.dt.int32
U32 = mybir.dt.uint32
U16 = mybir.dt.uint16
U8 = mybir.dt.uint8
FP8X4 = mybir.dt.float8_e4m3fn_x4
ALU = mybir.AluOpType
ACT = mybir.ActivationFunctionType

P = 128
K, H = 512, 512
TABLE = 2048
FACES, ENTRIES, D = 512, 1024, 4
PACK = 4
STRIPE = 16
QUADRANT = 32
SCALE_ROWS = K // 32
ROWS_A_QUADRANT = SCALE_ROWS * QUADRANT // P
FACE_TILES = FACES // P
ID_TILES = ENTRIES // (D * P)
ID_ENTRIES = D * P
HALF = FACES // 2
LINE = 4
RUN = 16
SCALAR_COLUMNS = 64
E_SCALE_ROW = 4
X_TABLE_ROW = P - SCALE_ROWS
E_TABLE_ROW = P // 2 - SCALE_ROWS
INV_ROW = P - 1
OWN_ROW = P // 2 - FACE_TILES
BEST_WEIGHT = 2.0 * D

FLOPS = 2 * K * H * FACES + 2 * H * FACES * ENTRIES
BYTES = 2 * (K + SCALE_ROWS) * TABLE + 4 * K * H + 4 * TABLE + 4 * FACES + 2 * P * (FACES + ENTRIES) // STRIPE + 4 * FACES * ENTRIES // D


def tile_picked_ycosm_cal_p_kernel(tc, x_words, x_scales, w1, e_words, e_scales, inv, own, offs, enr, out):
    nc = tc.nc
    with ExitStack() as ctx:
        keep = ctx.enter_context(tc.tile_pool(name="keep", bufs=1))
        psum = ctx.enter_context(tc.psum_pool(name="psum", bufs=1))

        def sb(name, shape, dtype, after=None):
            return keep.tile(shape, dtype, name=name, tag=after or name, align_bytes=64)

        def bank(b, name, shape):
            return psum.tile(shape, F32, name=name, tag="bank%d" % b)

        def list_slice(list_sb, first, count):
            return list_sb[:, first // STRIPE : (first + count) // STRIPE]

        offs_sb = keep.tile([P, FACES // STRIPE], U16, name="offs_sb")
        enr_sb = keep.tile([P, ENTRIES // STRIPE], U16, name="enr_sb")
        xs_table = sb("xs_table", [P, TABLE], U8)
        es_table = sb("es_table", [P, TABLE], U8)
        inv_table = sb("inv_table", [P, TABLE], F32)
        xw_table = sb("xw_table", [P, TABLE], I32)
        own_rows = sb("own_rows", [P, P], F32)
        ident = sb("ident", [P, P], F32)
        minus_one = sb("minus_one", [P, 1], F32)
        xs = sb("xs", [P, FACES], U8)
        es = sb("es", [P, ENTRIES], U8)

        nc.gpsimd.memset(minus_one[:], -1.0)
        nc.gpsimd.memset(es_table[P // 2 : P, :].bitcast(I32), 0)
        nc.gpsimd.memset(own_rows[P // 2 : P, :], 0.0)
        nc.vector.memset(xs_table[0:X_TABLE_ROW, :].bitcast(I32), 0)
        nc.vector.memset(inv_table[0:INV_ROW, :].bitcast(I32), 0)
        nc.vector.memset(es_table[0:E_TABLE_ROW, :].bitcast(I32), 0)
        nc.vector.memset(xs[:].bitcast(I32), 0)
        nc.vector.memset(es[:].bitcast(I32), 0)
        nc.vector.memset(own_rows[0:OWN_ROW, :], 0.0)
        make_identity(nc, ident[:])

        w_raw = sb("w_raw", [P, PACK, H], F32)
        nc.sync.dma_start(offs_sb[:], offs)
        nc.scalar.dma_start(out=xs_table[X_TABLE_ROW:P, :].bitcast(I32), in_=x_scales[0].bitcast(I32))
        nc.sync.dma_start(enr_sb[:], enr)
        nc.scalar.dma_start(out=es_table[E_TABLE_ROW : P // 2, :].bitcast(I32), in_=e_scales[0].bitcast(I32))
        nc.sync.dma_start(out=inv_table[INV_ROW : INV_ROW + 1, :], in_=inv[0:1, :])
        nc.scalar.dma_start(out=own_rows[OWN_ROW : P // 2, :], in_=own.rearrange("(q p) o -> q (p o)", p=P))
        nc.sync.dma_start(out=w_raw[:], in_=w1.rearrange("(p j) c -> p j c", j=PACK))
        nc.sync.dma_start(out=xw_table[:], in_=x_words[0].rearrange("p n t -> p (n t)").bitcast(I32))

        def place_scales(placed, listed, table_row, first_row):
            for r in range(ROWS_A_QUADRANT):
                nc.sync.dma_start(
                    out=placed[first_row + r : P : QUADRANT, :].bitcast(I32),
                    in_=listed[table_row + r : table_row + SCALE_ROWS : ROWS_A_QUADRANT, :].bitcast(I32),
                )

        xs_listed = sb("xs_listed", [P, FACES], U8)
        nc.vector.tensor_copy(xs_listed[:], xs_table[:].indirect(offs_sb[:]))
        place_scales(xs, xs_listed, X_TABLE_ROW, 0)
        ew_table = sb("ew_table", [P, TABLE], I32, after="xs_table")
        nc.sync.dma_start(out=ew_table[:], in_=e_words[0].rearrange("p n t -> p (n t)").bitcast(I32))
        es_listed = sb("es_listed", [P, ENTRIES], U8)
        nc.vector.tensor_copy(es_listed[:], es_table[:].indirect(enr_sb[:]))

        warm = sb("warm", [P, 1], F32)
        nc.scalar.activation(warm[:], minus_one[:], ACT.Sigmoid)

        inv_listed = sb("inv_listed", [P, ENTRIES], F32)
        nc.scalar.activation(inv_listed[:], inv_table[:].indirect(enr_sb[:]), ACT.Copy)
        inv_cols = sb("inv_cols", [P, ID_TILES, 2 * D], F32)
        for g in range(ID_TILES):
            nc.sync.dma_start(
                out=inv_cols[:, g, 0:D],
                in_=inv_listed[INV_ROW:P, g * ID_ENTRIES : (g + 1) * ID_ENTRIES].rearrange("o (v d) -> o v d", d=D),
            )

        w_codes = sb("w_codes", [P, H], U32)
        w_scales = sb("w_scales", [P, H], U8)
        w_grouped = [sb("w_grouped%d" % a, [P, HALF, PACK], BF16) for a in range(2)]

        def round_w(engine_copy, a, first, last):
            grouped = w_grouped[a][:].rearrange("p (c i) j -> p c j i", i=LINE)
            raw = w_raw[:, :, a * HALF : (a + 1) * HALF].rearrange("p j (c i) -> p c j i", i=LINE)
            engine_copy(grouped[:, first // LINE : last // LINE], raw[:, first // LINE : last // LINE])

        round_w(nc.scalar.copy, 0, 0, HALF)
        round_w(nc.scalar.copy, 1, 0, SCALAR_COLUMNS)
        round_w(nc.vector.tensor_copy, 1, SCALAR_COLUMNS, HALF)
        for a in range(2):
            cols = slice(a * HALF, (a + 1) * HALF)
            nc.vector.quantize_mx(out=w_codes[:, cols].bitcast(FP8X4), scales=w_scales[:, cols], in_=w_grouped[a][:].rearrange("p c j -> p (c j)"))

        xw = []
        for n, (first, count) in enumerate(((0, P), (P, P), (2 * P, 2 * P))):
            piece = sb("xw%d" % n, [P, count], U32)
            nc.vector.tensor_copy(piece[:], xw_table[:].bitcast(U32).indirect(list_slice(offs_sb, first, count)))
            for within in range(count // P):
                xw.append(piece[:, within * P : (within + 1) * P])

        es_dealt = sb("es_dealt", [P, ENTRIES], U8, after="xw_table")
        nc.vector.tensor_copy(
            es_dealt[:].rearrange("p (g d c i) -> p g c d i", g=ID_TILES, d=D, i=RUN),
            es_listed[:].rearrange("p (g c i d) -> p g c d i", g=ID_TILES, d=D, i=RUN),
        )
        place_scales(es, es_dealt, E_TABLE_ROW, E_SCALE_ROW)

        own_turned = bank(6, "own_turned", [P, P])
        nc.tensor.transpose(own_turned[:], own_rows[:], ident[:])
        sign = sb("sign", [P, FACE_TILES], F32, after="w_raw")
        quarter_abs = sb("quarter_abs", [P, FACE_TILES], F32, after="w_grouped1")
        nc.scalar.activation(sign[:], own_turned[:, OWN_ROW : P // 2], ACT.Sign)
        nc.scalar.activation(quarter_abs[:], own_turned[:, OWN_ROW : P // 2], ACT.Abs, scale=1.0 / D)

        h_accs = []
        for q in range(FACE_TILES):
            acc = bank(q, "h_acc%d" % q, [P, H])
            nc.tensor.matmul_mx(
                out=acc[:],
                lhsT=xw[q].bitcast(FP8X4),
                lhsT_scale=xs[:, q * P : (q + 1) * P],
                rhs=w_codes[:].bitcast(FP8X4),
                rhs_scale=w_scales[:],
                start=True,
                stop=True,
            )
            h_accs.append(acc)

        h_turned = []
        for q in range(FACE_TILES):
            h_rows = sb("h_rows%d" % q, [P, 2, P, 2], BF16)
            nc.scalar.activation(h_rows[:], h_accs[q][:].rearrange("t (p u e) -> t u p e", u=2, e=2), ACT.Copy, scale=sign[:, q : q + 1])
            turned = bank(FACE_TILES + q, "h_turned%d" % q, [P, 2, P])
            h_pairs = h_rows[:].rearrange("t u p e -> t (u p e)").bitcast(F32)
            for u in range(2):
                nc.tensor.transpose(turned[:, u, :], h_pairs[:, u * P : (u + 1) * P], ident[:])
            h_turned.append(turned)

        def group_h(q, engine_copy, grouped):
            engine_copy(grouped.bitcast(F32).rearrange("p (t u) -> p t u", u=2), h_turned[q][:].rearrange("p u t -> p t u"))

        h_codes = sb("h_codes", [P, FACES], U32)
        h_scales = sb("h_scales", [P, FACES], U8)

        def quantise_h(first, count, grouped):
            cols = slice(first * P, (first + count) * P)
            nc.vector.quantize_mx(out=h_codes[:, cols].bitcast(FP8X4), scales=h_scales[:, cols], in_=grouped)

        def gather_words(g, after):
            dealt = sb("ew%d" % g, [P, D, P], U32, after=after)
            nc.vector.tensor_copy(dealt[:].rearrange("p d v -> p v d"), ew_table[:].bitcast(U32).indirect(list_slice(enr_sb, g * ID_ENTRIES, ID_ENTRIES)))
            return dealt

        ew = [gather_words(0, None)]
        inv_eight = sb("inv_eight", [P, ID_TILES, D], F32)
        nc.vector.tensor_scalar(inv_eight[:], inv_cols[:, :, 0:D], BEST_WEIGHT, None, ALU.mult)
        first_half = sb("h_grouped0", [P, 2, P * PACK], BF16, after="inv_listed")
        for q in range(2):
            group_h(q, nc.vector.tensor_copy, first_half[:, q, :])
        for q in range(2):
            quantise_h(q, 1, first_half[:, q, :])
        ew.append(gather_words(1, "inv_listed"))
        second_half = sb("h_grouped1", [P, 2, P * PACK], BF16, after="xw_table")
        for within in range(2):
            group_h(2 + within, nc.scalar.copy, second_half[:, within, :])
        quantise_h(2, 2, second_half[:].rearrange("p w c -> p (w c)"))

        unit_banks = ((0, 1), (2, 3), (4, 5), (7, 0))
        y = {}
        term = {}

        def new_term(u, name, after=None):
            term[u, name] = sb("%s_%d" % (name, u), [P, HALF], F32, after=after)
            return term[u, name]

        def products(u):
            g, faces = u % ID_TILES, slice(u // ID_TILES * HALF, (u // ID_TILES + 1) * HALF)
            for pair in range(2):
                acc = bank(unit_banks[u][pair], "y%d_%d" % (u, pair), [P, 2, HALF])
                for e in range(2):
                    d = 2 * pair + e
                    nc.tensor.matmul_mx(
                        out=acc[:, e, :],
                        lhsT=ew[g][:, d, :].bitcast(FP8X4),
                        lhsT_scale=es[E_SCALE_ROW:P, (g * D + d) * P : (g * D + d + 1) * P],
                        rhs=h_codes[:, faces].bitcast(FP8X4),
                        rhs_scale=h_scales[:, faces],
                        start=True,
                        stop=True,
                    )
                    y[u, d] = acc[:, e, :]

        def read(u, name, d, factors):
            nc.scalar.activation(new_term(u, name)[:], y[u, d], ACT.Copy, scale=factors[:, u % ID_TILES, d : d + 1])

        def reads(u, after=None):
            read(u, "z0_eight", 0, inv_eight)
            read(u, "z1", 1, inv_cols)
            read(u, "z2", 2, inv_cols)
            nc.gpsimd.tensor_scalar(new_term(u, "z0", after)[:], term[u, "z0_eight"][:], 1.0 / BEST_WEIGHT, 0.0, ALU.mult, ALU.add)

        def step(u, name, d, factors, op, other):
            nc.vector.scalar_tensor_tensor(new_term(u, name)[:], y[u, d], factors[:, u % ID_TILES, d : d + 1], term[u, other][:], ALU.mult, op)

        def step_best01(u):
            step(u, "best01", 1, inv_eight, ALU.max, "z0_eight")

        def step_best012(u):
            step(u, "best012", 2, inv_eight, ALU.max, "best01")

        def step_best(u):
            step(u, "best", 3, inv_eight, ALU.max, "best012")

        def step_sum23(u):
            step(u, "sum23", 3, inv_cols, ALU.add, "z2")

        def larger(u, name, scaled, other, cols):
            nc.vector.scalar_tensor_tensor(term[u, name][:, cols], term[u, scaled][:, cols], BEST_WEIGHT, term[u, other][:, cols], ALU.mult, ALU.max)

        total = {}

        def turn(u, name, opens=False, closes=False, tiles=(0, 1)):
            for within in tiles:
                acc, first, last = total[u, within]
                nc.tensor.matmul(
                    acc,
                    lhsT=term[u, name][:, within * P : (within + 1) * P],
                    rhs=ident[:],
                    is_transpose=True,
                    start=(opens and first),
                    stop=(closes and last),
                )

        result = sb("result", [P, FACE_TILES, ID_TILES * P], F32)
        out_tiles = out.rearrange("(q p) v -> p q v", p=P)

        def finish(sums, tiles, cols, queue):
            for acc, q in zip(sums, range(tiles.start, tiles.stop)):
                nc.scalar.activation(result[:, q, cols], acc, ACT.Sigmoid, bias=minus_one[:], scale=quarter_abs[:, q : q + 1])
            queue.dma_start(out=out_tiles[:, tiles, cols], in_=result[:, tiles, cols])

        products(0)
        reads(0, after="xw_table")
        products(1)
        step_best01(0)
        step_sum23(0)
        reads(1)
        step_best012(0)
        products(2)
        products(3)
        step_best01(1)
        step_best(0)
        first_total = bank(6, "total01", [P, 2, ID_TILES, P])
        for u in range(2):
            for within in range(2):
                total[u, within] = (first_total[:, within, u, :], within == 0, within == 1)
        turn(0, "z1", opens=True)
        turn(0, "sum23")
        step_sum23(1)
        reads(2)
        read(2, "z3", 3, inv_cols)
        step_best012(1)
        turn(0, "z0")
        turn(1, "z1")
        turn(1, "z0")
        turn(0, "best")
        step_best01(2)
        step_best(1)
        turn(1, "sum23")
        turn(1, "best", closes=True)

        reads(3)
        read(3, "z3", 3, inv_cols)
        finish([first_total[:, within].rearrange("p g v -> p (g v)") for within in range(2)], slice(0, 2), slice(0, 2 * P), nc.sync)
        step_best012(2)
        step_best01(3)
        step_best(2)
        new_term(3, "best012")
        for within in range(2):
            larger(3, "best012", "z2", "best01", slice(within * P, (within + 1) * P))
        third_total = bank(1, "total2", [P, 2, P])
        for within in range(2):
            total[2, within] = (third_total[:, within, :], within == 0, within == 1)
            total[3, within] = (bank(2 + within, "total3_%d" % within, [P, P])[:], True, True)
        turn(2, "z1", opens=True)
        turn(2, "z0")
        turn(2, "z2")
        turn(2, "z3")
        turn(3, "z1", opens=True)
        turn(3, "z0")
        turn(2, "best", closes=True)
        turn(3, "z2")
        turn(3, "z3")
        finish([third_total[:, within, :] for within in range(2)], slice(2, 4), slice(0, P), nc.sync)
        new_term(3, "best")
        for within in range(2):
            larger(3, "best", "z3", "best012", slice(within * P, (within + 1) * P))
            turn(3, "best", closes=True, tiles=(within,))
            finish([total[3, within][0]], slice(2 + within, 3 + within), slice(P, 2 * P), (nc.sync, nc.scalar)[within])
